import numpy as np, ml_dtypes
CORES = [36,164,52,180,100,228,116,244]
N = 8
import mx_ref
BF = ml_dtypes.bfloat16
def entries(a):
    return np.ascontiguousarray(a.T).reshape(-1)
def table(e):
    return np.ascontiguousarray(np.reshape(e, (-1, 16)).T).astype(np.int32)
def gentries(a):
    return np.ascontiguousarray(a.reshape(8, 16, -1).transpose(0, 2, 1)).reshape(8, -1)
def gtable(e):
    e = np.asarray(e); return np.ascontiguousarray(e.reshape(8, -1, 16).transpose(0, 2, 1)).reshape(128, -1).astype(np.int32)
def gcols(t, e):
    v = np.concatenate([t.reshape(8, 16, -1, 4), np.zeros((8, 16, 1, 4), BF)], axis=2)
    return np.ascontiguousarray(np.stack([v[g][:, e[g]] for g in range(8)])).reshape(128, -1)
def tile(rs):
    return np.stack(rs, axis=2).reshape(128, -1).astype(BF)
def pick(q, e):
    c = np.concatenate([q[0].reshape(128, -1, 4), np.zeros((128, 1, 4), np.uint8)], axis=1); s = np.concatenate([q[1], np.ones((16, 1), np.uint8)], axis=1)
    return (np.ascontiguousarray(c[:, e].reshape(128, -1)), np.ascontiguousarray(s[:, e]))
def join(*qs):
    return (np.concatenate([q[0] for q in qs], axis=1), np.concatenate([q[1] for q in qs], axis=1))
def put(q, e, v):
    c, s = q[0].reshape(128, -1, 4).copy(), q[1].copy(); c[:, e] = v[0].reshape(128, -1, 4); s[:, e] = v[1]
    return (c.reshape(128, -1), s)
def pk(c, s):
    return (np.ascontiguousarray(c), mx_ref.live(s))
def emit(q):
    return q[0], q[1]
def packed(v, rng):
    q = [mx_ref.quantize(np.ascontiguousarray(v[r])) for r in range(N)]
    return np.stack([a for a, b in q]), np.stack([mx_ref.plane(b, rng) for a, b in q])
def values_of_codes():
    e, c = np.zeros((128, 128, 4), np.float32), np.zeros((128, 2, 4), np.uint8)
    e[np.arange(128), np.arange(128), 0] = 1
    c[:127, :, 0] = np.arange(256).reshape(2, 128).T[:127]
    return mx_ref.matmul(mx_ref.quantize(e.reshape(128, 512).astype(BF)), (c.reshape(128, 8), np.full((16, 2), 127, np.uint8))).T.reshape(-1).astype(np.float64)
CODE_VALUE, SCALE_VALUE = values_of_codes(), 2.0 ** (np.arange(256) - 127.0)
def decode(q):
    return (CODE_VALUE[q[0]].reshape(16, 8, -1, 4) * SCALE_VALUE[q[1]][:, None, :, None] + 0.0).reshape(128, -1).astype(np.float32)
def f(rng, *shape):
    return mx_ref.flush((rng.standard_normal(shape, dtype=np.float32) * np.exp2(rng.integers(-2, 3, shape[:-1] + (1,)))).astype(BF))
def wide(rng, *shape, cols=0):
    v = rng.standard_normal(shape, dtype=np.float32) * np.exp2(rng.integers(-12, 13, shape)).astype(np.float32)
    if cols: v *= np.repeat(np.exp2(rng.integers(-cols, cols + 1, shape[:-2] + (1, shape[-1] // 4))) * (rng.random(shape[:-2] + (1, shape[-1] // 4)) > 0.0625), 4, axis=-1).astype(np.float32)
    return mx_ref.flush(v.astype(BF))
C, L, M, CAP, E = 288, 3, 96, 32, 672
def pairs_of(e, lev):
    r, s = np.arange(N * C) // C, e // C
    return np.where((e < 0) | (s == r), -1, ((np.arange(8)[:, None] * L + lev) * N + r) * N + s)
def big(v):
    v = v.astype(np.float32)
    v[np.abs(v) < np.float32(2.0 ** -16)] = 0
    return v.astype(BF)
def levels(rng):
    return np.concatenate([rng.permutation(np.arange(C) // M) for r in range(N)])
def drawn(rng, lev, far=()):
    e = np.full((2, 8, N * C), -1)
    for k in range(2):
        for g in range(8):
            free = np.ones(N * C, bool)
            deep = g in far
            for l in range(L - 1 if deep else 1, L):
                a = rng.permutation(np.flatnonzero((lev < (1 if deep else l)) & free))[:E]
                e[k, g, rng.permutation(np.flatnonzero(lev == l))[:E]] = a
                free[a] = False
    return e
def fit(rng, e, lev):
    k = pairs_of(e, lev).reshape(-1)
    o = rng.permutation(k.size)
    o = o[np.argsort(k[o], kind="stable")]
    k = k[o]
    v = e.reshape(-1).copy()
    v[o[(k >= 0) & (np.arange(k.size) - np.searchsorted(k, k) >= CAP)]] = -1
    return v.reshape(e.shape)
def inputs(rng, x, e, lev, w, v):
    wc, ws = packed(w, rng)
    vc, vs = packed(v, rng)
    d = {"x": x, "lv": np.stack([table(a) for a in lev.reshape(N, C)])}
    for k in range(2): d["pr%d" % k] = np.stack([gtable(e[k][:, C * r:C * r + C]) for r in range(N)])
    return {**d, "u": np.array(f(rng, N, 128, 512)), "wc": wc, "ws": ws, "vc": vc, "vs": vs}
def still(k=32):
    w = np.zeros((N, 128, 4, 128, 4), np.float32)
    i = np.arange(128)
    for b in range(4): w[:, i, b, i, b] = k
    return w.reshape(N, 128, 2048).astype(BF)
def setup_inputs(rng):
    lev = levels(rng)
    return inputs(rng, big(f(rng, N, 128, 4 * C)), fit(rng, drawn(rng, lev), lev), lev, f(rng, N, 128, 2048), f(rng, N, 128, 2048))
def setup_inputs_same(rng):
    lev = levels(rng)
    o, p = rng.permutation(8), rng.permutation(N)
    e = drawn(rng, lev, o[[3, 7]])
    e[1, o[:4]] = e[0, o[:4]]
    e[0, o[4]] = -1
    e[1, o[5]] = -1
    e[:, o[6]] = -1
    e[:, :, C * p[0]:C * p[0] + C] = -1
    e[e // C == p[1]] = -1
    return inputs(rng, big(f(rng, N, 128, 4 * C)), fit(rng, e, lev), lev, f(rng, N, 128, 2048), f(rng, N, 128, 2048))
def setup_inputs_full(rng):
    lev = levels(rng)
    v, e = lev.reshape(N, C), np.full((2, 8, N * C), -1)
    o, n = rng.permutation(N), N - 1
    m = min(n - 1, 2 * (M // CAP))
    some = rng.permutation(8)
    far, near = some[:2], some[2:4]
    for g in range(8):
        flip, deep = int(rng.integers(2)), g in far
        for k in range(2):
            free = np.ones((N, C), bool)
            for l in range(L - 1 if deep else 1, L):
                may = v == 1 if g in near and l == L - 1 else v < (1 if deep else l)
                pool = [rng.permutation(np.flatnonzero(may[s] & free[s])) for s in range(N)]
                for i in range(N):
                    r, p = o[i], 0
                    to = C * r + rng.permutation(np.flatnonzero(v[r] == l))
                    want = [(o[(i + 1 + a) % n], CAP) for a in range(m) if (a + k + flip) % 2 == 0] if i < n else []
                    rest = M - CAP * len(want)
                    want.append((r, rest if l == L - 1 else rest // 2))
                    for s, c in want:
                        a, pool[s] = pool[s][:c], pool[s][c:]
                        e[k, g, to[p:p + c]] = C * s + a
                        free[s, a] = False
                        p += c
    return inputs(rng, big(f(rng, N, 128, 4 * C)), e, lev, f(rng, N, 128, 2048), f(rng, N, 128, 2048))
def setup_inputs_cancel(rng):
    lev = levels(rng)
    e, x = np.full((2, 8, N * C), -1), np.zeros((8, 16, N * C, 4))
    large = rng.permutation(8) % 2
    for g in range(8):
        v = rng.integers(4, 8, (16, N * C, 4)) * rng.choice([-1.0, 1.0], (16, N * C, 4)) * 2.0 ** -16
        half = []
        for l in range(L):
            p = rng.permutation(np.flatnonzero(lev == l)).reshape(2, -1)
            v[:, p[1]] = -v[:, p[0]]
            if l % 2 == large[g]: v[:, p] = v[:, p] * 2.0 ** 28
            half.append(p[:, :E // 2])
        for l in range(1, L):
            e[0, g, half[l]] = half[l - 1]
            e[1, g, half[l]] = half[l - 1][::-1]
        x[g] = v
    x = np.ascontiguousarray(x.reshape(128, N, 4 * C).transpose(1, 0, 2)).astype(np.float32).astype(BF)
    return inputs(rng, x, fit(rng, e, lev), lev, still(), still())
def setup_inputs_crowd(rng):
    lev = levels(rng)
    e, x = np.full((2, 8, N * C), -1), np.zeros((8, 16, N * C, 4))
    by, h, some = lev.reshape(N, C), CAP // 2, rng.permutation(8)
    for g in range(8):
        v = rng.integers(1, 32, (16, N * C, 4)) * rng.choice([-1.0, 1.0], (16, N * C, 4)) * 2.0 ** -13
        half = [rng.permutation(np.flatnonzero(lev == l)).reshape(2, -1) for l in range(L)]
        v[::8, half[0][0], 0] = 28
        v[::8, half[0][1], 0] = -28
        x[g] = v
        if g in some[L:]:
            for l in range(1, L):
                e[0, g, half[l][:, :E // 2]] = half[l - 1][:, :E // 2]
                e[1, g, half[l][:, :E // 2]] = half[l - 1][::-1, :E // 2]
            continue
        p = rng.permutation(N)
        for k in range(2):
            free = np.ones((N, C), bool)
            for l in range(1, L):
                if g == some[0]:
                    to = C * p[0] + rng.permutation(np.flatnonzero(by[p[0]] == l))
                    for j in range(N - 1):
                        s, t = p[j + 1], to[h * j:h * j + h]
                        a = rng.permutation(np.flatnonzero((by[s] < l) & free[s]))[:t.size]
                        e[k, g, t] = C * s + a
                        free[s, a] = False
                elif g == some[l]:
                    a = C * p[0] + rng.permutation(np.flatnonzero(by[p[0]] < l))
                    for j in range(N - 1):
                        r, t = p[j + 1], a[h * j:h * j + h]
                        e[k, g, C * r + rng.permutation(np.flatnonzero(by[r] == l))[:t.size]] = t
    x = np.ascontiguousarray(x.reshape(128, N, 4 * C).transpose(1, 0, 2)).astype(np.float32).astype(BF)
    return inputs(rng, x, fit(rng, e, lev), lev, still(36), still())
def setup_inputs_spread(rng):
    d = setup_inputs(rng)
    d["x"] = big(wide(rng, N, 128, 4 * C, cols=6))
    return d
def check_inputs(d):
    b = []
    for k in ("x", "u"):
        a = np.abs(d[k].astype(np.float32))
        if not (np.isfinite(a).all() and ((a == 0) | (a >= 2.0 ** -30) & (a <= 2.0 ** 30)).all()): b.append("a value of " + k)
    lev = np.concatenate([entries(a) for a in d["lv"]])
    if not all((np.sum(lev.reshape(N, C) == l, axis=1) == M).all() for l in range(L)): b.append("a number of columns of a level")
    e = np.stack([np.concatenate([gentries(a) for a in d[k]], axis=1) for k in ("pr0", "pr1")]).astype(np.int64)
    ok = (e >= -1) & (e < N * C)
    if not ok.all(): b.append("an entry out of range")
    e = np.where(ok, e, -1)
    if ((e >= 0) & (lev[np.maximum(e, 0)] >= lev)).any(): b.append("a predecessor that isn't of a lower level")
    s = np.sort(e, axis=2)
    if ((s[:, :, 1:] == s[:, :, :-1]) & (s[:, :, 1:] >= 0)).any(): b.append("a number twice in a list of a group")
    if np.bincount(pairs_of(e, np.clip(lev, 0, L - 1)).reshape(-1) + 1)[1:].max(initial=0) > CAP: b.append("too many entries of two ranks in a group and a level")
    return b
def sweep(base, links, lev, steps, layer):
    got = np.zeros((128, 4 * N * C), BF)
    kept, order = [], []
    for l in steps:
        at = np.flatnonzero(lev == l)
        a, b = [gcols(got, e[:, at]).astype(np.float32) for e in links]
        t = (base.reshape(128, -1, 4)[:, at].reshape(128, -1) - (a + b) * np.float32(0.5)).astype(BF)
        q = mx_ref.quantize(np.ascontiguousarray(t))
        made = []
        for r in range(N):
            mine = pick(q, np.arange(M * r, M * r + M))
            made.append(tile([mx_ref.matmul(pick(layer[r], np.arange(128 * i, 128 * i + 128)), mine) * np.float32(0.03125) for i in range(4)]))
        z = mx_ref.quantize(np.ascontiguousarray(np.concatenate(made, axis=1)))
        got.reshape(128, -1, 4)[:, at] = decode(z).astype(BF).reshape(128, -1, 4)
        kept.append(z)
        order.append(at)
    return pick(join(*kept), np.argsort(np.concatenate(order))), got
def reference(x, lv, pr0, pr1, u, wc, ws, vc, vs):
    lev = np.concatenate([entries(lv[r]) for r in range(N)])
    pr = [np.concatenate([gentries(a[r]) for r in range(N)], axis=1) for a in (pr0, pr1)]
    su = []
    for e in pr:
        i = np.full((8, N * C + 1), -1)
        i[np.arange(8)[:, None], e] = np.arange(N * C)
        su.append(i[:, :N * C])
    first = decode(mx_ref.quantize(np.ascontiguousarray(np.concatenate([x[r] for r in range(N)], axis=1))))
    qy, dy = sweep(first, pr, lev, range(L), [pk(wc[r], ws[r]) for r in range(N)])
    qz, dz = sweep(dy.astype(np.float32), su, lev, range(L - 1, -1, -1), [pk(vc[r], vs[r]) for r in range(N)])
    y = np.zeros((N, 128, C), np.float32)
    oc, osc = np.zeros((N, 128, 4 * C), np.uint8), np.zeros((N, 16, C), np.uint8)
    for r in range(N):
        mine = pick(qz, np.arange(C * r, C * r + C))
        y[r] = mx_ref.matmul(mx_ref.quantize(u[r]), mine)
        oc[r], osc[r] = emit(mine)
    return {"y": y, "oc": oc, "osc": osc}

@@ -1,0 +1,601 @@
+from concourse.bass import DstId, RemoteDMATransfer
+from concourse.mybir import dt, AluOpType, ActivationFunctionType
+
+N, C, M, CAP = 8, 288, 96, 32
+K = (N - 1) * CAP
+F, B, I, U, X4, SC = "float32", "bfloat16", "int32", "uint16", "float8_e4m3fn_x4", "uint8"
+ROUND = 12582912
+EMPTY = 4095 + 4096 * (128 + M)
+
+PACK_U = "PERM DUPO KOFF SEGO CODE POSU POSZ INV0 OI PFO OFU HI2 LO2 JU JO SUO OF1 OF2 OF3 OF4 G2 G3 G4 DBL".split()
+PACK_F = "t1 t2 t3 t4 TA TB TC TT TW D1 D2 D3 W32 OFF1 OFF2 PC1 PC2 KC1 KC2 CB CJ IDXC POSW".split()
+PLACE = {}
+
+
+def _scratch():
+    s = {}
+    for n, w, d in [
+        ("IOTA", 2308, F), ("PI", 4, I), ("CC", 16, F), ("J16", 224, F), ("JT", 224, F), ("DIAG", 224, B), ("RESET", 224, B),
+        ("KEYC", 128, F), ("CJ", 14, F), ("CB", 8, F), ("IDXC", 26, F), ("E4096", 192, F), ("VAL2", 416, F), ("VAL1", 416, F),
+        ("PERM", 18, U), ("DUPO", 4, U), ("KOFF", 8, U), ("SEGO", 8, U), ("ID", 128, B),
+        ("ET", 2048, B), ("LV1", 288, I), ("LVB", 288, I), ("PR", 36, I), ("CODE", 36, U), ("PF", 576, F),
+        ("t1", 36, F), ("t2", 36, F), ("t3", 36, F), ("t4", 36, F), ("i1", 32, I), ("i2", 32, I), ("i3", 32, I),
+        ("MK", 288, B), ("MKP", 288, B), ("L1", 384, F), ("L2", 384, F), ("L3", 384, F), ("MKL", 384, B), ("SD", 384, F),
+        ("POSW", 18, F), ("POSU", 18, U), ("POSS", 18, U), ("POSZ", 18, U), ("POSF", 292, F), ("PP", 148, F), ("PPU", 144, U),
+        ("INVF", 288, F), ("SCI", 288, F), ("INV0", 6, U), ("OI", 72, U), ("PFO", 24, U),
+        ("NW1", 192, F), ("NW2", 192, F), ("NV", 192, F), ("TW", 16, F), ("TT", 32, F), ("TA", 32, F), ("TB", 32, F), ("TC", 32, F),
+        ("OFF1", 16, F), ("OFF2", 16, F), ("OFU", 12, U), ("TL1", 416, F), ("TL2", 416, F), ("WL1", 14, F), ("WL2", 14, F),
+        ("LL1", 14, F), ("LL2", 14, F), ("HI2", 24, U), ("LO2", 24, U), ("JU", 14, U), ("JO", 12, U),
+        ("PC1", 26, F), ("PC2", 26, F), ("KC1", 26, F), ("KC2", 26, F), ("SUO", 26, U), ("SU", 800, F),
+        ("W32", 32, F), ("D1", 32, F), ("D2", 64, F), ("D3", 64, F), ("DBL", 24, U),
+        ("OF1", 32, U), ("OF2", 64, U), ("OF3", 32, U), ("OF4", 32, U), ("G2", 56, U), ("G3", 56, U), ("G4", 56, U),
+        ("TXN", 1152, B), ("X0", 1152, B), ("TY0", 1152, B), ("TX", 512, B), ("TYS", 896, B), ("TY2", 512, B),
+        ("TZ2", 512, B), ("TZ1", 512, B), ("TZ0", 512, B), ("SG", 1024, B), ("DS", 768, B), ("DY", 768, B),
+        ("TU", 512, B), ("YO", 288, F), ("HP", 18, U), ("HL1", 2, F), ("HL2", 2, F),
+    ]:
+        s[n] = ("sbuf", [128, w], d)
+    for n, w in [("QE", 512), ("QH0", 512), ("QH1", 512), ("QW", 512), ("QV", 512), ("QU", 128), ("QS", 384), ("QX0", 288),
+                 ("QY0", 288), ("QX", 128), ("QY2", 128), ("WF1", 896), ("WF2", 448), ("WB", 832), ("QO", 288),
+                 ("P1", 448), ("P2", 448), ("P3", 448), ("P4", 448), ("S2", 256), ("S3", 256), ("S4", 256)]:
+        s[n + "c"] = ("sbuf", [128, w], X4)
+        s[n + "s"] = ("sbuf", [128, w], SC)
+    for n, w in [("H1", 96), ("H2", 64), ("H3", 64), ("H4", 64)]:
+        s[n + "c"] = ("sbuf", [128, w], X4)
+        s[n + "s"] = ("sbuf", [128, 4 * w], SC)
+    for arena, d, names in (("AU", U, PACK_U), ("AF", F, PACK_F)):
+        at = 0
+        for n in names:
+            PLACE[n] = (arena, at, s[n][1][1])
+            at += -(-s.pop(n)[1][1] // 16) * 16
+        s[arena] = ("sbuf", [128, at], d)
+    s["PA"] = ("psum", [128, 2048], F)
+    s["PB"] = ("psum", [128, 2048], F)
+    return s
+
+
+SCRATCH = _scratch()
+SEMAPHORES = (["cv", "ca", "cp", "cg", "ls"] + ["d%d" % i for i in range(18)] + ["xp", "xl1", "xl2", "x1", "x2", "x3", "x4"]
+              + ["hp", "hl1", "hl2"] + ["hc%d" % i for i in (1, 2, 3, 4)] + ["hs%d" % i for i in (1, 2, 3, 4)])
+BIG = {1: ("QS", "WF1", M, 0), 2: ("S2", "WF2", CAP, 0), 3: ("S3", "WB", CAP, 0), 4: ("S4", "WB", CAP, K + 128)}
+SMALL = {"p": ("POSS", "HP", "PPU", 18), "l2": ("WL2", "HL2", "LL2", 2), "l1": ("WL1", "HL1", "LL1", 2)}
+ORDER = ["p", 1, "l2", 2, 3, "l1", 4]
+
+
+def _bits(engines):
+    return sum(1 << e for e in engines)
+
+
+def _helpers(topo, rc):
+    rest = [c for c in topo.cores_of(rc) if c != rc]
+    near = [c for c in rest if topo.die(c) == topo.die(rc)]
+    far = [c for c in rest if topo.die(c) != topo.die(rc)]
+    mixed = []
+    while near or far:
+        if near: mixed.append(near.pop(0))
+        if far: mixed.append(far.pop(0))
+    return mixed
+
+
+def _to(topo, src, dst, mask, sem, a, b):
+    rid, pid = topo.addr(dst, src)
+    return RemoteDMATransfer(dst_ids=[DstId(rid=rid, pnc=pid)], dma_engine_mask=mask, remote_sem=sem, src=a, dst=b)
+
+
+def _land(k, r, u):
+    return M * r if k == 1 else BIG[k][3] + CAP * (N - 2 - u)
+
+
+def helper_program(g, core, T, topo, r, h):
+    peer = [T.cores[(r + 1 + u) % N] for u in range(N - 1)]
+    eng = topo.engines(core, peer[0])
+    half = len(eng) // 2
+    sent = 0
+    for k in ORDER:
+        if k in SMALL:
+            _s, hb, land, w = SMALL[k]
+            g.wait_ge(T.sem["h" + k], 2)
+            o = w * (N - 2 - h)
+            g.remote_dma_fused([_to(topo, core, peer[h], _bits(eng), T.sem["x" + k], T[hb][:, 0:w], T[land][:, o:o + w])], local_sem=T.sem.ls)
+            sent += len(eng)
+            continue
+        _s, land, w, _o = BIG[k]
+        jobs = []
+        if h <= 3: jobs.append(("c", [u for u in (2 * h, 2 * h + 1) if u < N - 1]))
+        if h >= 3: jobs.append(("s", [N - 2] if h == 3 else [2 * (h - 4), 2 * (h - 4) + 1]))
+        at = 0
+        for kind, us in jobs:
+            g.wait_ge(T.sem["h%s%d" % (kind, k)], 2)
+            ts = []
+            for u in us:
+                o = _land(k, r, u)
+                a = 0 if k == 1 else (w * (u % 2) if kind == "c" else w * u)
+                src, dst = T["H%d%s" % (k, kind)][:, a:a + w], T[land + kind][:, o:o + w]
+                if kind == "c": src, dst = src.bitcast(dt.uint8), dst.bitcast(dt.uint8)
+                ts.append(_to(topo, core, peer[u], _bits(eng[half * at:half * at + half]), T.sem["x%d" % k], src, dst))
+                at += 1
+                sent += half
+            g.remote_dma_fused(ts, local_sem=T.sem.ls)
+    g.wait_ge(T.sem.ls, sent)
+
+
+def rank_program(g, core, T, topo):
+    r = T.rank_of(core)
+    if r is None:
+        for i, rc in enumerate(T.cores):
+            if core in topo.cores_of(rc):
+                helper_program(g, core, T, topo, i, _helpers(topo, rc).index(core))
+        return
+    A, ACT = AluOpType, ActivationFunctionType
+    queue = {"v": g.vector, "a": g.scalar, "p": g.tensor, "g": g, "s": g.sync}
+    count = {"v": 0, "a": 0, "p": 0, "g": 0, "ls": 0, "d": 0}
+    known = {e: {} for e in queue}
+    log = {}
+    final = {}
+
+    def V(name, a=0, b=None, step=1):
+        if name in PLACE:
+            name, at, w = PLACE[name]
+            a, b = at + a, at + (w if b is None else b)
+        b = T[name].shape[1] if b is None else b
+        ap = T[name][:, a:b] if step == 1 else T[name][:, a:b:step]
+        return (ap, [(name, a, b, step)])
+
+    def bank(name, i, n):
+        return (T[name][:, 512 * i:512 * i + n], [(name, 512 * i, 512 * i + 512, 1)])
+
+    def ind(win, off):
+        return (win[0].indirect(off[0]), win[1] + off[1])
+
+    def words(v):
+        return (v[0].bitcast(dt.uint32), v[1])
+
+    def meet(a, b):
+        if a[1] >= b[2] or b[1] >= a[2]: return False
+        return not (a[3] > 1 and a[3] == b[3] and (a[1] - b[1]) % a[3] != 0)
+
+    def wait(e, tok):
+        if known[e].get(tok[0], 0) >= tok[1]: return
+        queue[e].wait_ge(T.sem[tok[0]], tok[1])
+        for s, n in list(tok[2].items()) + [(tok[0], tok[1])]:
+            known[e][s] = max(known[e].get(s, 0), n)
+
+    def order(e, reads, writes, acc=False):
+        rs = [x for v in reads if isinstance(v, tuple) for x in v[1]]
+        ws = [x for v in writes for x in v[1]] + [x for x in rs if x[0] in ("PA", "PB")]
+        need = {}
+        for x, w in [(x, False) for x in rs] + [(x, True) for x in ws]:
+            for y, yw, tok in log.get(x[0], []):
+                if (w or yw) and meet(x, y) and not (acc and w and tok[0] == "cp"):
+                    if tok[0] not in need or need[tok[0]][1] < tok[1]: need[tok[0]] = tok
+        for tok in sorted(need.values(), key=lambda t: -len(t[2])):
+            wait(e, tok)
+        return rs, ws
+
+    def note(rs, ws, tok):
+        for x in rs: log.setdefault(x[0], []).append((x, False, tok))
+        for x in ws: log.setdefault(x[0], []).append((x, True, tok))
+        final[tok[0]] = max(final.get(tok[0], 0), tok[1])
+
+    def op(e, call, writes, reads, acc=False):
+        rs, ws = order(e, reads, writes, acc)
+        count[e] += 1
+        call().then_inc(T.sem["c" + e], 1)
+        note(rs, ws, ("c" + e, count[e], dict(known[e])))
+
+    def raw(v):
+        return v[0] if isinstance(v, tuple) else v
+
+    def dma(e, out, in_):
+        rs, ws = order(e, [in_], [out])
+        s = "d%d" % count["d"]
+        count["d"] += 1
+        queue[e].dma_start(out[0], in_[0]).then_inc(T.sem[s], 16)
+        note(rs, ws, (s, 16, dict(known[e])))
+
+    def ext(ap):
+        return (ap, [])
+
+    def memset(o, c): op("v", lambda: g.vector.memset(o[0], c), [o], [])
+    def copy(o, i): op("v", lambda: g.vector.tensor_copy(o[0], i[0]), [o], [i])
+    def tt(o, a, b, f): op("v", lambda: g.vector.tensor_tensor(o[0], a[0], b[0], f), [o], [a, b])
+    def tr(o, i): op("v", lambda: g.vector.transpose(o[0], i[0]), [o], [i])
+
+    def ts(o, a, s1, f1, s2=None, f2=None):
+        if f2 is None: op("v", lambda: g.vector.tensor_scalar(o[0], a[0], raw(s1), None, f1), [o], [a, s1])
+        else: op("v", lambda: g.vector.tensor_scalar(o[0], a[0], raw(s1), raw(s2), f1, f2), [o], [a, s1, s2])
+
+    def scan(o, a, b, init, f0, f1):
+        op("v", lambda: g.vector.tensor_tensor_scan(o[0], a[0], b[0], raw(init), f0, f1), [o], [a, b, init])
+
+    def act(o, i, f=ACT.Copy, bias=None, scale=None):
+        kw = {}
+        if bias is not None: kw["bias"] = raw(bias)
+        if scale is not None: kw["scale"] = raw(scale)
+        op("a", lambda: g.scalar.activation(o[0], i[0], f, **kw), [o], [i, bias, scale])
+
+    def iota(o, pat, base, cm, fl=True):
+        if fl: op("g", lambda: g.iota(o[0], pat, base, cm, allow_small_or_imprecise_dtypes=True), [o], [])
+        else: op("g", lambda: g.iota(o[0], pat, base, cm), [o], [])
+
+    def quant(q, a, n, tile):
+        c, s = V(q + "c", a, a + n), V(q + "s", a, a + n)
+        op("v", lambda: g.vector.quantize_mx(c[0], s[0], tile[0]), [c, s], [tile])
+
+    def mm(out, w, wa, x, xa, n, start=True, stop=True):
+        wc, ws, xc, xs = V(w + "c", wa, wa + 128), V(w + "s", wa, wa + 128), V(x + "c", xa, xa + n), V(x + "s", xa, xa + n)
+        op("p", lambda: g.tensor.matmul_mx(out[0], wc[0], ws[0], xc[0], xs[0], start, stop), [out], [wc, ws, xc, xs], acc=not start)
+
+    def pick(q, a, win, wn, off, n):
+        copy(words(V(q + "c", a, a + n)), ind(words(V(win + "c", 0, wn)), off))
+        act(V(q + "s", a, a + n), ind(V(win + "s", 0, wn), off))
+
+    def col(i): return V("CC", i, i + 1)
+
+    def fold(o, table, n):
+        tt(V("L1", 0, n), table, V("DIAG", 0, n), A.mult)
+        scan(o, V("RESET", 0, n), V("L1", 0, n), 0.0, A.mult, A.add)
+
+    peer = [T.cores[(r + 1 + u) % N] for u in range(N - 1)]
+    help_ = _helpers(topo, core)
+    out_engines = len(topo.engines(core, peer[0]))
+
+    def fused(ts_, srcs):
+        order("g", srcs, [])
+        g.remote_dma_fused(ts_, local_sem=T.sem.ls)
+        count["ls"] += 2 * len(ts_)
+
+    def arrives(views, sem):
+        note([], [x for v in views for x in v[1]], (sem, (N - 1) * out_engines, {}))
+
+    def send_small(k):
+        src, hb, land, w = SMALL[k]
+        tsf = []
+        for u in range(N - 1):
+            a, e = (0 if k == "p" else w * u), topo.engines(core, help_[u])
+            tsf.append(_to(topo, core, help_[u], _bits(e[2 * u:2 * u + 2]), T.sem["h" + k], T[src][:, a:a + w], T[hb][:, 0:w]))
+        fused(tsf, [V(src)])
+        arrives([V(land, 0, w * (N - 1))], "x" + k)
+
+    def send_big(k):
+        src, land, w, o0 = BIG[k]
+        tsf = []
+        hw = w if k == 1 else 2 * w
+        for i in range(8):
+            h = help_[i if i < 7 else 3]
+            e = topo.engines(core, h)
+            if i < 4:
+                a = 0 if k == 1 else hw * i
+                s, d = T[src + "c"][:, a:a + hw].bitcast(dt.uint8), T["H%dc" % k][:, 0:hw].bitcast(dt.uint8)
+            else:
+                s, d = T[src + "s"][:, 0:4 * hw], T["H%ds" % k][:, 0:4 * hw]
+            tsf.append(_to(topo, core, h, _bits(e[2 * i:2 * i + 2]), T.sem["h%s%d" % ("c" if i < 4 else "s", k)], s, d))
+        fused(tsf, [V(src + "c"), V(src + "s")])
+        if k == 1:
+            views = [V(land + c, M * s, M * s + M) for c in "cs" for s in range(N) if s != r]
+        else:
+            views = [V(land + c, o0, o0 + K) for c in "cs"]
+        arrives(views, "x%d" % k)
+
+    def scatter(win, off, val):
+        op("v", lambda: g.vector.tensor_copy(win[0].indirect(off[0]), val[0]), [win], [off, val])
+
+    def fill(name, a, b, c):
+        act(V(name, a, b), V("IOTA", 0, b - a), ACT.Identity, bias=float(c), scale=0.0)
+
+    def lin(o, i, scale, bias):
+        act(o, i, ACT.Identity, bias=bias, scale=scale)
+
+    u8 = lambda v: (v[0].bitcast(dt.uint8), v[1])
+    lvb, lv1 = V("LVB"), (T.LV1[0:1, :], V("LV1")[1])
+    dma("a", lv1, ext(T.lv[:]))
+    dma("s", V("TXN"), ext(T.x[:]))
+    dma("a", V("PR", 0, 18), ext(T.pr0[:]))
+    dma("a", V("PR", 18, 36), ext(T.pr1[:]))
+    dma("s", V("QWs"), ext(T.ws[:]))
+    dma("s", u8(V("QWc")), ext(T.wc[:]))
+    dma("s", V("QVs"), ext(T.vs[:]))
+    dma("s", u8(V("QVc")), ext(T.vc[:]))
+    dma("s", V("TU"), ext(T.u[:]))
+
+    iota(V("PI", 0, 1), [[1, 1]], 0, 1, fl=False)
+    iota(V("IOTA", 0, 577), [[1, 577]], 0, 0)
+    op("g", lambda: g.partition_broadcast(lvb[0], lv1[0], 128), [lvb], [lv1])
+    iota(V("J16"), [[0, 14], [1, 16]], 0, 0)
+    iota(V("KEYC"), [[1, 8], [0, 16]], ROUND, 0)
+    iota(V("CJ"), [[-C, N - 1], [0, 2]], C * (N - 2) - 1, 0)
+    memset(V("ET"), 0.0)
+    ts(V("PI", 1, 2), V("PI", 0, 1), 15, A.bitwise_and)
+    ts(V("PI", 2, 3), V("PI", 0, 1), 4, A.logical_shift_right, 1, A.bitwise_and)
+    copy(V("CC", 0, 3), V("PI", 0, 3))
+    for b in range(4):
+        ts(V("ET", 512 * b + b, 512 * b + 512, 4), V("IOTA", 0, 128), col(0), A.is_equal)
+    ts(col(4), col(1), 18.0, A.mult, col(2), A.add)
+    quant("QE", 0, 512, V("ET"))
+    for h in range(2):
+        ts(V("PERM", h, 18, 2), V("IOTA", 0, 18, 2), col(4), A.add)
+    lin(col(3), col(1), float(M), 0.0)
+    lin(V("CC", 5, 7), V("CC", 0, 2), -1.0, 0.0)
+    lin(V("IOTA", 577, 1154), V("IOTA", 0, 577), 1.0, 577.0)
+    lin(V("IOTA", 1154, 1731), V("IOTA", 0, 577), 1.0, 1154.0)
+
+    quant("QS", M, C, V("TXN"))
+    for b in range(4):
+        mm(bank("PA", b, C), "QE", 128 * b, "QS", M, C)
+    ts(V("MK"), V("LVB"), col(1), A.is_equal)
+    act(V("MKP"), ind(V("MK"), V("PERM")))
+    for b in range(4):
+        act(V("X0", b, 4 * C, 4), bank("PA", b, C))
+    act(V("JT"), V("J16"), ACT.Abs, bias=col(6))
+    act(V("DIAG"), V("JT"), ACT.Relu, bias=1.0, scale=-1.0)
+    act(V("RESET"), V("J16"), ACT.Sign)
+    scan(V("L1", 0, C), V("MK"), V("MK"), col(3), A.add, A.max)
+    ts(V("t1"), V("PR"), -float(C * (r + 1)), A.add)
+    ts(V("t3"), V("PR"), 0.0, A.is_lt, float(C * (r + 1) + 1), A.mult)
+    tt(V("L3", 0, C), ind(V("L1", 0, C), V("PERM")), V("MKP"), A.mult)
+    ts(V("t2"), V("t1"), 0.0, A.is_lt, float(N * C), A.mult)
+    tr(V("L1", 0, C), V("L3", 0, C))
+    tt(V("t4"), V("t1"), V("t3"), A.add)
+    tt(V("TA", 0, 18), V("L1", 0, C, 16), V("L1", 1, C, 16), A.add)
+    tt(V("t1"), V("t4"), V("t2"), A.add)
+    tt(V("POSW"), V("TA", 0, 18), V("L1", 2, C, 16), A.add)
+    ts(V("POSS"), V("POSW"), float(M * r - 1), A.add)
+    ts(V("POSU"), V("POSW"), -1.0, A.add)
+    quant("QX0", 0, C, V("X0"))
+    send_small("p")
+    copy(V("CODE"), V("t1"))
+    for b in range(4):
+        mm(bank("PB", b, C), "QW", 128 * b, "QX0", 0, C)
+    for b in range(4):
+        act(V("TY0", b, 4 * C, 4), bank("PB", b, C), scale=0.03125)
+    dma("s", V("PPU", 126, 144), V("POSS"))
+    scatter(V("INVF"), V("POSU"), V("IOTA", 0, C))
+    fold(V("SCI", 0, M), V("INVF", 0, M), M)
+    copy(V("INV0"), V("SCI", 15, M, 16))
+    lin(V("IOTA", 1731, 2308), V("IOTA", 0, 577), 1.0, 1731.0)
+    quant("QY0", 0, C, V("TY0"))
+    pick("QS", 0, "QY0", C, V("INV0"), M)
+    send_big(1)
+
+    def codes(l):
+        fold(V("NW%d" % l), ind(V("PF"), V("PFO", 12 * (l - 1), 12 * l)), 2 * M)
+
+    def lists(l):
+        nw, off, tl = V("NW%d" % l, 15, 2 * M, 16), "OFF%d" % l, "TL%d" % l
+        ts(V("t2", 0, 12), nw, float(N * C - 1), A.min, -143.5, A.add)
+        ts(V("TW", 0, 12), V("t2", 0, 12), 1.0 / C, A.mult, float(ROUND), A.add)
+        tt(V("L2", 0, 128), ind(V("TW"), V("KOFF")), V("KEYC"), A.is_equal)
+        scan(V("L3", 0, 128), V("RESET", 0, 128), V("L2", 0, 128), 0.0, A.mult, A.add)
+        copy(V("TT", 0, 8), V("L3", 15, 128, 16))
+        tr(V("TA"), V("TT"))
+        tt(V("NV"), ind(V("PF"), V("PFO", 12 * (l - 1), 12 * l)), V("E4096"), A.add)
+        scan(V("TB", 1, 32), V("TA", 0, 31), V("RESET", 1, 32), 0.0, A.add, A.mult)
+        tr(V("TC"), V("TB"))
+        tt(V("t2", 0, 8), V("TC", 0, 8), V("CB"), A.add)
+        tt(V("L1", 0, 128), ind(V("t2", 0, 8), V("SEGO")), V("L3", 0, 128), A.add)
+        tt(V("L3", 128, 256), V("L1", 0, 128), V("L2", 0, 128), A.mult)
+        tt(V("L1", 128, 192), V("L3", 128, 192), V("L3", 192, 256), A.add)
+        tt(V("L1", 192, 224), V("L1", 128, 160), V("L1", 160, 192), A.add)
+        tt(V(off), V("L1", 192, 208), V("L1", 208, 224), A.add)
+        copy(V("OFU"), V(off, 0, 12))
+        scatter(V(tl), V("OFU"), V("NV"))
+        fold(V("L2", 0, K), V(tl, 0, K), K)
+        copy(V("WL%d" % l), V("L2", 15, K, 16))
+        send_small("l%d" % l)
+
+    def unit(c):
+        for b in range(4):
+            act(V("ET", 512 * b + b, 512 * b + 512, 4), V("ID"), scale=c)
+
+    act(V("PF"), ind(V("IOTA"), V("CODE")))
+    lin(V("CB"), V("IOTA", 0, 8), float(CAP), -1.0)
+    fill("TW", 12, 16, 0)
+    fill("TT", 0, 32, 0)
+    fill("TB", 0, 1, 0)
+    for k in range(2):
+        lin(V("E4096", M * k, M * k + M), V("IOTA", 128 * k, 128 * k + M), 4096.0, 0.0)
+    fill("TL2", 0, K, EMPTY)
+    lin(col(8), col(2), 0.5, 0.0)
+    lin(col(7), col(2), -0.5, 0.5)
+    act(V("JT", 0, 128), V("IOTA", 0, 128), ACT.Abs, bias=col(5))
+    act(V("ID"), V("JT", 0, 128), ACT.Relu, bias=1.0, scale=-1.0)
+    unit(col(7))
+    fold(V("SCI", M, C), V("INVF", M, C), 2 * M)
+    ts(V("KOFF"), V("IOTA", 0, 8), 0.0, A.mult, col(1), A.add)
+    copy(V("SEGO"), V("IOTA", 0, 8))
+    for l in (2, 1):
+        for k in range(2):
+            a = 12 * (l - 1) + 6 * k
+            ts(V("PFO", a, a + 6), V("SCI", M * l + 15, M * l + M, 16), float(C * k), A.add)
+    for t in range(4):
+        ts(V("OI", 18 * t, 18 * t + 18), V("SCI", 15, C, 16), 4.0, A.mult, float(t), A.add)
+    codes(2)
+    fill("TX", 0, 512, 0)
+    for t in range(4):
+        act(V("DS", 192 * t, 192 * t + 192), ind(V("X0"), V("OI", 18 * t + 6, 18 * t + 18)))
+    for t in range(4):
+        act(V("TYS", t, 4 * M, 4), ind(V("TY0"), V("OI", 18 * t, 18 * t + 6)))
+    lists(2)
+    quant("QH0", 0, 512, V("ET"))
+    unit(col(8))
+    act(V("POSF", 1, C + 1), ind(V("IOTA", 0, C), V("POSU")))
+    fill("PP", 144, 148, N * M)
+    fill("POSF", 0, 1, 2 * M)
+    fill("POSF", C + 1, C + 2, 2 * M)
+    codes(1)
+    for h in range(2):
+        copy(V("i1", h, 24, 2), V("NW1", 15, 2 * M, 16))
+    memset(V("OF1"), 0)
+    ts(V("i2", 0, 24), V("i1", 0, 24), 15, A.bitwise_and)
+    ts(V("i3", 0, 24), V("i1", 0, 24), 4, A.logical_shift_right)
+    copy(V("LO2"), V("i2", 0, 24))
+    copy(V("HI2"), V("i3", 0, 24))
+    act(V("MKL"), ind(V("DIAG", 0, 16), V("LO2")))
+    quant("QH1", 0, 512, V("ET"))
+    quant("WF1", N * M, 128, V("TX"))
+    pick("WF1", M * r, "QY0", C, V("INV0"), M)
+    fill("TYS", 8 * M, 896, 0)
+    fill("SG", 4 * K, 1024, 0)
+    copy(V("PP", 0, 144), V("PPU"))
+    tt(V("L2"), ind(V("PP"), V("HI2")), V("MKL"), A.mult)
+    tr(V("L3"), V("L2"))
+    for h in range(2):
+        scan(V("L1", 192 * h, 192 * h + 192), V("RESET", 0, 192), V("L3", 192 * h, 192 * h + 192), 0.0, A.mult, A.add)
+    for h in range(2):
+        copy(V("OF1", 16 * h, 16 * h + 12), V("L1", 16 * h + 15, 384, 32))
+
+    def gather_sum(p, win, wn, of, second, d, between=None):
+        for h in range(2):
+            pick(p, K * h, win, wn, V(of, second * h, second * h + 14), K)
+        for h in range(2):
+            for b in range(4):
+                for k in range(2):
+                    mm(bank("PA", b, 128), "QH%d" % h, 128 * b, p, K * h + M * k, 128, start=(h, k) == (0, 0), stop=(h, k) == (1, 1))
+        if between: between()
+        for b in range(4):
+            tt(V("TX", b, 4 * M, 4), d(b), bank("PA", b, M), A.subtract)
+
+    def layer(w, tile, a):
+        quant("QX", 0, 128, V("TX"))
+        for b in range(4):
+            mm(bank("PB", b, 128), w, 128 * b, "QX", 0, 128)
+        for b in range(4):
+            o = V(tile, a + b, a + 4 * M, 4)
+            if b % 2: ts(o, bank("PB", b, M), 0.03125, A.mult)
+            else: act(o, bank("PB", b, M), scale=0.03125)
+
+    def compose(k, tile, off):
+        for t in range(4):
+            o, i = V("SG", t, 4 * K, 4), ind(V(tile), V(off, 14 * t, 14 * t + 14))
+            if t % 2: copy(o, i)
+            else: act(o, i)
+        quant("S%d" % k, 0, 256, V("SG"))
+        send_big(k)
+
+    def arrived(l):
+        copy(V("i1", 0, 14), V("LL%d" % l))
+        ts(V("i2", 0, 14), V("i1", 0, 14), 4095, A.bitwise_and)
+        tt(V("t2", 0, 14), V("i2", 0, 14), V("CJ"), A.subtract)
+        ts(V("JU"), V("t2", 0, 14), float(C + 1), A.min)
+        fold(V("L2", 0, K), ind(V("POSF", 0, C + 2), V("JU")), K)
+
+    def keep(l):
+        copy(V("PC%d" % l, 0, 14), V("L2", 15, K, 16))
+        ts(V("KC%d" % l, 0, 14), V("LL%d" % l), 4096.0 * 128, A.is_ge, float(2 * M), A.mult)
+
+    def own(l):
+        ts(V("JO"), V("NW%d" % l, 15, 2 * M, 16), -float(C * (N - 1) - 1), A.add)
+        fold(V("L2", 0, 2 * M), ind(V("POSF", 0, C + 2), V("JO")), 2 * M)
+        copy(V("PC%d" % l, 14, 26), V("L2", 15, 2 * M, 16))
+
+    def back_send(l, out):
+        copy(V("i1", 0, 14), V("WL%d" % l))
+        ts(V("i2", 0, 14), V("i1", 0, 14), 12, A.logical_shift_right, 127, A.bitwise_and)
+        for t in range(4):
+            ts(V(out, 14 * t, 14 * t + 14), V("i2", 0, 14), 4.0, A.mult, float(t), A.add)
+
+    def successors(l, of):
+        pc, kc = V("PC%d" % l), V("KC%d" % l)
+        ts(V("t2", 0, 26), pc, float(2 * M), A.is_ge)
+        tt(V("t3", 0, 26), pc, kc, A.add)
+        tt(V("t4", 0, 26), V("t2", 0, 26), V("IDXC"), A.mult)
+        memset(V(of), 0)
+        tt(V("t1", 0, 26), V("t3", 0, 26), V("t4", 0, 26), A.add)
+        copy(V("SUO"), V("t1", 0, 26))
+        scatter(V("SU"), V("SUO"), V("VAL%d" % l))
+        act(V("SD"), ind(V("SU", M * (l - 1), 4 * M), V("DBL")))
+
+    def successors_end(of):
+        tr(V("L3"), V("SD"))
+        for h in range(2):
+            copy(V(of, 16 * h, 16 * h + 12), V("L3", 16 * h, 384, 32))
+
+    def asked():
+        arrived(2)
+        for t in range(4):
+            ts(V("G2", 14 * t, 14 * t + 14), V("L2", 15, K, 16), 4.0, A.mult, float(t), A.add)
+
+    gather_sum("P1", "WF1", 896, "OF1", 16, lambda b: V("DS", 192 * b, 192 * b + M), asked)
+    layer("QW", "TYS", 4 * M)
+    compose(2, "TYS", "G2")
+    keep(2)
+    fill("W32", 0, 32, 0)
+    lin(V("IDXC"), V("IOTA", 0, 416, 16), 1.0, col(1))
+    lin(V("IDXC", 14, 20), V("IDXC", 14, 20), 1.0, float(2 * M))
+    for l in (2, 1):
+        fill("KC%d" % l, 14, 20, 0)
+        fill("KC%d" % l, 20, 26, 2 * M)
+    act(V("VAL2", 0, K + M), V("IOTA", 0, K + M))
+    act(V("VAL2", K + M, K + 2 * M), V("IOTA", K, K + M))
+    fill("SU", 0, 4 * M, K + M)
+    quant("WF2", K, K, V("TYS"))
+    for b in range(4):
+        mm(bank("PA", b, 2 * M), "QE", 128 * b, "WF2", K, 2 * M)
+    for b in range(4):
+        act(V("DY", 192 * b, 192 * b + 192), bank("PA", b, 2 * M))
+    for n in ("TY2", "TZ2", "TZ1", "TZ0"):
+        fill(n, 4 * M, 512, 0)
+    fill("TL1", 0, K, EMPTY)
+    lin(V("VAL1"), V("VAL2"), 1.0, float(K + 128))
+    for h in range(2):
+        ts(V("DUPO", h, 4, 2), V("IOTA", 0, 32, 16), col(1), A.add)
+    own(2)
+    ts(V("t1", 0, 12), V("OFF2", 0, 12), float(K), A.is_ge, 1000.0, A.mult)
+    ts(V("t2", 0, 12), V("PC2", 14, 26), float(K), A.add)
+    tt(V("t3", 0, 12), V("t1", 0, 12), V("OFF2", 0, 12), A.add)
+    for k in range(2):
+        ts(V("DBL", 12 * k, 12 * k + 12, 2), V("IOTA", 0, M, 16), col(1), A.add, float(2 * M * k), A.add)
+    tt(V("W32", 0, 12), V("t3", 0, 12), V("t2", 0, 12), A.min)
+    for k in range(2):
+        ts(V("DBL", 12 * k + 1, 12 * k + 12, 2), V("IOTA", 0, M, 16), col(1), A.add, float(2 * M * k), A.add)
+    tr(V("D1"), V("W32"))
+    copy(V("D2"), ind(V("D1"), V("DUPO")))
+    tr(V("D3"), V("D2"))
+    copy(V("OF2"), V("D3"))
+    successors(2, "OF3")
+    own(1)
+
+    gather_sum("P2", "WF2", 448, "OF2", 32, lambda b: V("DS", 192 * b + M, 192 * b + 2 * M), lambda: back_send(2, "G3"))
+    layer("QW", "TY2", 0)
+    quant("QY2", 0, 128, V("TY2"))
+    for b in range(4):
+        mm(bank("PA", b, 128), "QE", 128 * b, "QY2", 0, 128)
+    for b in range(4):
+        if b % 2: copy(V("TX", b, 4 * M, 4), bank("PA", b, M))
+        else: act(V("TX", b, 4 * M, 4), bank("PA", b, M))
+    layer("QV", "TZ2", 0)
+    compose(3, "TZ2", "G3")
+    lists(1)
+    quant("WB", K, 128, V("TZ2"))
+    successors_end("OF3")
+
+    gather_sum("P3", "WB", K + 128, "OF3", 16, lambda b: V("DY", 192 * b + M, 192 * b + 2 * M), lambda: back_send(1, "G4"))
+    layer("QV", "TZ1", 0)
+    compose(4, "TZ1", "G4")
+    arrived(1)
+    keep(1)
+    successors(1, "OF4")
+    quant("WB", 2 * K + 128, 128, V("TZ1"))
+    quant("QU", 0, 128, V("TU"))
+    successors_end("OF4")
+
+    def places():
+        ts(V("t1", 0, 18), V("POSW"), M + 0.5, A.is_ge, -float(K), A.mult)
+        ts(V("t2", 0, 18), V("POSW"), 2 * M + 0.5, A.is_ge, -float(2 * K), A.mult)
+        tt(V("t3", 0, 18), V("t1", 0, 18), V("POSW"), A.add)
+        tt(V("t4", 0, 18), V("t3", 0, 18), V("t2", 0, 18), A.add)
+        ts(V("POSZ"), V("t4", 0, 18), float(2 * K + 255), A.add)
+
+    gather_sum("P4", "WB", 2 * K + 256, "OF4", 16, lambda b: V("DY", 192 * b, 192 * b + M), places)
+    layer("QV", "TZ0", 0)
+    quant("WB", 2 * K + 256, 128, V("TZ0"))
+    pick("QO", 0, "WB", 832, V("POSZ"), C)
+    mm(bank("PA", 0, C), "QU", 0, "QO", 0, C)
+    scales = lambda k: dma("a" if k else "s", ext(T.osc[4 * k:4 * k + 4, :]), (T.QOs[32 * k:32 * k + 4, :], V("QOs")[1]))
+    dma("s", ext(T.oc[:]), u8(V("QOc")))
+    for k in range(4):
+        scales(k)
+    copy(V("YO"), bank("PA", 0, C))
+    dma("s", ext(T.y[:]), V("YO"))
+    g.wait_ge(T.sem.ls, count["ls"])
+    for s in sorted(final):
+        wait("g", (s, final[s], {}))

@@ -7,9 +7,12 @@ F, B, I, U, X4, SC = "float32", "bfloat16", "int32", "uint16", "float8_e4m3fn_x4
 ROUND = 12582912
 EMPTY = 4095 + 4096 * (128 + M)
 
-PACK_U = "PERM DUPO KOFF SEGO CODE POSU POSZ INV0 OI PFO OFU HI2 LO2 JU JO SUO OF1 OF2 OF3 OF4 G2 G3 G4 DBL".split()
-PACK_F = "t1 t2 t3 t4 TA TB TC TT TW D1 D2 D3 W32 OFF1 OFF2 PC1 PC2 KC1 KC2 CB CJ IDXC POSW".split()
+PACK_U = "DUPO KOFF SEGO DBL OF1 OF3 OF4 PERM CODE POSU POSZ INV0 OI PFO OFU HI2 LO2 JU JO SUO OF2 G2 G3 G4".split()
+PACK_F = "t1 t2 t3 t4 TA TB TC TT TW D1 D2 D3 W32 OFF1 OFF2 PC1 PC2 KC1 KC2 CB CJ IDXC POSW OIF".split()
 PLACE = {}
+TEMPS = "t1 t2 t3 t4 i1 i2 i3 L1 L2 L3".split()
+TRAVEL = {"p": 11.0, 1: 6.5, "l2": 4.0, 2: 4.5, 3: 4.5, "l1": 4.0, 4: 4.5}
+HOP = 0.12
 
 
 def _scratch():
@@ -17,32 +20,34 @@ def _scratch():
     for n, w, d in [
         ("IOTA", 2308, F), ("PI", 4, I), ("CC", 16, F), ("J16", 224, F), ("JT", 224, F), ("DIAG", 224, B), ("RESET", 224, B),
         ("KEYC", 128, F), ("CJ", 14, F), ("CB", 8, F), ("IDXC", 26, F), ("E4096", 192, F), ("VAL2", 416, F), ("VAL1", 416, F),
-        ("PERM", 18, U), ("DUPO", 4, U), ("KOFF", 8, U), ("SEGO", 8, U), ("ID", 128, B),
-        ("ET", 2048, B), ("LV1", 288, I), ("LVB", 288, I), ("PR", 36, I), ("CODE", 36, U), ("PF", 576, F),
+        ("PERM", 18, U), ("DUPO", 4, U), ("KOFF", 8, U), ("SEGO", 8, U), ("ID", 128, B), ("ST", 176, F), ("OIF", 72, F),
+        ("ET", 520, B), ("LV1", 288, I), ("LVB", 288, I), ("PR", 36, I), ("CODE", 36, U), ("PF", 576, F),
         ("t1", 36, F), ("t2", 36, F), ("t3", 36, F), ("t4", 36, F), ("i1", 32, I), ("i2", 32, I), ("i3", 32, I),
         ("MK", 288, B), ("MKP", 288, B), ("L1", 384, F), ("L2", 384, F), ("L3", 384, F), ("MKL", 384, B), ("SD", 384, F),
         ("POSW", 18, F), ("POSU", 18, U), ("POSS", 18, U), ("POSZ", 18, U), ("POSF", 292, F), ("PP", 148, F), ("PPU", 144, U),
         ("INVF", 288, F), ("SCI", 288, F), ("INV0", 6, U), ("OI", 72, U), ("PFO", 24, U),
         ("NW1", 192, F), ("NW2", 192, F), ("NV", 192, F), ("TW", 16, F), ("TT", 32, F), ("TA", 32, F), ("TB", 32, F), ("TC", 32, F),
-        ("OFF1", 16, F), ("OFF2", 16, F), ("OFU", 12, U), ("TL1", 416, F), ("TL2", 416, F), ("WL1", 14, F), ("WL2", 14, F),
+        ("OFF1", 16, F), ("OFF2", 16, F), ("OFU", 12, U), ("TL1", 416, F), ("TL2", 416, F), ("WL1", 16, F), ("WL2", 16, F),
         ("LL1", 14, F), ("LL2", 14, F), ("HI2", 24, U), ("LO2", 24, U), ("JU", 14, U), ("JO", 12, U),
         ("PC1", 26, F), ("PC2", 26, F), ("KC1", 26, F), ("KC2", 26, F), ("SUO", 26, U), ("SU", 800, F),
         ("W32", 32, F), ("D1", 32, F), ("D2", 64, F), ("D3", 64, F), ("DBL", 24, U),
         ("OF1", 32, U), ("OF2", 64, U), ("OF3", 32, U), ("OF4", 32, U), ("G2", 56, U), ("G3", 56, U), ("G4", 56, U),
         ("TXN", 1152, B), ("X0", 1152, B), ("TY0", 1152, B), ("TX", 512, B), ("TYS", 896, B), ("TY2", 512, B),
         ("TZ2", 512, B), ("TZ1", 512, B), ("TZ0", 512, B), ("SG", 1024, B), ("DS", 768, B), ("DY", 768, B),
-        ("TU", 512, B), ("YO", 288, F), ("HP", 18, U), ("HL1", 2, F), ("HL2", 2, F),
+        ("TU", 512, B), ("YO", 288, F), ("HP", 18, U), ("HL1", 4, F), ("HL2", 4, F),
     ]:
         s[n] = ("sbuf", [128, w], d)
     for n, w in [("QE", 512), ("QH0", 512), ("QH1", 512), ("QW", 512), ("QV", 512), ("QU", 128), ("QS", 384), ("QX0", 288),
                  ("QY0", 288), ("QX", 128), ("QY2", 128), ("WF1", 896), ("WF2", 448), ("WB", 832), ("QO", 288),
-                 ("P1", 448), ("P2", 448), ("P3", 448), ("P4", 448), ("S2", 256), ("S3", 256), ("S4", 256)]:
+                 ("P1", 416), ("P2", 416), ("P3", 416), ("P4", 416), ("S2", 256), ("S3", 256), ("S4", 256),
+                 ("H1", 96), ("H2", 64), ("H3", 64), ("H4", 64)]:
         s[n + "c"] = ("sbuf", [128, w], X4)
         s[n + "s"] = ("sbuf", [128, w], SC)
-    for n, w in [("H1", 96), ("H2", 64), ("H3", 64), ("H4", 64)]:
-        s[n + "c"] = ("sbuf", [128, w], X4)
-        s[n + "s"] = ("sbuf", [128, 4 * w], SC)
-    for arena, d, names in (("AU", U, PACK_U), ("AF", F, PACK_F)):
+    for n in TEMPS:
+        for c in "bcd": s[n + c] = s[n]
+    for c in "0123": s["FL" + c] = ("sbuf", [128, 224], F)
+    more = lambda first: [n + c for n in TEMPS if n[0] in first for c in ("", "b", "c", "d") if n + c not in PACK_F]
+    for arena, d, names in (("AU", U, PACK_U), ("AF", F, PACK_F + more("tL") + ["FL" + c for c in "0123"]), ("AI", I, more("i"))):
         at = 0
         for n in names:
             PLACE[n] = (arena, at, s[n][1][1])
@@ -89,26 +94,30 @@ def helper_program(g, core, T, topo, r, h):
     peer = [T.cores[(r + 1 + u) % N] for u in range(N - 1)]
     eng = topo.engines(core, peer[0])
     half = len(eng) // 2
+    pair = lambda i: [u for u in (2 * i, 2 * i + 1) if u < N - 1]
     sent = 0
     for k in ORDER:
         if k in SMALL:
             _s, hb, land, w = SMALL[k]
-            g.wait_ge(T.sem["h" + k], 2)
-            o = w * (N - 2 - h)
-            g.remote_dma_fused([_to(topo, core, peer[h], _bits(eng), T.sem["x" + k], T[hb][:, 0:w], T[land][:, o:o + w])], local_sem=T.sem.ls)
+            if k != "p" and h < 3: continue
+            us = [h] if k == "p" else pair((h - 4) % 4)
+            n = len(eng) // len(us)
+            g.wait_ge(T.sem["h" + k], 2 if k == "p" else 4)
+            g.remote_dma_fused([_to(topo, core, peer[u], _bits(eng[n * j:n * j + n]), T.sem["x" + k], T[hb][:, w * j:w * j + w],
+                                    T[land][:, w * (N - 2 - u):w * (N - 1 - u)]) for j, u in enumerate(us)], local_sem=T.sem.ls)
             sent += len(eng)
             continue
         _s, land, w, _o = BIG[k]
         jobs = []
-        if h <= 3: jobs.append(("c", [u for u in (2 * h, 2 * h + 1) if u < N - 1]))
-        if h >= 3: jobs.append(("s", [N - 2] if h == 3 else [2 * (h - 4), 2 * (h - 4) + 1]))
+        if h <= 3: jobs.append(("c", pair(h)))
+        if h >= 3: jobs.append(("s", pair((h - 4) % 4)))
         at = 0
         for kind, us in jobs:
-            g.wait_ge(T.sem["h%s%d" % (kind, k)], 2)
+            g.wait_ge(T.sem["h%s%d" % (kind, k)], 4)
             ts = []
             for u in us:
                 o = _land(k, r, u)
-                a = 0 if k == 1 else (w * (u % 2) if kind == "c" else w * u)
+                a = 0 if k == 1 else w * (u % 2)
                 src, dst = T["H%d%s" % (k, kind)][:, a:a + w], T[land + kind][:, o:o + w]
                 if kind == "c": src, dst = src.bitcast(dt.uint8), dst.bitcast(dt.uint8)
                 ts.append(_to(topo, core, peer[u], _bits(eng[half * at:half * at + half]), T.sem["x%d" % k], src, dst))
@@ -131,8 +140,10 @@ def rank_program(g, core, T, topo):
     known = {e: {} for e in queue}
     log = {}
     final = {}
+    use, folds, nodes = [""], [0], []
 
     def V(name, a=0, b=None, step=1):
+        if name in TEMPS: name += use[0]
         if name in PLACE:
             name, at, w = PLACE[name]
             a, b = at + a, at + (w if b is None else b)
@@ -176,28 +187,74 @@ def rank_program(g, core, T, topo):
         for x in ws: log.setdefault(x[0], []).append((x, True, tok))
         final[tok[0]] = max(final.get(tok[0], 0), tok[1])
 
-    def op(e, call, writes, reads, acc=False):
-        rs, ws = order(e, reads, writes, acc)
-        count[e] += 1
-        call().then_inc(T.sem["c" + e], 1)
-        note(rs, ws, ("c" + e, count[e], dict(known[e])))
+    def later(e, emit, writes, reads, cost, lat):
+        rs = [x for v in reads if isinstance(v, tuple) for x in v[1]]
+        nodes.append((e, emit, rs, [x for v in writes for x in v[1]] + [x for x in rs if x[0] in ("PA", "PB")], cost, lat))
+
+    def op(e, call, writes, reads, acc=False, rate=1.0):
+        def emit():
+            rs, ws = order(e, reads, writes, acc)
+            count[e] += 1
+            call().then_inc(T.sem["c" + e], 1)
+            note(rs, ws, ("c" + e, count[e], dict(known[e])))
+        x = writes[0][1][0]
+        n = -(-(x[2] - x[1]) // x[3])
+        if x[0] in ("PA", "PB"): n = reads[2][1][0][2] - reads[2][1][0][1] + 16
+        if reads and isinstance(reads[0], tuple) and len(reads[0][1]) == 2: rate = 1.7
+        later(e, emit, writes, reads, max(64, n * rate) * 0.00105, HOP)
+
+    def schedule():
+        n = len(nodes)
+        pre, seen, last = [set() for _ in nodes], {}, {}
+        for i, (e, _e, rs, ws, _c, _l) in enumerate(nodes):
+            for x, w in [(x, False) for x in rs] + [(x, True) for x in ws]:
+                for y, yw, j in seen.get(x[0], []):
+                    if (w or yw) and meet(x, y): pre[i].add(j)
+            key = "g" if e == "x" else e
+            if key in "gps" and key in last: pre[i].add(last[key])
+            if e in "gps": last[e] = i
+            for x in rs: seen.setdefault(x[0], []).append((x, False, i))
+            for x in ws: seen.setdefault(x[0], []).append((x, True, i))
+        way, post = [0.0] * n, [[] for _ in nodes]
+        for i in range(n - 1, -1, -1):
+            way[i] = nodes[i][4] + nodes[i][5] + max([way[j] for j in post[i]], default=0.0)
+            for j in pre[i]: post[j].append(i)
+        left, ready, free, cand = [len(p) for p in pre], [0.0] * n, {}, [i for i in range(n) if not pre[i]]
+        while cand:
+            i = min(cand, key=lambda j: (max(ready[j], free.get(nodes[j][0], 0.0)), -way[j]))
+            e = nodes[i][0]
+            t = max(ready[i], free.get(e, 0.0))
+            i = max([j for j in cand if nodes[j][0] == e and ready[j] <= t], key=lambda j: way[j])
+            soon = [j for j in cand if nodes[j][0] == e and way[j] > way[i] and ready[j] < t + nodes[i][4]]
+            if soon: i = max(soon, key=lambda j: way[j])
+            t = max(t, ready[i])
+            cand.remove(i)
+            nodes[i][1]()
+            if e != "x": free[e] = t + nodes[i][4]
+            for j in post[i]:
+                same = nodes[j][0] == e and e in "gps"
+                ready[j] = max(ready[j], t + nodes[i][4] + (0.0 if same else nodes[i][5]))
+                left[j] -= 1
+                if not left[j]: cand.append(j)
 
     def raw(v):
         return v[0] if isinstance(v, tuple) else v
 
-    def dma(e, out, in_):
-        rs, ws = order(e, [in_], [out])
-        s = "d%d" % count["d"]
-        count["d"] += 1
-        queue[e].dma_start(out[0], in_[0]).then_inc(T.sem[s], 16)
-        note(rs, ws, (s, 16, dict(known[e])))
+    def dma(e, out, in_, lat=2.0):
+        def emit():
+            rs, ws = order(e, [in_], [out])
+            s = "d%d" % count["d"]
+            count["d"] += 1
+            queue[e].dma_start(out[0], in_[0]).then_inc(T.sem[s], 16)
+            note(rs, ws, (s, 16, dict(known[e])))
+        later(e, emit, [out], [in_], 0.3, lat)
 
     def ext(ap):
         return (ap, [])
 
-    def memset(o, c): op("v", lambda: g.vector.memset(o[0], c), [o], [])
+    def memset(o, c): op("v", lambda: g.vector.memset(o[0], c), [o], [], rate=0.6)
     def copy(o, i): op("v", lambda: g.vector.tensor_copy(o[0], i[0]), [o], [i])
-    def tt(o, a, b, f): op("v", lambda: g.vector.tensor_tensor(o[0], a[0], b[0], f), [o], [a, b])
+    def tt(o, a, b, f): op("v", lambda: g.vector.tensor_tensor(o[0], a[0], b[0], f), [o], [a, b], rate=1.0 if b[1][0][0] == "PA" else 2.0)
     def tr(o, i): op("v", lambda: g.vector.transpose(o[0], i[0]), [o], [i])
 
     def ts(o, a, s1, f1, s2=None, f2=None):
@@ -214,16 +271,16 @@ def rank_program(g, core, T, topo):
         op("a", lambda: g.scalar.activation(o[0], i[0], f, **kw), [o], [i, bias, scale])
 
     def iota(o, pat, base, cm, fl=True):
-        if fl: op("g", lambda: g.iota(o[0], pat, base, cm, allow_small_or_imprecise_dtypes=True), [o], [])
+        if fl: op("g", lambda: g.iota(o[0], pat, base, cm, allow_small_or_imprecise_dtypes=True), [o], [], rate=2.2)
         else: op("g", lambda: g.iota(o[0], pat, base, cm), [o], [])
 
     def quant(q, a, n, tile):
         c, s = V(q + "c", a, a + n), V(q + "s", a, a + n)
-        op("v", lambda: g.vector.quantize_mx(c[0], s[0], tile[0]), [c, s], [tile])
+        op("v", lambda: g.vector.quantize_mx(c[0], s[0], tile[0]), [c, s], [tile], rate=1.1)
 
     def mm(out, w, wa, x, xa, n, start=True, stop=True):
         wc, ws, xc, xs = V(w + "c", wa, wa + 128), V(w + "s", wa, wa + 128), V(x + "c", xa, xa + n), V(x + "s", xa, xa + n)
-        op("p", lambda: g.tensor.matmul_mx(out[0], wc[0], ws[0], xc[0], xs[0], start, stop), [out], [wc, ws, xc, xs], acc=not start)
+        op("p", lambda: g.tensor.matmul_mx(out[0], wc[0], ws[0], xc[0], xs[0], start, stop), [out], [wc, ws, xc, xs], acc=not start, rate=0.6)
 
     def pick(q, a, win, wn, off, n):
         copy(words(V(q + "c", a, a + n)), ind(words(V(win + "c", 0, wn)), off))
@@ -232,52 +289,47 @@ def rank_program(g, core, T, topo):
     def col(i): return V("CC", i, i + 1)
 
     def fold(o, table, n):
-        tt(V("L1", 0, n), table, V("DIAG", 0, n), A.mult)
-        scan(o, V("RESET", 0, n), V("L1", 0, n), 0.0, A.mult, A.add)
+        folds[0] += 1
+        tmp = V("FL%d" % (folds[0] % 4), 0, n)
+        tt(tmp, table, V("DIAG", 0, n), A.mult)
+        scan(o, V("RESET", 0, n), tmp, 0.0, A.mult, A.add)
 
     peer = [T.cores[(r + 1 + u) % N] for u in range(N - 1)]
     help_ = _helpers(topo, core)
     out_engines = len(topo.engines(core, peer[0]))
 
-    def fused(ts_, srcs):
-        order("g", srcs, [])
-        g.remote_dma_fused(ts_, local_sem=T.sem.ls)
-        count["ls"] += 2 * len(ts_)
+    def hand(to, e, sem, src, dst, reads):
+        def emit():
+            order("g", [reads], [])
+            g.remote_dma_fused([_to(topo, core, help_[h], _bits(topo.engines(core, help_[h])[e * i:e * i + e]), T.sem[sem], src(i), dst)
+                                for i, h in enumerate(to)], local_sem=T.sem.ls)
+            count["ls"] += e * len(to)
+        later("g", emit, [], [reads], 0.5, 0.0)
 
-    def arrives(views, sem):
-        note([], [x for v in views for x in v[1]], (sem, (N - 1) * out_engines, {}))
+    def arrives(views, k, n):
+        later("x", lambda: note([], [x for v in views for x in v[1]], ("x%s" % k, n * out_engines, {})), views, [], TRAVEL[k], 0.0)
 
     def send_small(k):
         src, hb, land, w = SMALL[k]
-        tsf = []
-        for u in range(N - 1):
-            a, e = (0 if k == "p" else w * u), topo.engines(core, help_[u])
-            tsf.append(_to(topo, core, help_[u], _bits(e[2 * u:2 * u + 2]), T.sem["h" + k], T[src][:, a:a + w], T[hb][:, 0:w]))
-        fused(tsf, [V(src)])
-        arrives([V(land, 0, w * (N - 1))], "x" + k)
+        if k == "p": hand(range(N - 1), 2, "hp", lambda i: T[src][:, 0:w], T[hb][:, 0:w], V(src))
+        else: hand([4, 5, 6, 3], 4, "h" + k, lambda i: T[src][:, 2 * w * i:2 * w * i + 2 * w], T[hb][:, 0:2 * w], V(src))
+        arrives([V(land, 0, w * (N - 1))], k, N - 1 if k == "p" else 4)
 
     def send_big(k):
         src, land, w, o0 = BIG[k]
-        tsf = []
-        hw = w if k == 1 else 2 * w
-        for i in range(8):
-            h = help_[i if i < 7 else 3]
-            e = topo.engines(core, h)
-            if i < 4:
-                a = 0 if k == 1 else hw * i
-                s, d = T[src + "c"][:, a:a + hw].bitcast(dt.uint8), T["H%dc" % k][:, 0:hw].bitcast(dt.uint8)
-            else:
-                s, d = T[src + "s"][:, 0:4 * hw], T["H%ds" % k][:, 0:4 * hw]
-            tsf.append(_to(topo, core, h, _bits(e[2 * i:2 * i + 2]), T.sem["h%s%d" % ("c" if i < 4 else "s", k)], s, d))
-        fused(tsf, [V(src + "c"), V(src + "s")])
+        hw, step = (w, 0) if k == 1 else (2 * w, 2 * w)
+        hand([0, 1, 2, 3], 4, "hc%d" % k, lambda i: T[src + "c"][:, step * i:step * i + hw].bitcast(dt.uint8),
+             T["H%dc" % k][:, 0:hw].bitcast(dt.uint8), V(src + "c", 0, 3 * step + hw))
+        hand([4, 5, 6, 3], 4, "hs%d" % k, lambda i: T[src + "s"][:, step * i:step * i + hw], T["H%ds" % k][:, 0:hw], V(src + "s", 0, 3 * step + hw))
         if k == 1:
             views = [V(land + c, M * s, M * s + M) for c in "cs" for s in range(N) if s != r]
         else:
             views = [V(land + c, o0, o0 + K) for c in "cs"]
-        arrives(views, "x%d" % k)
+        arrives(views, k, N - 1)
 
     def scatter(win, off, val):
-        op("v", lambda: g.vector.tensor_copy(win[0].indirect(off[0]), val[0]), [win], [off, val])
+        op("v", lambda: g.vector.tensor_copy(win[0].indirect(off[0]), val[0]), [win], [off, val],
+           rate=3.5 * (val[1][0][2] - val[1][0][1]) / (win[1][0][2] - win[1][0][1]))
 
     def fill(name, a, b, c):
         act(V(name, a, b), V("IOTA", 0, b - a), ACT.Identity, bias=float(c), scale=0.0)
@@ -285,34 +337,47 @@ def rank_program(g, core, T, topo):
     def lin(o, i, scale, bias):
         act(o, i, ACT.Identity, bias=bias, scale=scale)
 
+    def unit(q):
+        for b in range(4):
+            quant(q, 128 * b, 128, V("ET", 3 - b, 515 - b))
+
     u8 = lambda v: (v[0].bitcast(dt.uint8), v[1])
     lvb, lv1 = V("LVB"), (T.LV1[0:1, :], V("LV1")[1])
     dma("a", lv1, ext(T.lv[:]))
-    dma("s", V("TXN"), ext(T.x[:]))
-    dma("a", V("PR", 0, 18), ext(T.pr0[:]))
-    dma("a", V("PR", 18, 36), ext(T.pr1[:]))
+    dma("s", V("TXN"), ext(T.x[:]), 2.8)
+    dma("a", V("PR", 0, 18), ext(T.pr0[:]), 4.0)
+    dma("a", V("PR", 18, 36), ext(T.pr1[:]), 4.0)
     dma("s", V("QWs"), ext(T.ws[:]))
-    dma("s", u8(V("QWc")), ext(T.wc[:]))
+    dma("s", u8(V("QWc")), ext(T.wc[:]), 3.5)
     dma("s", V("QVs"), ext(T.vs[:]))
     dma("s", u8(V("QVc")), ext(T.vc[:]))
-    dma("s", V("TU"), ext(T.u[:]))
+    dma("s", V("TU"), ext(T.u[:]), 12.0)
 
     iota(V("PI", 0, 1), [[1, 1]], 0, 1, fl=False)
     iota(V("IOTA", 0, 577), [[1, 577]], 0, 0)
-    op("g", lambda: g.partition_broadcast(lvb[0], lv1[0], 128), [lvb], [lv1])
+    op("g", lambda: g.partition_broadcast(lvb[0], lv1[0], 128), [lvb], [lv1], rate=4.3)
     iota(V("J16"), [[0, 14], [1, 16]], 0, 0)
     iota(V("KEYC"), [[1, 8], [0, 16]], ROUND, 0)
     iota(V("CJ"), [[-C, N - 1], [0, 2]], C * (N - 2) - 1, 0)
     memset(V("ET"), 0.0)
+    memset(V("TX"), 0.0)
+    memset(V("ST"), 0.0)
     ts(V("PI", 1, 2), V("PI", 0, 1), 15, A.bitwise_and)
     ts(V("PI", 2, 3), V("PI", 0, 1), 4, A.logical_shift_right, 1, A.bitwise_and)
+    quant("WF1", N * M, 128, V("TX"))
     copy(V("CC", 0, 3), V("PI", 0, 3))
-    for b in range(4):
-        ts(V("ET", 512 * b + b, 512 * b + 512, 4), V("IOTA", 0, 128), col(0), A.is_equal)
     ts(col(4), col(1), 18.0, A.mult, col(2), A.add)
-    quant("QE", 0, 512, V("ET"))
+    ts(col(9), col(1), float(2 * M), A.add)
+    ts(V("ET", 3, 515, 4), V("IOTA", 0, 128), col(0), A.is_equal)
     for h in range(2):
         ts(V("PERM", h, 18, 2), V("IOTA", 0, 18, 2), col(4), A.add)
+    unit("QE")
+    for h in range(2):
+        ts(V("ST", h, 4, 2), V("IOTA", 0, 32, 16), col(1), A.add)
+        for k in range(2):
+            ts(V("ST", 48 + 12 * k + h, 60 + 12 * k, 2), V("IOTA", 0, M, 16), col(9 if k else 1), A.add)
+    ts(V("ST", 16, 24), V("IOTA", 0, 8), 0.0, A.mult, col(1), A.add)
+    copy(V("ST", 32, 40), V("IOTA", 0, 8))
     lin(col(3), col(1), float(M), 0.0)
     lin(V("CC", 5, 7), V("CC", 0, 2), -1.0, 0.0)
     lin(V("IOTA", 577, 1154), V("IOTA", 0, 577), 1.0, 577.0)
@@ -347,7 +412,7 @@ def rank_program(g, core, T, topo):
         mm(bank("PB", b, C), "QW", 128 * b, "QX0", 0, C)
     for b in range(4):
         act(V("TY0", b, 4 * C, 4), bank("PB", b, C), scale=0.03125)
-    dma("s", V("PPU", 126, 144), V("POSS"))
+    dma("s", V("PPU", 126, 144), V("POSS"), 5.0)
     scatter(V("INVF"), V("POSU"), V("IOTA", 0, C))
     fold(V("SCI", 0, M), V("INVF", 0, M), M)
     copy(V("INV0"), V("SCI", 15, M, 16))
@@ -360,6 +425,7 @@ def rank_program(g, core, T, topo):
         fold(V("NW%d" % l), ind(V("PF"), V("PFO", 12 * (l - 1), 12 * l)), 2 * M)
 
     def lists(l):
+        use[0] = ""
         nw, off, tl = V("NW%d" % l, 15, 2 * M, 16), "OFF%d" % l, "TL%d" % l
         ts(V("t2", 0, 12), nw, float(N * C - 1), A.min, -143.5, A.add)
         ts(V("TW", 0, 12), V("t2", 0, 12), 1.0 / C, A.mult, float(ROUND), A.add)
@@ -379,12 +445,8 @@ def rank_program(g, core, T, topo):
         copy(V("OFU"), V(off, 0, 12))
         scatter(V(tl), V("OFU"), V("NV"))
         fold(V("L2", 0, K), V(tl, 0, K), K)
-        copy(V("WL%d" % l), V("L2", 15, K, 16))
+        copy(V("WL%d" % l, 0, 14), V("L2", 15, K, 16))
         send_small("l%d" % l)
-
-    def unit(c):
-        for b in range(4):
-            act(V("ET", 512 * b + b, 512 * b + 512, 4), V("ID"), scale=c)
 
     act(V("PF"), ind(V("IOTA"), V("CODE")))
     lin(V("CB"), V("IOTA", 0, 8), float(CAP), -1.0)
@@ -394,47 +456,46 @@ def rank_program(g, core, T, topo):
     for k in range(2):
         lin(V("E4096", M * k, M * k + M), V("IOTA", 128 * k, 128 * k + M), 4096.0, 0.0)
     fill("TL2", 0, K, EMPTY)
+    fill("WL2", 14, 16, 0)
     lin(col(8), col(2), 0.5, 0.0)
     lin(col(7), col(2), -0.5, 0.5)
     act(V("JT", 0, 128), V("IOTA", 0, 128), ACT.Abs, bias=col(5))
     act(V("ID"), V("JT", 0, 128), ACT.Relu, bias=1.0, scale=-1.0)
-    unit(col(7))
+    act(V("ET", 3, 515, 4), V("ID"), scale=col(7))
     fold(V("SCI", M, C), V("INVF", M, C), 2 * M)
-    ts(V("KOFF"), V("IOTA", 0, 8), 0.0, A.mult, col(1), A.add)
-    copy(V("SEGO"), V("IOTA", 0, 8))
+    copy(V("AU", 0, 176), V("ST"))
     for l in (2, 1):
         for k in range(2):
             a = 12 * (l - 1) + 6 * k
             ts(V("PFO", a, a + 6), V("SCI", M * l + 15, M * l + M, 16), float(C * k), A.add)
     for t in range(4):
-        ts(V("OI", 18 * t, 18 * t + 18), V("SCI", 15, C, 16), 4.0, A.mult, float(t), A.add)
+        lin(V("OIF", 18 * t, 18 * t + 18), V("SCI", 15, C, 16), 4.0, float(t))
     codes(2)
-    fill("TX", 0, 512, 0)
-    for t in range(4):
-        act(V("DS", 192 * t, 192 * t + 192), ind(V("X0"), V("OI", 18 * t + 6, 18 * t + 18)))
-    for t in range(4):
-        act(V("TYS", t, 4 * M, 4), ind(V("TY0"), V("OI", 18 * t, 18 * t + 6)))
     lists(2)
-    quant("QH0", 0, 512, V("ET"))
-    unit(col(8))
+    copy(V("OI"), V("OIF"))
+    unit("QH0")
+    act(V("ET", 3, 515, 4), V("ID"), scale=col(8))
     act(V("POSF", 1, C + 1), ind(V("IOTA", 0, C), V("POSU")))
     fill("PP", 144, 148, N * M)
     fill("POSF", 0, 1, 2 * M)
     fill("POSF", C + 1, C + 2, 2 * M)
+    for t in range(2):
+        act(V("DS", 192 * t, 192 * t + 192), ind(V("X0"), V("OI", 18 * t + 6, 18 * t + 18)))
     codes(1)
+    use[0] = "b"
     for h in range(2):
         copy(V("i1", h, 24, 2), V("NW1", 15, 2 * M, 16))
-    memset(V("OF1"), 0)
     ts(V("i2", 0, 24), V("i1", 0, 24), 15, A.bitwise_and)
     ts(V("i3", 0, 24), V("i1", 0, 24), 4, A.logical_shift_right)
     copy(V("LO2"), V("i2", 0, 24))
     copy(V("HI2"), V("i3", 0, 24))
     act(V("MKL"), ind(V("DIAG", 0, 16), V("LO2")))
-    quant("QH1", 0, 512, V("ET"))
-    quant("WF1", N * M, 128, V("TX"))
+    unit("QH1")
     pick("WF1", M * r, "QY0", C, V("INV0"), M)
-    fill("TYS", 8 * M, 896, 0)
-    fill("SG", 4 * K, 1024, 0)
+    for t in range(2, 4):
+        act(V("DS", 192 * t, 192 * t + 192), ind(V("X0"), V("OI", 18 * t + 6, 18 * t + 18)))
+    for t in range(4):
+        act(V("TYS", t, 4 * M, 4), ind(V("TY0"), V("OI", 18 * t, 18 * t + 6)))
     copy(V("PP", 0, 144), V("PPU"))
     tt(V("L2"), ind(V("PP"), V("HI2")), V("MKL"), A.mult)
     tr(V("L3"), V("L2"))
@@ -444,20 +505,22 @@ def rank_program(g, core, T, topo):
         copy(V("OF1", 16 * h, 16 * h + 12), V("L1", 16 * h + 15, 384, 32))
 
     def gather_sum(p, win, wn, of, second, d, between=None):
-        for h in range(2):
-            pick(p, K * h, win, wn, V(of, second * h, second * h + 14), K)
-        for h in range(2):
-            for b in range(4):
-                for k in range(2):
-                    mm(bank("PA", b, 128), "QH%d" % h, 128 * b, p, K * h + M * k, 128, start=(h, k) == (0, 0), stop=(h, k) == (1, 1))
+        pick(p, 0, win, wn, V(of, 0, 12), 2 * M)
+        pick(p, 2 * M, win, wn, V(of, second, second + 14), K)
+        for b in range(4):
+            mm(bank("PA", b, 128), "QH0", 128 * b, p, 0, 128, start=True, stop=False)
+        for b in range(4):
+            for i in range(1, 4):
+                mm(bank("PA", b, 128), "QH%d" % (i // 2), 128 * b, p, M * i, 128, start=False, stop=i == 3)
         if between: between()
         for b in range(4):
             tt(V("TX", b, 4 * M, 4), d(b), bank("PA", b, M), A.subtract)
 
-    def layer(w, tile, a):
+    def layer(w, tile, a, between=None):
         quant("QX", 0, 128, V("TX"))
         for b in range(4):
             mm(bank("PB", b, 128), w, 128 * b, "QX", 0, 128)
+        if between: between()
         for b in range(4):
             o = V(tile, a + b, a + 4 * M, 4)
             if b % 2: ts(o, bank("PB", b, M), 0.03125, A.mult)
@@ -472,6 +535,7 @@ def rank_program(g, core, T, topo):
         send_big(k)
 
     def arrived(l):
+        use[0] = "c"
         copy(V("i1", 0, 14), V("LL%d" % l))
         ts(V("i2", 0, 14), V("i1", 0, 14), 4095, A.bitwise_and)
         tt(V("t2", 0, 14), V("i2", 0, 14), V("CJ"), A.subtract)
@@ -479,45 +543,58 @@ def rank_program(g, core, T, topo):
         fold(V("L2", 0, K), ind(V("POSF", 0, C + 2), V("JU")), K)
 
     def keep(l):
+        use[0] = "c"
         copy(V("PC%d" % l, 0, 14), V("L2", 15, K, 16))
         ts(V("KC%d" % l, 0, 14), V("LL%d" % l), 4096.0 * 128, A.is_ge, float(2 * M), A.mult)
 
     def own(l):
+        use[0] = "b"
         ts(V("JO"), V("NW%d" % l, 15, 2 * M, 16), -float(C * (N - 1) - 1), A.add)
         fold(V("L2", 0, 2 * M), ind(V("POSF", 0, C + 2), V("JO")), 2 * M)
         copy(V("PC%d" % l, 14, 26), V("L2", 15, 2 * M, 16))
 
     def back_send(l, out):
-        copy(V("i1", 0, 14), V("WL%d" % l))
+        use[0] = "d"
+        copy(V("i1", 0, 14), V("WL%d" % l, 0, 14))
         ts(V("i2", 0, 14), V("i1", 0, 14), 12, A.logical_shift_right, 127, A.bitwise_and)
         for t in range(4):
             ts(V(out, 14 * t, 14 * t + 14), V("i2", 0, 14), 4.0, A.mult, float(t), A.add)
 
-    def successors(l, of):
+    def successors(l):
+        use[0] = "d"
         pc, kc = V("PC%d" % l), V("KC%d" % l)
         ts(V("t2", 0, 26), pc, float(2 * M), A.is_ge)
         tt(V("t3", 0, 26), pc, kc, A.add)
         tt(V("t4", 0, 26), V("t2", 0, 26), V("IDXC"), A.mult)
-        memset(V(of), 0)
         tt(V("t1", 0, 26), V("t3", 0, 26), V("t4", 0, 26), A.add)
         copy(V("SUO"), V("t1", 0, 26))
         scatter(V("SU"), V("SUO"), V("VAL%d" % l))
         act(V("SD"), ind(V("SU", M * (l - 1), 4 * M), V("DBL")))
 
     def successors_end(of):
+        use[0] = "d"
         tr(V("L3"), V("SD"))
         for h in range(2):
             copy(V(of, 16 * h, 16 * h + 12), V("L3", 16 * h, 384, 32))
 
+    def places():
+        use[0] = "c"
+        ts(V("t1", 0, 18), V("POSW"), M + 0.5, A.is_ge, -float(K), A.mult)
+        ts(V("t2", 0, 18), V("POSW"), 2 * M + 0.5, A.is_ge, -float(2 * K), A.mult)
+        tt(V("t3", 0, 18), V("t1", 0, 18), V("POSW"), A.add)
+        tt(V("t4", 0, 18), V("t3", 0, 18), V("t2", 0, 18), A.add)
+        ts(V("POSZ"), V("t4", 0, 18), float(2 * K + 255), A.add)
+
     def asked():
+        fill("TYS", 8 * M, 896, 0)
+        fill("SG", 4 * K, 1024, 0)
         arrived(2)
         for t in range(4):
             ts(V("G2", 14 * t, 14 * t + 14), V("L2", 15, K, 16), 4.0, A.mult, float(t), A.add)
 
     gather_sum("P1", "WF1", 896, "OF1", 16, lambda b: V("DS", 192 * b, 192 * b + M), asked)
-    layer("QW", "TYS", 4 * M)
+    layer("QW", "TYS", 4 * M, lambda: keep(2))
     compose(2, "TYS", "G2")
-    keep(2)
     fill("W32", 0, 32, 0)
     lin(V("IDXC"), V("IOTA", 0, 416, 16), 1.0, col(1))
     lin(V("IDXC", 14, 20), V("IDXC", 14, 20), 1.0, float(2 * M))
@@ -535,27 +612,21 @@ def rank_program(g, core, T, topo):
     for n in ("TY2", "TZ2", "TZ1", "TZ0"):
         fill(n, 4 * M, 512, 0)
     fill("TL1", 0, K, EMPTY)
+    fill("WL1", 14, 16, 0)
     lin(V("VAL1"), V("VAL2"), 1.0, float(K + 128))
-    for h in range(2):
-        ts(V("DUPO", h, 4, 2), V("IOTA", 0, 32, 16), col(1), A.add)
     own(2)
     ts(V("t1", 0, 12), V("OFF2", 0, 12), float(K), A.is_ge, 1000.0, A.mult)
     ts(V("t2", 0, 12), V("PC2", 14, 26), float(K), A.add)
     tt(V("t3", 0, 12), V("t1", 0, 12), V("OFF2", 0, 12), A.add)
-    for k in range(2):
-        ts(V("DBL", 12 * k, 12 * k + 12, 2), V("IOTA", 0, M, 16), col(1), A.add, float(2 * M * k), A.add)
     tt(V("W32", 0, 12), V("t3", 0, 12), V("t2", 0, 12), A.min)
-    for k in range(2):
-        ts(V("DBL", 12 * k + 1, 12 * k + 12, 2), V("IOTA", 0, M, 16), col(1), A.add, float(2 * M * k), A.add)
     tr(V("D1"), V("W32"))
     copy(V("D2"), ind(V("D1"), V("DUPO")))
     tr(V("D3"), V("D2"))
     copy(V("OF2"), V("D3"))
-    successors(2, "OF3")
-    own(1)
+    successors(2)
 
-    gather_sum("P2", "WF2", 448, "OF2", 32, lambda b: V("DS", 192 * b + M, 192 * b + 2 * M), lambda: back_send(2, "G3"))
-    layer("QW", "TY2", 0)
+    gather_sum("P2", "WF2", 448, "OF2", 32, lambda b: V("DS", 192 * b + M, 192 * b + 2 * M), lambda: (back_send(2, "G3"), successors_end("OF3")))
+    layer("QW", "TY2", 0, lambda: quant("QU", 0, 128, V("TU")))
     quant("QY2", 0, 128, V("TY2"))
     for b in range(4):
         mm(bank("PA", b, 128), "QE", 128 * b, "QY2", 0, 128)
@@ -566,36 +637,27 @@ def rank_program(g, core, T, topo):
     compose(3, "TZ2", "G3")
     lists(1)
     quant("WB", K, 128, V("TZ2"))
-    successors_end("OF3")
 
-    gather_sum("P3", "WB", K + 128, "OF3", 16, lambda b: V("DY", 192 * b + M, 192 * b + 2 * M), lambda: back_send(1, "G4"))
+    gather_sum("P3", "WB", K + 128, "OF3", 16, lambda b: V("DY", 192 * b + M, 192 * b + 2 * M), lambda: (back_send(1, "G4"), own(1)))
     layer("QV", "TZ1", 0)
     compose(4, "TZ1", "G4")
     arrived(1)
     keep(1)
-    successors(1, "OF4")
+    successors(1)
     quant("WB", 2 * K + 128, 128, V("TZ1"))
-    quant("QU", 0, 128, V("TU"))
     successors_end("OF4")
-
-    def places():
-        ts(V("t1", 0, 18), V("POSW"), M + 0.5, A.is_ge, -float(K), A.mult)
-        ts(V("t2", 0, 18), V("POSW"), 2 * M + 0.5, A.is_ge, -float(2 * K), A.mult)
-        tt(V("t3", 0, 18), V("t1", 0, 18), V("POSW"), A.add)
-        tt(V("t4", 0, 18), V("t3", 0, 18), V("t2", 0, 18), A.add)
-        ts(V("POSZ"), V("t4", 0, 18), float(2 * K + 255), A.add)
 
     gather_sum("P4", "WB", 2 * K + 256, "OF4", 16, lambda b: V("DY", 192 * b, 192 * b + M), places)
     layer("QV", "TZ0", 0)
     quant("WB", 2 * K + 256, 128, V("TZ0"))
     pick("QO", 0, "WB", 832, V("POSZ"), C)
     mm(bank("PA", 0, C), "QU", 0, "QO", 0, C)
-    scales = lambda k: dma("a" if k else "s", ext(T.osc[4 * k:4 * k + 4, :]), (T.QOs[32 * k:32 * k + 4, :], V("QOs")[1]))
     dma("s", ext(T.oc[:]), u8(V("QOc")))
     for k in range(4):
-        scales(k)
+        dma("a" if k else "s", ext(T.osc[4 * k:4 * k + 4, :]), (T.QOs[32 * k:32 * k + 4, :], V("QOs")[1]))
     copy(V("YO"), bank("PA", 0, C))
     dma("s", ext(T.y[:]), V("YO"))
+    schedule()
     g.wait_ge(T.sem.ls, count["ls"])
     for s in sorted(final):
         wait("g", (s, final[s], {}))

@@ -7,12 +7,13 @@ F, B, I, U, X4, SC = "float32", "bfloat16", "int32", "uint16", "float8_e4m3fn_x4
 ROUND = 12582912
 EMPTY = 4095 + 4096 * (128 + M)
 
-PACK_U = "DUPO KOFF SEGO DBL OF1 OF3 OF4 PERM CODE POSU POSZ INV0 OI PFO OFU HI2 LO2 JU JO SUO OF2 G2 G3 G4".split()
-PACK_F = "t1 t2 t3 t4 TA TB TC TT TW D1 D2 D3 W32 OFF1 OFF2 PC1 PC2 KC1 KC2 CB CJ IDXC POSW OIF".split()
+PACK_U = "DUPO KOFF SEGO DBL OF1 OF3 OF4 CODE POSU POSZ INV0 OI PFO OFU HI2 LO2 JU JO SUO OF2 G2 G3 G4".split()
+PACK_F = "t1 t2 t3 t4 TA TB TC TT TW D1 D2 D3 W32 OFF1 OFF2 PC1 PC2 KC1 KC2 CB CJ IDXC POSW OIF MK CS NM CT CU CV CW".split()
 PLACE = {}
 TEMPS = "t1 t2 t3 t4 i1 i2 i3 L1 L2 L3".split()
-TRAVEL = {"p": 11.0, 1: 6.5, "l2": 4.0, 2: 4.5, 3: 4.5, "l1": 4.0, 4: 4.5}
+TRAVEL = {"p": 8.0, 1: 6.5, "l2": 4.0, 2: 4.5, 3: 4.5, "l1": 4.0, 4: 4.5}
 HOP = 0.12
+SLACK = 0.6
 
 
 def _scratch():
@@ -20,10 +21,11 @@ def _scratch():
     for n, w, d in [
         ("IOTA", 2308, F), ("PI", 4, I), ("CC", 16, F), ("J16", 224, F), ("JT", 224, F), ("DIAG", 224, B), ("RESET", 224, B),
         ("KEYC", 128, F), ("CJ", 14, F), ("CB", 8, F), ("IDXC", 26, F), ("E4096", 192, F), ("VAL2", 416, F), ("VAL1", 416, F),
-        ("PERM", 18, U), ("DUPO", 4, U), ("KOFF", 8, U), ("SEGO", 8, U), ("ID", 128, B), ("ST", 176, F), ("OIF", 72, F),
-        ("ET", 520, B), ("LV1", 288, I), ("LVB", 288, I), ("PR", 36, I), ("CODE", 36, U), ("PF", 576, F),
+        ("DUPO", 4, U), ("KOFF", 8, U), ("SEGO", 8, U), ("ST", 176, F), ("OIF", 72, F),
+        ("ET", 520, B), ("LVT", 18, I), ("PR", 36, I), ("CODE", 36, U), ("PF", 576, F),
         ("t1", 36, F), ("t2", 36, F), ("t3", 36, F), ("t4", 36, F), ("i1", 32, I), ("i2", 32, I), ("i3", 32, I),
-        ("MK", 288, B), ("MKP", 288, B), ("L1", 384, F), ("L2", 384, F), ("L3", 384, F), ("MKL", 384, B), ("SD", 384, F),
+        ("MK", 96, F), ("CS", 96, F), ("NM", 96, F), ("CT", 96, F), ("CU", 96, F), ("CV", 96, F), ("CW", 96, F),
+        ("L1", 384, F), ("L2", 384, F), ("L3", 384, F), ("MKL", 384, B), ("SD", 384, F),
         ("POSW", 18, F), ("POSU", 18, U), ("POSS", 18, U), ("POSZ", 18, U), ("POSF", 292, F), ("PP", 148, F), ("PPU", 144, U),
         ("INVF", 288, F), ("SCI", 288, F), ("INV0", 6, U), ("OI", 72, U), ("PFO", 24, U),
         ("NW1", 192, F), ("NW2", 192, F), ("NV", 192, F), ("TW", 16, F), ("TT", 32, F), ("TA", 32, F), ("TB", 32, F), ("TC", 32, F),
@@ -59,7 +61,7 @@ def _scratch():
 
 
 SCRATCH = _scratch()
-SEMAPHORES = (["cv", "ca", "cp", "cg", "ls"] + ["d%d" % i for i in range(18)] + ["xp", "xl1", "xl2", "x1", "x2", "x3", "x4"]
+SEMAPHORES = (["cv", "ca", "cp", "cg", "ls", "dl"] + ["d%d" % i for i in range(18)] + ["xp", "xl1", "xl2", "x1", "x2", "x3", "x4"]
               + ["hp", "hl1", "hl2"] + ["hc%d" % i for i in (1, 2, 3, 4)] + ["hs%d" % i for i in (1, 2, 3, 4)])
 BIG = {1: ("QS", "WF1", M, 0), 2: ("S2", "WF2", CAP, 0), 3: ("S3", "WB", CAP, 0), 4: ("S4", "WB", CAP, K + 128)}
 SMALL = {"p": ("POSS", "HP", "PPU", 18), "l2": ("WL2", "HL2", "LL2", 2), "l1": ("WL1", "HL1", "LL1", 2)}
@@ -135,6 +137,7 @@ def rank_program(g, core, T, topo):
                 helper_program(g, core, T, topo, i, _helpers(topo, rc).index(core))
         return
     A, ACT = AluOpType, ActivationFunctionType
+    MUL, ADD = A.mult, A.add
     queue = {"v": g.vector, "a": g.scalar, "p": g.tensor, "g": g, "s": g.sync}
     count = {"v": 0, "a": 0, "p": 0, "g": 0, "ls": 0, "d": 0}
     known = {e: {} for e in queue}
@@ -192,10 +195,10 @@ def rank_program(g, core, T, topo):
         nodes.append((e, emit, rs, [x for v in writes for x in v[1]] + [x for x in rs if x[0] in ("PA", "PB")], cost, lat))
 
     def op(e, call, writes, reads, acc=False, rate=1.0):
-        def emit():
+        def emit(e):
             rs, ws = order(e, reads, writes, acc)
             count[e] += 1
-            call().then_inc(T.sem["c" + e], 1)
+            (call[e] if isinstance(call, dict) else call)().then_inc(T.sem["c" + e], 1)
             note(rs, ws, ("c" + e, count[e], dict(known[e])))
         x = writes[0][1][0]
         n = -(-(x[2] - x[1]) // x[3])
@@ -221,15 +224,15 @@ def rank_program(g, core, T, topo):
             for j in pre[i]: post[j].append(i)
         left, ready, free, cand = [len(p) for p in pre], [0.0] * n, {}, [i for i in range(n) if not pre[i]]
         while cand:
-            i = min(cand, key=lambda j: (max(ready[j], free.get(nodes[j][0], 0.0)), -way[j]))
-            e = nodes[i][0]
+            i = min(cand, key=lambda j: (min(max(ready[j], free.get(q, 0.0)) for q in nodes[j][0]), -way[j]))
+            e = min(nodes[i][0], key=lambda q: max(ready[i], free.get(q, 0.0)))
             t = max(ready[i], free.get(e, 0.0))
-            i = max([j for j in cand if nodes[j][0] == e and ready[j] <= t], key=lambda j: way[j])
-            soon = [j for j in cand if nodes[j][0] == e and way[j] > way[i] and ready[j] < t + nodes[i][4]]
+            i = max([j for j in cand if e in nodes[j][0] and ready[j] <= t], key=lambda j: way[j])
+            soon = [j for j in cand if nodes[j][0] == e and way[j] > way[i] and ready[j] < t + SLACK * nodes[i][4]]
             if soon: i = max(soon, key=lambda j: way[j])
             t = max(t, ready[i])
             cand.remove(i)
-            nodes[i][1]()
+            nodes[i][1](e)
             if e != "x": free[e] = t + nodes[i][4]
             for j in post[i]:
                 same = nodes[j][0] == e and e in "gps"
@@ -241,7 +244,7 @@ def rank_program(g, core, T, topo):
         return v[0] if isinstance(v, tuple) else v
 
     def dma(e, out, in_, lat=2.0):
-        def emit():
+        def emit(_e):
             rs, ws = order(e, [in_], [out])
             s = "d%d" % count["d"]
             count["d"] += 1
@@ -253,18 +256,36 @@ def rank_program(g, core, T, topo):
         return (ap, [])
 
     def memset(o, c): op("v", lambda: g.vector.memset(o[0], c), [o], [], rate=0.6)
-    def copy(o, i): op("v", lambda: g.vector.tensor_copy(o[0], i[0]), [o], [i])
+    def real(v): return SCRATCH[v[1][0][0]][2] in (F, B, SC)
+
+    def either(o, i, scale=None, bias=None):
+        kw = {k: raw(x) for k, x in (("scale", scale), ("bias", bias)) if x is not None}
+        if scale is None and bias is None: v = lambda: g.vector.tensor_copy(o[0], i[0])
+        elif bias is None: v = lambda: g.vector.tensor_scalar(o[0], i[0], raw(scale), None, MUL)
+        elif scale is None: v = lambda: g.vector.tensor_scalar(o[0], i[0], raw(bias), None, ADD)
+        else: v = lambda: g.vector.tensor_scalar(o[0], i[0], raw(scale), raw(bias), MUL, ADD)
+        f = ACT.Copy if bias is None else ACT.Identity
+        op("av", {"a": lambda: g.scalar.activation(o[0], i[0], f, **kw), "v": v}, [o], [i, scale, bias])
+
+    def copy(o, i):
+        if real(o) and real(i): either(o, i)
+        else: op("v", lambda: g.vector.tensor_copy(o[0], i[0]), [o], [i])
+
     def tt(o, a, b, f): op("v", lambda: g.vector.tensor_tensor(o[0], a[0], b[0], f), [o], [a, b], rate=1.0 if b[1][0][0] == "PA" else 2.0)
     def tr(o, i): op("v", lambda: g.vector.transpose(o[0], i[0]), [o], [i])
 
     def ts(o, a, s1, f1, s2=None, f2=None):
-        if f2 is None: op("v", lambda: g.vector.tensor_scalar(o[0], a[0], raw(s1), None, f1), [o], [a, s1])
+        if real(o) and real(a) and f2 is None and f1 is MUL: either(o, a, scale=s1)
+        elif real(o) and real(a) and f2 is None and f1 is ADD: either(o, a, bias=s1)
+        elif real(o) and real(a) and f1 is MUL and f2 is ADD: either(o, a, s1, s2)
+        elif f2 is None: op("v", lambda: g.vector.tensor_scalar(o[0], a[0], raw(s1), None, f1), [o], [a, s1])
         else: op("v", lambda: g.vector.tensor_scalar(o[0], a[0], raw(s1), raw(s2), f1, f2), [o], [a, s1, s2])
 
     def scan(o, a, b, init, f0, f1):
         op("v", lambda: g.vector.tensor_tensor_scan(o[0], a[0], b[0], raw(init), f0, f1), [o], [a, b, init])
 
-    def act(o, i, f=ACT.Copy, bias=None, scale=None):
+    def act(o, i, f=None, bias=None, scale=None):
+        if f is None: return either(o, i, scale, bias)
         kw = {}
         if bias is not None: kw["bias"] = raw(bias)
         if scale is not None: kw["scale"] = raw(scale)
@@ -291,15 +312,15 @@ def rank_program(g, core, T, topo):
     def fold(o, table, n):
         folds[0] += 1
         tmp = V("FL%d" % (folds[0] % 4), 0, n)
-        tt(tmp, table, V("DIAG", 0, n), A.mult)
-        scan(o, V("RESET", 0, n), tmp, 0.0, A.mult, A.add)
+        tt(tmp, table, V("DIAG", 0, n), MUL)
+        scan(o, V("RESET", 0, n), tmp, 0.0, MUL, ADD)
 
     peer = [T.cores[(r + 1 + u) % N] for u in range(N - 1)]
     help_ = _helpers(topo, core)
     out_engines = len(topo.engines(core, peer[0]))
 
     def hand(to, e, sem, src, dst, reads):
-        def emit():
+        def emit(_e):
             order("g", [reads], [])
             g.remote_dma_fused([_to(topo, core, help_[h], _bits(topo.engines(core, help_[h])[e * i:e * i + e]), T.sem[sem], src(i), dst)
                                 for i, h in enumerate(to)], local_sem=T.sem.ls)
@@ -307,7 +328,7 @@ def rank_program(g, core, T, topo):
         later("g", emit, [], [reads], 0.5, 0.0)
 
     def arrives(views, k, n):
-        later("x", lambda: note([], [x for v in views for x in v[1]], ("x%s" % k, n * out_engines, {})), views, [], TRAVEL[k], 0.0)
+        later("x", lambda _e: note([], [x for v in views for x in v[1]], ("x%s" % k, n * out_engines, {})), views, [], TRAVEL[k], 0.0)
 
     def send_small(k):
         src, hb, land, w = SMALL[k]
@@ -332,21 +353,29 @@ def rank_program(g, core, T, topo):
            rate=3.5 * (val[1][0][2] - val[1][0][1]) / (win[1][0][2] - win[1][0][1]))
 
     def fill(name, a, b, c):
-        act(V(name, a, b), V("IOTA", 0, b - a), ACT.Identity, bias=float(c), scale=0.0)
+        either(V(name, a, b), V("IOTA", 0, b - a), 0.0, float(c))
 
     def lin(o, i, scale, bias):
-        act(o, i, ACT.Identity, bias=bias, scale=scale)
+        either(o, i, scale, bias)
 
     def unit(q):
         for b in range(4):
             quant(q, 128 * b, 128, V("ET", 3 - b, 515 - b))
 
     u8 = lambda v: (v[0].bitcast(dt.uint8), v[1])
-    lvb, lv1 = V("LVB"), (T.LV1[0:1, :], V("LV1")[1])
-    dma("a", lv1, ext(T.lv[:]))
+
+    def levels(e, h):
+        def emit(_e):
+            for k in range(4 * h, 4 * h + 4):
+                queue[e].dma_start(T.LVT[16 * k:16 * k + 16, :], T.lv[:]).then_inc(T.sem.dl, 16)
+            note([], V("LVT", 9 * h, 9 * h + 9)[1], ("dl", 128, {}))
+        later(e, emit, [V("LVT", 9 * h, 9 * h + 9)], [], 0.6, 1.8)
+
+    levels("a", 0)
     dma("s", V("TXN"), ext(T.x[:]), 2.8)
-    dma("a", V("PR", 0, 18), ext(T.pr0[:]), 4.0)
-    dma("a", V("PR", 18, 36), ext(T.pr1[:]), 4.0)
+    levels("s", 1)
+    dma("a", V("PR", 0, 18), ext(T.pr0[:]), 2.0)
+    dma("a", V("PR", 18, 36), ext(T.pr1[:]), 2.0)
     dma("s", V("QWs"), ext(T.ws[:]))
     dma("s", u8(V("QWc")), ext(T.wc[:]), 3.5)
     dma("s", V("QVs"), ext(T.vs[:]))
@@ -355,30 +384,28 @@ def rank_program(g, core, T, topo):
 
     iota(V("PI", 0, 1), [[1, 1]], 0, 1, fl=False)
     iota(V("IOTA", 0, 577), [[1, 577]], 0, 0)
-    op("g", lambda: g.partition_broadcast(lvb[0], lv1[0], 128), [lvb], [lv1], rate=4.3)
     iota(V("J16"), [[0, 14], [1, 16]], 0, 0)
     iota(V("KEYC"), [[1, 8], [0, 16]], ROUND, 0)
     iota(V("CJ"), [[-C, N - 1], [0, 2]], C * (N - 2) - 1, 0)
+    iota(V("IOTA", 1731, 2308), [[1, 577]], 1731, 0)
     memset(V("ET"), 0.0)
     memset(V("TX"), 0.0)
     memset(V("ST"), 0.0)
+    for n in ("MK", "CS"): memset(V(n), 0.0)
+    memset(V("CU", 0, 1), 0.0)
     ts(V("PI", 1, 2), V("PI", 0, 1), 15, A.bitwise_and)
     ts(V("PI", 2, 3), V("PI", 0, 1), 4, A.logical_shift_right, 1, A.bitwise_and)
     quant("WF1", N * M, 128, V("TX"))
     copy(V("CC", 0, 3), V("PI", 0, 3))
-    ts(col(4), col(1), 18.0, A.mult, col(2), A.add)
-    ts(col(9), col(1), float(2 * M), A.add)
+    ts(col(9), col(1), float(2 * M), ADD)
     ts(V("ET", 3, 515, 4), V("IOTA", 0, 128), col(0), A.is_equal)
-    for h in range(2):
-        ts(V("PERM", h, 18, 2), V("IOTA", 0, 18, 2), col(4), A.add)
     unit("QE")
     for h in range(2):
-        ts(V("ST", h, 4, 2), V("IOTA", 0, 32, 16), col(1), A.add)
+        ts(V("ST", h, 4, 2), V("IOTA", 0, 32, 16), col(1), ADD)
         for k in range(2):
-            ts(V("ST", 48 + 12 * k + h, 60 + 12 * k, 2), V("IOTA", 0, M, 16), col(9 if k else 1), A.add)
-    ts(V("ST", 16, 24), V("IOTA", 0, 8), 0.0, A.mult, col(1), A.add)
+            ts(V("ST", 48 + 12 * k + h, 60 + 12 * k, 2), V("IOTA", 0, M, 16), col(9 if k else 1), ADD)
+    ts(V("ST", 16, 24), V("IOTA", 0, 8), 0.0, MUL, col(1), ADD)
     copy(V("ST", 32, 40), V("IOTA", 0, 8))
-    lin(col(3), col(1), float(M), 0.0)
     lin(V("CC", 5, 7), V("CC", 0, 2), -1.0, 0.0)
     lin(V("IOTA", 577, 1154), V("IOTA", 0, 577), 1.0, 577.0)
     lin(V("IOTA", 1154, 1731), V("IOTA", 0, 577), 1.0, 1154.0)
@@ -386,25 +413,32 @@ def rank_program(g, core, T, topo):
     quant("QS", M, C, V("TXN"))
     for b in range(4):
         mm(bank("PA", b, C), "QE", 128 * b, "QS", M, C)
-    ts(V("MK"), V("LVB"), col(1), A.is_equal)
-    act(V("MKP"), ind(V("MK"), V("PERM")))
+    for l in range(3):
+        ts(V("MK", 32 * l, 32 * l + 18), V("LVT"), float(l), A.is_equal)
     for b in range(4):
         act(V("X0", b, 4 * C, 4), bank("PA", b, C))
     act(V("JT"), V("J16"), ACT.Abs, bias=col(6))
     act(V("DIAG"), V("JT"), ACT.Relu, bias=1.0, scale=-1.0)
     act(V("RESET"), V("J16"), ACT.Sign)
-    scan(V("L1", 0, C), V("MK"), V("MK"), col(3), A.add, A.max)
-    ts(V("t1"), V("PR"), -float(C * (r + 1)), A.add)
-    ts(V("t3"), V("PR"), 0.0, A.is_lt, float(C * (r + 1) + 1), A.mult)
-    tt(V("L3", 0, C), ind(V("L1", 0, C), V("PERM")), V("MKP"), A.mult)
-    ts(V("t2"), V("t1"), 0.0, A.is_lt, float(N * C), A.mult)
-    tr(V("L1", 0, C), V("L3", 0, C))
-    tt(V("t4"), V("t1"), V("t3"), A.add)
-    tt(V("TA", 0, 18), V("L1", 0, C, 16), V("L1", 1, C, 16), A.add)
-    tt(V("t1"), V("t4"), V("t2"), A.add)
-    tt(V("POSW"), V("TA", 0, 18), V("L1", 2, C, 16), A.add)
-    ts(V("POSS"), V("POSW"), float(M * r - 1), A.add)
-    ts(V("POSU"), V("POSW"), -1.0, A.add)
+    for l in range(3):
+        mk = V("MK", 32 * l, 32 * l + 18)
+        scan(V("CS", 32 * l, 32 * l + 18), mk, mk, 0.0, ADD, A.max)
+    tr(V("CT"), V("CS"))
+    scan(V("CU", 1, 96), V("CT", 0, 95), V("RESET", 1, 96), 0.0, ADD, MUL)
+    tr(V("CV"), V("CU"))
+    lin(V("NM"), V("MK"), 1000.0, -1000.0)
+    tt(V("CW", 0, 82), V("CS", 0, 82), V("NM", 0, 82), ADD)
+    for l in range(3):
+        ts(V("CT", 32 * l, 32 * l + 18), V("CW", 32 * l, 32 * l + 18), V("CV", 32 * l + 17, 32 * l + 18), ADD, float(M * l), ADD)
+    ts(V("t1"), V("PR"), -float(C * (r + 1)), ADD)
+    ts(V("t3"), V("PR"), 0.0, A.is_lt, float(C * (r + 1) + 1), MUL)
+    ts(V("t2"), V("t1"), 0.0, A.is_lt, float(N * C), MUL)
+    tt(V("t4"), V("t1"), V("t3"), ADD)
+    tt(V("TA", 0, 18), V("CT", 0, 18), V("CT", 32, 50), A.max)
+    tt(V("t1"), V("t4"), V("t2"), ADD)
+    tt(V("POSW"), V("TA", 0, 18), V("CT", 64, 82), A.max)
+    ts(V("POSS"), V("POSW"), float(M * r - 1), ADD)
+    ts(V("POSU"), V("POSW"), -1.0, ADD)
     quant("QX0", 0, C, V("X0"))
     send_small("p")
     copy(V("CODE"), V("t1"))
@@ -416,7 +450,6 @@ def rank_program(g, core, T, topo):
     scatter(V("INVF"), V("POSU"), V("IOTA", 0, C))
     fold(V("SCI", 0, M), V("INVF", 0, M), M)
     copy(V("INV0"), V("SCI", 15, M, 16))
-    lin(V("IOTA", 1731, 2308), V("IOTA", 0, 577), 1.0, 1731.0)
     quant("QY0", 0, C, V("TY0"))
     pick("QS", 0, "QY0", C, V("INV0"), M)
     send_big(1)
@@ -427,21 +460,21 @@ def rank_program(g, core, T, topo):
     def lists(l):
         use[0] = ""
         nw, off, tl = V("NW%d" % l, 15, 2 * M, 16), "OFF%d" % l, "TL%d" % l
-        ts(V("t2", 0, 12), nw, float(N * C - 1), A.min, -143.5, A.add)
-        ts(V("TW", 0, 12), V("t2", 0, 12), 1.0 / C, A.mult, float(ROUND), A.add)
+        ts(V("t2", 0, 12), nw, float(N * C - 1), A.min, -143.5, ADD)
+        ts(V("TW", 0, 12), V("t2", 0, 12), 1.0 / C, MUL, float(ROUND), ADD)
         tt(V("L2", 0, 128), ind(V("TW"), V("KOFF")), V("KEYC"), A.is_equal)
-        scan(V("L3", 0, 128), V("RESET", 0, 128), V("L2", 0, 128), 0.0, A.mult, A.add)
+        scan(V("L3", 0, 128), V("RESET", 0, 128), V("L2", 0, 128), 0.0, MUL, ADD)
         copy(V("TT", 0, 8), V("L3", 15, 128, 16))
         tr(V("TA"), V("TT"))
-        tt(V("NV"), ind(V("PF"), V("PFO", 12 * (l - 1), 12 * l)), V("E4096"), A.add)
-        scan(V("TB", 1, 32), V("TA", 0, 31), V("RESET", 1, 32), 0.0, A.add, A.mult)
+        tt(V("NV"), ind(V("PF"), V("PFO", 12 * (l - 1), 12 * l)), V("E4096"), ADD)
+        scan(V("TB", 1, 32), V("TA", 0, 31), V("RESET", 1, 32), 0.0, ADD, MUL)
         tr(V("TC"), V("TB"))
-        tt(V("t2", 0, 8), V("TC", 0, 8), V("CB"), A.add)
-        tt(V("L1", 0, 128), ind(V("t2", 0, 8), V("SEGO")), V("L3", 0, 128), A.add)
-        tt(V("L3", 128, 256), V("L1", 0, 128), V("L2", 0, 128), A.mult)
-        tt(V("L1", 128, 192), V("L3", 128, 192), V("L3", 192, 256), A.add)
-        tt(V("L1", 192, 224), V("L1", 128, 160), V("L1", 160, 192), A.add)
-        tt(V(off), V("L1", 192, 208), V("L1", 208, 224), A.add)
+        tt(V("t2", 0, 8), V("TC", 0, 8), V("CB"), ADD)
+        tt(V("L1", 0, 128), ind(V("t2", 0, 8), V("SEGO")), V("L3", 0, 128), ADD)
+        tt(V("L3", 128, 256), V("L1", 0, 128), V("L2", 0, 128), MUL)
+        tt(V("L1", 128, 192), V("L3", 128, 192), V("L3", 192, 256), ADD)
+        tt(V("L1", 192, 224), V("L1", 128, 160), V("L1", 160, 192), ADD)
+        tt(V(off), V("L1", 192, 208), V("L1", 208, 224), ADD)
         copy(V("OFU"), V(off, 0, 12))
         scatter(V(tl), V("OFU"), V("NV"))
         fold(V("L2", 0, K), V(tl, 0, K), K)
@@ -459,22 +492,20 @@ def rank_program(g, core, T, topo):
     fill("WL2", 14, 16, 0)
     lin(col(8), col(2), 0.5, 0.0)
     lin(col(7), col(2), -0.5, 0.5)
-    act(V("JT", 0, 128), V("IOTA", 0, 128), ACT.Abs, bias=col(5))
-    act(V("ID"), V("JT", 0, 128), ACT.Relu, bias=1.0, scale=-1.0)
-    act(V("ET", 3, 515, 4), V("ID"), scale=col(7))
+    ts(V("ET", 3, 515, 4), V("IOTA", 0, 128), col(0), A.is_equal, col(7), MUL)
     fold(V("SCI", M, C), V("INVF", M, C), 2 * M)
     copy(V("AU", 0, 176), V("ST"))
     for l in (2, 1):
         for k in range(2):
             a = 12 * (l - 1) + 6 * k
-            ts(V("PFO", a, a + 6), V("SCI", M * l + 15, M * l + M, 16), float(C * k), A.add)
+            ts(V("PFO", a, a + 6), V("SCI", M * l + 15, M * l + M, 16), float(C * k), ADD)
     for t in range(4):
         lin(V("OIF", 18 * t, 18 * t + 18), V("SCI", 15, C, 16), 4.0, float(t))
     codes(2)
     lists(2)
     copy(V("OI"), V("OIF"))
     unit("QH0")
-    act(V("ET", 3, 515, 4), V("ID"), scale=col(8))
+    ts(V("ET", 3, 515, 4), V("IOTA", 0, 128), col(0), A.is_equal, col(8), MUL)
     act(V("POSF", 1, C + 1), ind(V("IOTA", 0, C), V("POSU")))
     fill("PP", 144, 148, N * M)
     fill("POSF", 0, 1, 2 * M)
@@ -497,10 +528,10 @@ def rank_program(g, core, T, topo):
     for t in range(4):
         act(V("TYS", t, 4 * M, 4), ind(V("TY0"), V("OI", 18 * t, 18 * t + 6)))
     copy(V("PP", 0, 144), V("PPU"))
-    tt(V("L2"), ind(V("PP"), V("HI2")), V("MKL"), A.mult)
+    tt(V("L2"), ind(V("PP"), V("HI2")), V("MKL"), MUL)
     tr(V("L3"), V("L2"))
     for h in range(2):
-        scan(V("L1", 192 * h, 192 * h + 192), V("RESET", 0, 192), V("L3", 192 * h, 192 * h + 192), 0.0, A.mult, A.add)
+        scan(V("L1", 192 * h, 192 * h + 192), V("RESET", 0, 192), V("L3", 192 * h, 192 * h + 192), 0.0, MUL, ADD)
     for h in range(2):
         copy(V("OF1", 16 * h, 16 * h + 12), V("L1", 16 * h + 15, 384, 32))
 
@@ -522,15 +553,11 @@ def rank_program(g, core, T, topo):
             mm(bank("PB", b, 128), w, 128 * b, "QX", 0, 128)
         if between: between()
         for b in range(4):
-            o = V(tile, a + b, a + 4 * M, 4)
-            if b % 2: ts(o, bank("PB", b, M), 0.03125, A.mult)
-            else: act(o, bank("PB", b, M), scale=0.03125)
+            act(V(tile, a + b, a + 4 * M, 4), bank("PB", b, M), scale=0.03125)
 
     def compose(k, tile, off):
         for t in range(4):
-            o, i = V("SG", t, 4 * K, 4), ind(V(tile), V(off, 14 * t, 14 * t + 14))
-            if t % 2: copy(o, i)
-            else: act(o, i)
+            act(V("SG", t, 4 * K, 4), ind(V(tile), V(off, 14 * t, 14 * t + 14)))
         quant("S%d" % k, 0, 256, V("SG"))
         send_big(k)
 
@@ -545,11 +572,11 @@ def rank_program(g, core, T, topo):
     def keep(l):
         use[0] = "c"
         copy(V("PC%d" % l, 0, 14), V("L2", 15, K, 16))
-        ts(V("KC%d" % l, 0, 14), V("LL%d" % l), 4096.0 * 128, A.is_ge, float(2 * M), A.mult)
+        ts(V("KC%d" % l, 0, 14), V("LL%d" % l), 4096.0 * 128, A.is_ge, float(2 * M), MUL)
 
     def own(l):
         use[0] = "b"
-        ts(V("JO"), V("NW%d" % l, 15, 2 * M, 16), -float(C * (N - 1) - 1), A.add)
+        ts(V("JO"), V("NW%d" % l, 15, 2 * M, 16), -float(C * (N - 1) - 1), ADD)
         fold(V("L2", 0, 2 * M), ind(V("POSF", 0, C + 2), V("JO")), 2 * M)
         copy(V("PC%d" % l, 14, 26), V("L2", 15, 2 * M, 16))
 
@@ -558,15 +585,15 @@ def rank_program(g, core, T, topo):
         copy(V("i1", 0, 14), V("WL%d" % l, 0, 14))
         ts(V("i2", 0, 14), V("i1", 0, 14), 12, A.logical_shift_right, 127, A.bitwise_and)
         for t in range(4):
-            ts(V(out, 14 * t, 14 * t + 14), V("i2", 0, 14), 4.0, A.mult, float(t), A.add)
+            ts(V(out, 14 * t, 14 * t + 14), V("i2", 0, 14), 4.0, MUL, float(t), ADD)
 
     def successors(l):
         use[0] = "d"
         pc, kc = V("PC%d" % l), V("KC%d" % l)
         ts(V("t2", 0, 26), pc, float(2 * M), A.is_ge)
-        tt(V("t3", 0, 26), pc, kc, A.add)
-        tt(V("t4", 0, 26), V("t2", 0, 26), V("IDXC"), A.mult)
-        tt(V("t1", 0, 26), V("t3", 0, 26), V("t4", 0, 26), A.add)
+        tt(V("t3", 0, 26), pc, kc, ADD)
+        tt(V("t4", 0, 26), V("t2", 0, 26), V("IDXC"), MUL)
+        tt(V("t1", 0, 26), V("t3", 0, 26), V("t4", 0, 26), ADD)
         copy(V("SUO"), V("t1", 0, 26))
         scatter(V("SU"), V("SUO"), V("VAL%d" % l))
         act(V("SD"), ind(V("SU", M * (l - 1), 4 * M), V("DBL")))
@@ -579,18 +606,18 @@ def rank_program(g, core, T, topo):
 
     def places():
         use[0] = "c"
-        ts(V("t1", 0, 18), V("POSW"), M + 0.5, A.is_ge, -float(K), A.mult)
-        ts(V("t2", 0, 18), V("POSW"), 2 * M + 0.5, A.is_ge, -float(2 * K), A.mult)
-        tt(V("t3", 0, 18), V("t1", 0, 18), V("POSW"), A.add)
-        tt(V("t4", 0, 18), V("t3", 0, 18), V("t2", 0, 18), A.add)
-        ts(V("POSZ"), V("t4", 0, 18), float(2 * K + 255), A.add)
+        ts(V("t1", 0, 18), V("POSW"), M + 0.5, A.is_ge, -float(K), MUL)
+        ts(V("t2", 0, 18), V("POSW"), 2 * M + 0.5, A.is_ge, -float(2 * K), MUL)
+        tt(V("t3", 0, 18), V("t1", 0, 18), V("POSW"), ADD)
+        tt(V("t4", 0, 18), V("t3", 0, 18), V("t2", 0, 18), ADD)
+        ts(V("POSZ"), V("t4", 0, 18), float(2 * K + 255), ADD)
 
     def asked():
         fill("TYS", 8 * M, 896, 0)
         fill("SG", 4 * K, 1024, 0)
         arrived(2)
         for t in range(4):
-            ts(V("G2", 14 * t, 14 * t + 14), V("L2", 15, K, 16), 4.0, A.mult, float(t), A.add)
+            ts(V("G2", 14 * t, 14 * t + 14), V("L2", 15, K, 16), 4.0, MUL, float(t), ADD)
 
     gather_sum("P1", "WF1", 896, "OF1", 16, lambda b: V("DS", 192 * b, 192 * b + M), asked)
     layer("QW", "TYS", 4 * M, lambda: keep(2))
@@ -615,9 +642,9 @@ def rank_program(g, core, T, topo):
     fill("WL1", 14, 16, 0)
     lin(V("VAL1"), V("VAL2"), 1.0, float(K + 128))
     own(2)
-    ts(V("t1", 0, 12), V("OFF2", 0, 12), float(K), A.is_ge, 1000.0, A.mult)
-    ts(V("t2", 0, 12), V("PC2", 14, 26), float(K), A.add)
-    tt(V("t3", 0, 12), V("t1", 0, 12), V("OFF2", 0, 12), A.add)
+    ts(V("t1", 0, 12), V("OFF2", 0, 12), float(K), A.is_ge, 1000.0, MUL)
+    ts(V("t2", 0, 12), V("PC2", 14, 26), float(K), ADD)
+    tt(V("t3", 0, 12), V("t1", 0, 12), V("OFF2", 0, 12), ADD)
     tt(V("W32", 0, 12), V("t3", 0, 12), V("t2", 0, 12), A.min)
     tr(V("D1"), V("W32"))
     copy(V("D2"), ind(V("D1"), V("DUPO")))
@@ -631,8 +658,7 @@ def rank_program(g, core, T, topo):
     for b in range(4):
         mm(bank("PA", b, 128), "QE", 128 * b, "QY2", 0, 128)
     for b in range(4):
-        if b % 2: copy(V("TX", b, 4 * M, 4), bank("PA", b, M))
-        else: act(V("TX", b, 4 * M, 4), bank("PA", b, M))
+        act(V("TX", b, 4 * M, 4), bank("PA", b, M))
     layer("QV", "TZ2", 0)
     compose(3, "TZ2", "G3")
     lists(1)

@@ -6,50 +6,56 @@ K = (N - 1) * CAP
 F, B, I, U, X4, SC = "float32", "bfloat16", "int32", "uint16", "float8_e4m3fn_x4", "uint8"
 ROUND = 12582912
 EMPTY = 4095 + 4096 * (128 + M)
+STEP = float(1 << 20)
+Y0, HALF = C, C + 128
+OWN = (N - 1) * M
+YW, ZW = 208, 112
 
-PACK_U = "DUPO KOFF SEGO DBL OF1 OF3 OF4 CODE POSU POSZ INV0 OI PFO OFU HI2 LO2 JU JO SUO OF2 G2 G3 G4".split()
-PACK_F = "t1 t2 t3 t4 TA TB TC TT TW D1 D2 D3 W32 OFF1 OFF2 PC1 PC2 KC1 KC2 CB CJ IDXC POSW OIF MK CS NM CT CU CV CW".split()
+PACK_U = "DUPO KOFF DBL OF1 OF3 OF4 CODE POSU POSZ INV0 INV12 PFO OFU HI2 LO2 JU JO SUO OF2 G2 G3 G4".split()
+PACK_F = ("t1 t2 t3 t4 TA TB TC TT TW D1 D2 D3 W32 OFF1 OFF2 PC1 PC2 KC1 KC2 CB CJ IDXC ETAB NW1 NW2 MK CS NM CT CU CV CW "
+          "C3 PS R3 R32 R18 MP T7 U7 V7 W7 B7").split()
 PLACE = {}
 TEMPS = "t1 t2 t3 t4 i1 i2 i3 L1 L2 L3".split()
-TRAVEL = {"p": 8.0, 1: 6.5, "l2": 4.0, 2: 4.5, 3: 4.5, "l1": 4.0, 4: 4.5}
-HOP = 0.12
-SLACK = 0.6
+LAID = "010a0I1g0O1m221W0U281E1sb80m0d2w3G1L0s10fubD2f0y3i3p162UazbP0E612I1c2C6j3A2O3vk32k36qfbI3d67313N1z6d4K455k5q5w4SbUqw6o7y7s3T6M6ubkqC1Q6A6S3Z6G7Ec67K6Y747ajW4a7g7Q7mfp7W4g824pat4v4B4H51542r5C5Pr15ac05gaR88bf5U5Jccci8ebqcocG8D8x8lcM8rf6cSqPaEr7cucY8Igad5ql8R8Xda939d99gg9j9pdg9vfH9AaLdncAb3gmeU9Ia2fZdsgsa8f0fTC29OdyfcssC9dEs5gyfi9Xbxi1szaXqJi6dKgEgKicdQhqijshfBdWhkGoe2ioGviugQe8iACehPqVeeiGh8hDgWekiMsEeqsLh3g5sQiSsXewqriYeDCkeKj4CreTjaNQCwjgt2jmCCwqt8jtO2tejyCItlwwjEhJCOwCaejQhVjKheakl7l0aqljlclDlvlolJlPlVCUhxm1fNm7mdmjmpk8kUmvmBkemHD0mNmTkkmZnen5kqn8nkkxnqtqnwD6kCnFnLDcnRo1nXkIkPDio7octwoptCoioAovGAoHtItOpnoMp5tUpgpboUpWpRq8q3u0psp0DorcpAu6rlrrpGrxrHrDsbpPrZDurNsnrTudupuiuuuBuVuGuNv1v7wIvdvjvpvvDAvBvHvNvTvZw5wbx6whx0wnxcwOxixoDGxxG6xDxJxZGcxPy4yaxSyhymwUyvyByHyQyNyWGiz3z9zeznztzzzJzFzOzUA0AdA6ApAiANAZAuASB5ACBEBRBKBaAIByBWBiGGBoBxDODXE5DYEaEhEBEmEtEHENJYETEZF5K4FbFhKaFnFtKgFzFFKnFLFRGSFXGMG3GYH4HaKsHjNWHpKEHvKzHEHBO8HLKKHRKQI2HXI9IeIlKWIJIqJ1L2IOIVIyL8JvJGJNJ6JBIELeJeJkJtOeLlLqJSLCLILPLwM1LUMlMdM6MrMxMDMJMPMVN1N7NdNjNpOkNvNBOqNHNNOwOCOIOROXP3P9PjPdPoPuPAPGPNPSPZQ7QkQRQdQqQtQyQLQIQX"
+LETTERS = "0123456789abcdefghijklmnopqrstuvwxyzABCDEFGHIJKLMNOPQRSTUVWXYZ"
 
 
 def _scratch():
     s = {}
     for n, w, d in [
-        ("IOTA", 2308, F), ("PI", 4, I), ("CC", 16, F), ("J16", 224, F), ("JT", 224, F), ("DIAG", 224, B), ("RESET", 224, B),
-        ("KEYC", 128, F), ("CJ", 14, F), ("CB", 8, F), ("IDXC", 26, F), ("E4096", 192, F), ("VAL2", 416, F), ("VAL1", 416, F),
-        ("DUPO", 4, U), ("KOFF", 8, U), ("SEGO", 8, U), ("ST", 176, F), ("OIF", 72, F),
+        ("IOTA", 2308, F), ("PI", 4, I), ("CC", 16, F), ("J16", 224, F), ("JT", 224, F), ("DIAG", 224, B), ("RESET", 224, B), ("DD", 224, F),
+        ("KEYC", 128, F), ("CJ", 14, F), ("CB", 8, F), ("IDXC", 26, F), ("E4096", 192, F), ("ETAB", 12, F), ("VAL2", 416, F), ("VAL1", 416, F),
+        ("DUPO", 4, U), ("KOFF", 8, U), ("ST", 160, F),
         ("ET", 520, B), ("LVT", 18, I), ("PR", 36, I), ("CODE", 36, U), ("PF", 576, F),
         ("t1", 36, F), ("t2", 36, F), ("t3", 36, F), ("t4", 36, F), ("i1", 32, I), ("i2", 32, I), ("i3", 32, I),
         ("MK", 96, F), ("CS", 96, F), ("NM", 96, F), ("CT", 96, F), ("CU", 96, F), ("CV", 96, F), ("CW", 96, F),
-        ("L1", 384, F), ("L2", 384, F), ("L3", 384, F), ("MKL", 384, B), ("SD", 384, F),
-        ("POSW", 18, F), ("POSU", 18, U), ("POSS", 18, U), ("POSZ", 18, U), ("POSF", 292, F), ("PP", 148, F), ("PPU", 144, U),
-        ("INVF", 288, F), ("SCI", 288, F), ("INV0", 6, U), ("OI", 72, U), ("PFO", 24, U),
-        ("NW1", 192, F), ("NW2", 192, F), ("NV", 192, F), ("TW", 16, F), ("TT", 32, F), ("TA", 32, F), ("TB", 32, F), ("TC", 32, F),
+        ("C3", 54, F), ("PS", 54, F), ("R3", 54, F), ("R32", 96, F),
+        ("R18", 126, F), ("MP", 126, F), ("T7", 32, F), ("U7", 32, F), ("V7", 32, F), ("W7", 32, F), ("B7", 7, F),
+        ("L1", 384, F), ("L2", 384, F), ("L3", 384, F), ("MKL", 192, B), ("SD", 384, F),
+        ("POSU", 18, U), ("POSS", 18, U), ("POSZ", 18, U), ("POSF", 292, F), ("PP", 148, F), ("PPU", 128, U),
+        ("INVF", 288, F), ("SCI", 192, F), ("INV0", 6, U), ("INV12", 12, U), ("PFO", 24, U),
+        ("NW1", 12, F), ("NW2", 12, F), ("NV1", 192, F), ("NV2", 192, F), ("TW", 16, F), ("TT", 32, F), ("TA", 32, F), ("TB", 32, F), ("TC", 32, F),
         ("OFF1", 16, F), ("OFF2", 16, F), ("OFU", 12, U), ("TL1", 416, F), ("TL2", 416, F), ("WL1", 16, F), ("WL2", 16, F),
-        ("LL1", 14, F), ("LL2", 14, F), ("HI2", 24, U), ("LO2", 24, U), ("JU", 14, U), ("JO", 12, U),
+        ("LL1", 14, F), ("LL2", 14, F), ("HI2", 12, U), ("LO2", 12, U), ("JU", 14, U), ("JO", 12, U),
         ("PC1", 26, F), ("PC2", 26, F), ("KC1", 26, F), ("KC2", 26, F), ("SUO", 26, U), ("SU", 800, F),
         ("W32", 32, F), ("D1", 32, F), ("D2", 64, F), ("D3", 64, F), ("DBL", 24, U),
-        ("OF1", 32, U), ("OF2", 64, U), ("OF3", 32, U), ("OF4", 32, U), ("G2", 56, U), ("G3", 56, U), ("G4", 56, U),
-        ("TXN", 1152, B), ("X0", 1152, B), ("TY0", 1152, B), ("TX", 512, B), ("TYS", 896, B), ("TY2", 512, B),
-        ("TZ2", 512, B), ("TZ1", 512, B), ("TZ0", 512, B), ("SG", 1024, B), ("DS", 768, B), ("DY", 768, B),
+        ("OF1", 32, U), ("OF2", 64, U), ("OF3", 32, U), ("OF4", 32, U), ("G2", 14, U), ("G3", 14, U), ("G4", 14, U),
+        ("TXN", 1152, B), ("X0", 1152, B), ("TX", 512, B), ("TYS", 896, B), ("TZ", 512, B), ("YP", 4 * YW, B), ("ZP", 4 * ZW, B),
+        ("SG", 1024, B), ("DS", 768, B), ("DY", 768, B),
         ("TU", 512, B), ("YO", 288, F), ("HP", 18, U), ("HL1", 4, F), ("HL2", 4, F),
     ]:
         s[n] = ("sbuf", [128, w], d)
-    for n, w in [("QE", 512), ("QH0", 512), ("QH1", 512), ("QW", 512), ("QV", 512), ("QU", 128), ("QS", 384), ("QX0", 288),
-                 ("QY0", 288), ("QX", 128), ("QY2", 128), ("WF1", 896), ("WF2", 448), ("WB", 832), ("QO", 288),
-                 ("P1", 416), ("P2", 416), ("P3", 416), ("P4", 416), ("S2", 256), ("S3", 256), ("S4", 256),
+    for n, w in [("QE", 512), ("QH0", 512), ("QH1", 512), ("QW", 512), ("QV", 512), ("QU", 128), ("QS", HALF + 6 * 128),
+                 ("QX", 128), ("QY2", 128), ("WF1", OWN + 128), ("WF2", 448), ("WB", 832), ("QO", 288),
+                 ("P1", 416), ("P2", 416), ("P3", 416), ("P4", 416),
                  ("H1", 96), ("H2", 64), ("H3", 64), ("H4", 64)]:
         s[n + "c"] = ("sbuf", [128, w], X4)
         s[n + "s"] = ("sbuf", [128, w], SC)
     for n in TEMPS:
         for c in "bcd": s[n + c] = s[n]
-    for c in "0123": s["FL" + c] = ("sbuf", [128, 224], F)
+    for c in "01234567": s["FL" + c] = ("sbuf", [128, 224], F)
     more = lambda first: [n + c for n in TEMPS if n[0] in first for c in ("", "b", "c", "d") if n + c not in PACK_F]
-    for arena, d, names in (("AU", U, PACK_U), ("AF", F, PACK_F + more("tL") + ["FL" + c for c in "0123"]), ("AI", I, more("i"))):
+    for arena, d, names in (("AU", U, PACK_U), ("AF", F, PACK_F + more("tL") + ["FL" + c for c in "01234567"]), ("AI", I, more("i"))):
         at = 0
         for n in names:
             PLACE[n] = (arena, at, s[n][1][1])
@@ -61,11 +67,12 @@ def _scratch():
 
 
 SCRATCH = _scratch()
-SEMAPHORES = (["cv", "ca", "cp", "cg", "ls", "dl"] + ["d%d" % i for i in range(18)] + ["xp", "xl1", "xl2", "x1", "x2", "x3", "x4"]
+SEMAPHORES = (["cv", "ca", "cp", "cg", "ls", "dl"] + ["d%d" % i for i in range(22)] + ["xp", "xl1", "xl2", "x1", "x2", "x3", "x4"]
               + ["hp", "hl1", "hl2"] + ["hc%d" % i for i in (1, 2, 3, 4)] + ["hs%d" % i for i in (1, 2, 3, 4)])
-BIG = {1: ("QS", "WF1", M, 0), 2: ("S2", "WF2", CAP, 0), 3: ("S3", "WB", CAP, 0), 4: ("S4", "WB", CAP, K + 128)}
+BIG = {1: ("WF1", M, 0), 2: ("WF2", CAP, 0), 3: ("WB", CAP, 0), 4: ("WB", CAP, K + 128)}
 SMALL = {"p": ("POSS", "HP", "PPU", 18), "l2": ("WL2", "HL2", "LL2", 2), "l1": ("WL1", "HL1", "LL1", 2)}
 ORDER = ["p", 1, "l2", 2, 3, "l1", 4]
+SCALES = [4, 5, 6, 3]
 
 
 def _bits(engines):
@@ -88,10 +95,6 @@ def _to(topo, src, dst, mask, sem, a, b):
     return RemoteDMATransfer(dst_ids=[DstId(rid=rid, pnc=pid)], dma_engine_mask=mask, remote_sem=sem, src=a, dst=b)
 
 
-def _land(k, r, u):
-    return M * r if k == 1 else BIG[k][3] + CAP * (N - 2 - u)
-
-
 def helper_program(g, core, T, topo, r, h):
     peer = [T.cores[(r + 1 + u) % N] for u in range(N - 1)]
     eng = topo.engines(core, peer[0])
@@ -101,24 +104,24 @@ def helper_program(g, core, T, topo, r, h):
     for k in ORDER:
         if k in SMALL:
             _s, hb, land, w = SMALL[k]
-            if k != "p" and h < 3: continue
-            us = [h] if k == "p" else pair((h - 4) % 4)
+            if k != "p" and h not in SCALES: continue
+            us = [h] if k == "p" else pair(SCALES.index(h))
             n = len(eng) // len(us)
             g.wait_ge(T.sem["h" + k], 2 if k == "p" else 4)
             g.remote_dma_fused([_to(topo, core, peer[u], _bits(eng[n * j:n * j + n]), T.sem["x" + k], T[hb][:, w * j:w * j + w],
                                     T[land][:, w * (N - 2 - u):w * (N - 1 - u)]) for j, u in enumerate(us)], local_sem=T.sem.ls)
             sent += len(eng)
             continue
-        _s, land, w, _o = BIG[k]
+        land, w, o0 = BIG[k]
         jobs = []
         if h <= 3: jobs.append(("c", pair(h)))
-        if h >= 3: jobs.append(("s", pair((h - 4) % 4)))
+        if h in SCALES: jobs.append(("s", pair(SCALES.index(h))))
         at = 0
         for kind, us in jobs:
-            g.wait_ge(T.sem["h%s%d" % (kind, k)], 4)
+            g.wait_ge(T.sem["h%s%d" % (kind, k)], 4 if k == 1 else 8)
             ts = []
             for u in us:
-                o = _land(k, r, u)
+                o = o0 + w * (N - 2 - u)
                 a = 0 if k == 1 else w * (u % 2)
                 src, dst = T["H%d%s" % (k, kind)][:, a:a + w], T[land + kind][:, o:o + w]
                 if kind == "c": src, dst = src.bitcast(dt.uint8), dst.bitcast(dt.uint8)
@@ -190,72 +193,39 @@ def rank_program(g, core, T, topo):
         for x in ws: log.setdefault(x[0], []).append((x, True, tok))
         final[tok[0]] = max(final.get(tok[0], 0), tok[1])
 
-    def later(e, emit, writes, reads, cost, lat):
+    def later(e, emit, writes, reads):
         rs = [x for v in reads if isinstance(v, tuple) for x in v[1]]
-        nodes.append((e, emit, rs, [x for v in writes for x in v[1]] + [x for x in rs if x[0] in ("PA", "PB")], cost, lat))
+        nodes.append((e, emit, rs, [x for v in writes for x in v[1]] + [x for x in rs if x[0] in ("PA", "PB")]))
 
-    def op(e, call, writes, reads, acc=False, rate=1.0):
+    def op(e, call, writes, reads, acc=False):
         def emit(e):
             rs, ws = order(e, reads, writes, acc)
             count[e] += 1
             (call[e] if isinstance(call, dict) else call)().then_inc(T.sem["c" + e], 1)
             note(rs, ws, ("c" + e, count[e], dict(known[e])))
-        x = writes[0][1][0]
-        n = -(-(x[2] - x[1]) // x[3])
-        if x[0] in ("PA", "PB"): n = reads[2][1][0][2] - reads[2][1][0][1] + 16
-        if reads and isinstance(reads[0], tuple) and len(reads[0][1]) == 2: rate = 1.7
-        later(e, emit, writes, reads, max(64, n * rate) * 0.00105, HOP)
+        later(e, emit, writes, reads)
 
     def schedule():
-        n = len(nodes)
-        pre, seen, last = [set() for _ in nodes], {}, {}
-        for i, (e, _e, rs, ws, _c, _l) in enumerate(nodes):
-            for x, w in [(x, False) for x in rs] + [(x, True) for x in ws]:
-                for y, yw, j in seen.get(x[0], []):
-                    if (w or yw) and meet(x, y): pre[i].add(j)
-            key = "g" if e == "x" else e
-            if key in "gps" and key in last: pre[i].add(last[key])
-            if e in "gps": last[e] = i
-            for x in rs: seen.setdefault(x[0], []).append((x, False, i))
-            for x in ws: seen.setdefault(x[0], []).append((x, True, i))
-        way, post = [0.0] * n, [[] for _ in nodes]
-        for i in range(n - 1, -1, -1):
-            way[i] = nodes[i][4] + nodes[i][5] + max([way[j] for j in post[i]], default=0.0)
-            for j in pre[i]: post[j].append(i)
-        left, ready, free, cand = [len(p) for p in pre], [0.0] * n, {}, [i for i in range(n) if not pre[i]]
-        while cand:
-            i = min(cand, key=lambda j: (min(max(ready[j], free.get(q, 0.0)) for q in nodes[j][0]), -way[j]))
-            e = min(nodes[i][0], key=lambda q: max(ready[i], free.get(q, 0.0)))
-            t = max(ready[i], free.get(e, 0.0))
-            i = max([j for j in cand if e in nodes[j][0] and ready[j] <= t], key=lambda j: way[j])
-            soon = [j for j in cand if nodes[j][0] == e and way[j] > way[i] and ready[j] < t + SLACK * nodes[i][4]]
-            if soon: i = max(soon, key=lambda j: way[j])
-            t = max(t, ready[i])
-            cand.remove(i)
-            nodes[i][1](e)
-            if e != "x": free[e] = t + nodes[i][4]
-            for j in post[i]:
-                same = nodes[j][0] == e and e in "gps"
-                ready[j] = max(ready[j], t + nodes[i][4] + (0.0 if same else nodes[i][5]))
-                left[j] -= 1
-                if not left[j]: cand.append(j)
+        for k in range(0, len(LAID), 2):
+            z = len(LETTERS) * LETTERS.index(LAID[k]) + LETTERS.index(LAID[k + 1])
+            nodes[z // 6][1]("vagpsx"[z % 6])
 
     def raw(v):
         return v[0] if isinstance(v, tuple) else v
 
-    def dma(e, out, in_, lat=2.0):
+    def dma(e, out, in_):
         def emit(_e):
             rs, ws = order(e, [in_], [out])
             s = "d%d" % count["d"]
             count["d"] += 1
             queue[e].dma_start(out[0], in_[0]).then_inc(T.sem[s], 16)
             note(rs, ws, (s, 16, dict(known[e])))
-        later(e, emit, [out], [in_], 0.3, lat)
+        later(e, emit, [out], [in_])
 
     def ext(ap):
         return (ap, [])
 
-    def memset(o, c): op("v", lambda: g.vector.memset(o[0], c), [o], [], rate=0.6)
+    def memset(o, c): op("v", lambda: g.vector.memset(o[0], c), [o], [])
     def real(v): return SCRATCH[v[1][0][0]][2] in (F, B, SC)
 
     def either(o, i, scale=None, bias=None):
@@ -271,7 +241,7 @@ def rank_program(g, core, T, topo):
         if real(o) and real(i): either(o, i)
         else: op("v", lambda: g.vector.tensor_copy(o[0], i[0]), [o], [i])
 
-    def tt(o, a, b, f): op("v", lambda: g.vector.tensor_tensor(o[0], a[0], b[0], f), [o], [a, b], rate=1.0 if b[1][0][0] == "PA" else 2.0)
+    def tt(o, a, b, f): op("v", lambda: g.vector.tensor_tensor(o[0], a[0], b[0], f), [o], [a, b])
     def tr(o, i): op("v", lambda: g.vector.transpose(o[0], i[0]), [o], [i])
 
     def ts(o, a, s1, f1, s2=None, f2=None):
@@ -292,68 +262,77 @@ def rank_program(g, core, T, topo):
         op("a", lambda: g.scalar.activation(o[0], i[0], f, **kw), [o], [i, bias, scale])
 
     def iota(o, pat, base, cm, fl=True):
-        if fl: op("g", lambda: g.iota(o[0], pat, base, cm, allow_small_or_imprecise_dtypes=True), [o], [], rate=2.2)
+        if fl: op("g", lambda: g.iota(o[0], pat, base, cm, allow_small_or_imprecise_dtypes=True), [o], [])
         else: op("g", lambda: g.iota(o[0], pat, base, cm), [o], [])
 
     def quant(q, a, n, tile):
         c, s = V(q + "c", a, a + n), V(q + "s", a, a + n)
-        op("v", lambda: g.vector.quantize_mx(c[0], s[0], tile[0]), [c, s], [tile], rate=1.1)
+        op("v", lambda: g.vector.quantize_mx(c[0], s[0], tile[0]), [c, s], [tile])
 
     def mm(out, w, wa, x, xa, n, start=True, stop=True):
         wc, ws, xc, xs = V(w + "c", wa, wa + 128), V(w + "s", wa, wa + 128), V(x + "c", xa, xa + n), V(x + "s", xa, xa + n)
-        op("p", lambda: g.tensor.matmul_mx(out[0], wc[0], ws[0], xc[0], xs[0], start, stop), [out], [wc, ws, xc, xs], acc=not start, rate=0.6)
+        op("p", lambda: g.tensor.matmul_mx(out[0], wc[0], ws[0], xc[0], xs[0], start, stop), [out], [wc, ws, xc, xs], acc=not start)
 
     def pick(q, a, win, wn, off, n):
         copy(words(V(q + "c", a, a + n)), ind(words(V(win + "c", 0, wn)), off))
-        act(V(q + "s", a, a + n), ind(V(win + "s", 0, wn), off))
+        copy(V(q + "s", a, a + n), ind(V(win + "s", 0, wn), off))
 
     def col(i): return V("CC", i, i + 1)
 
-    def fold(o, table, n):
+    def fold(table, n):
+        if len(table[1]) == 2:
+            folds[0] += 1
+            tmp = V("FL%d" % (folds[0] % 8), 0, n)
+            copy(tmp, table)
+            table = tmp
         folds[0] += 1
-        tmp = V("FL%d" % (folds[0] % 4), 0, n)
-        tt(tmp, table, V("DIAG", 0, n), MUL)
-        scan(o, V("RESET", 0, n), tmp, 0.0, MUL, ADD)
+        name = "FL%d" % (folds[0] % 8)
+        scan(V(name, 0, n), V("DD", 0, n), table, 0.0, ADD, A.max)
+        return V(name, 15, n, 16)
 
     peer = [T.cores[(r + 1 + u) % N] for u in range(N - 1)]
     help_ = _helpers(topo, core)
     out_engines = len(topo.engines(core, peer[0]))
+    u8 = lambda v: (v[0].bitcast(dt.uint8), v[1])
 
-    def hand(to, e, sem, src, dst, reads):
+    def hand(e, jobs):
+        reads = [j[2] for j in jobs]
+        mask = lambda h, i: _bits(topo.engines(core, help_[h])[2 * e * (i // 2):2 * e * (i // 2 + 1)][i % 2::2])
+
         def emit(_e):
-            order("g", [reads], [])
-            g.remote_dma_fused([_to(topo, core, help_[h], _bits(topo.engines(core, help_[h])[e * i:e * i + e]), T.sem[sem], src(i), dst)
-                                for i, h in enumerate(to)], local_sem=T.sem.ls)
-            count["ls"] += e * len(to)
-        later("g", emit, [], [reads], 0.5, 0.0)
+            order("g", reads, [])
+            g.remote_dma_fused([_to(topo, core, help_[h], mask(h, i), T.sem[sem], src[0], dst)
+                                for i, (h, sem, src, dst) in enumerate(jobs)], local_sem=T.sem.ls)
+            count["ls"] += e * len(jobs)
+        later("g", emit, [], reads)
 
     def arrives(views, k, n):
-        later("x", lambda _e: note([], [x for v in views for x in v[1]], ("x%s" % k, n * out_engines, {})), views, [], TRAVEL[k], 0.0)
+        later("x", lambda _e: note([], [x for v in views for x in v[1]], ("x%s" % k, n * out_engines, {})), views, [])
 
     def send_small(k):
         src, hb, land, w = SMALL[k]
-        if k == "p": hand(range(N - 1), 2, "hp", lambda i: T[src][:, 0:w], T[hb][:, 0:w], V(src))
-        else: hand([4, 5, 6, 3], 4, "h" + k, lambda i: T[src][:, 2 * w * i:2 * w * i + 2 * w], T[hb][:, 0:2 * w], V(src))
+        if k == "p": hand(2, [(h, "hp", V(src), T[hb][:, 0:w]) for h in range(N - 1)])
+        else: hand(4, [(h, "h" + k, V(src, 2 * w * i, 2 * w * i + 2 * w), T[hb][:, 0:2 * w]) for i, h in enumerate(SCALES)])
         arrives([V(land, 0, w * (N - 1))], k, N - 1 if k == "p" else 4)
 
-    def send_big(k):
-        src, land, w, o0 = BIG[k]
-        hw, step = (w, 0) if k == 1 else (2 * w, 2 * w)
-        hand([0, 1, 2, 3], 4, "hc%d" % k, lambda i: T[src + "c"][:, step * i:step * i + hw].bitcast(dt.uint8),
-             T["H%dc" % k][:, 0:hw].bitcast(dt.uint8), V(src + "c", 0, 3 * step + hw))
-        hand([4, 5, 6, 3], 4, "hs%d" % k, lambda i: T[src + "s"][:, step * i:step * i + hw], T["H%ds" % k][:, 0:hw], V(src + "s", 0, 3 * step + hw))
-        if k == 1:
-            views = [V(land + c, M * s, M * s + M) for c in "cs" for s in range(N) if s != r]
-        else:
-            views = [V(land + c, o0, o0 + K) for c in "cs"]
-        arrives(views, k, N - 1)
+    def send_whole():
+        hand(4, [(h, "hc1", u8(V("QSc", Y0, Y0 + M)), T.H1c[:, 0:M].bitcast(dt.uint8)) for h in range(4)])
+        hand(4, [(h, "hs1", V("QSs", Y0, Y0 + M), T.H1s[:, 0:M]) for h in SCALES])
+        arrives([V("WF1" + c, 0, OWN) for c in "cs"], 1, N - 1)
+
+    def send_half(k, h):
+        a = HALF + 128 * (2 * (k - 2) + h)
+        hand(8, [(2 * h + i, "hc%d" % k, u8(V("QSc", a + 64 * i, a + 64 * i + 64)), T["H%dc" % k][:, 0:64].bitcast(dt.uint8)) for i in range(2)])
+        hand(8, [(SCALES[2 * h + i], "hs%d" % k, V("QSs", a + 64 * i, a + 64 * i + 64), T["H%ds" % k][:, 0:64]) for i in range(2)])
+        if h:
+            land, _w, o0 = BIG[k]
+            arrives([V(land + c, o0, o0 + K) for c in "cs"], k, N - 1)
 
     def scatter(win, off, val):
-        op("v", lambda: g.vector.tensor_copy(win[0].indirect(off[0]), val[0]), [win], [off, val],
-           rate=3.5 * (val[1][0][2] - val[1][0][1]) / (win[1][0][2] - win[1][0][1]))
+        op("v", lambda: g.vector.tensor_copy(win[0].indirect(off[0]), val[0]), [win], [off, val])
 
-    def fill(name, a, b, c):
-        either(V(name, a, b), V("IOTA", 0, b - a), 0.0, float(c))
+    def fill(name, a, b, c, step=1):
+        either(V(name, a, b, step), V("IOTA", 0, -(-(b - a) // step)), 0.0, float(c))
 
     def lin(o, i, scale, bias):
         either(o, i, scale, bias)
@@ -362,204 +341,222 @@ def rank_program(g, core, T, topo):
         for b in range(4):
             quant(q, 128 * b, 128, V("ET", 3 - b, 515 - b))
 
-    u8 = lambda v: (v[0].bitcast(dt.uint8), v[1])
-
     def levels(e, h):
         def emit(_e):
             for k in range(4 * h, 4 * h + 4):
                 queue[e].dma_start(T.LVT[16 * k:16 * k + 16, :], T.lv[:]).then_inc(T.sem.dl, 16)
             note([], V("LVT", 9 * h, 9 * h + 9)[1], ("dl", 128, {}))
-        later(e, emit, [V("LVT", 9 * h, 9 * h + 9)], [], 0.6, 1.8)
+        later(e, emit, [V("LVT", 9 * h, 9 * h + 9)], [])
 
     levels("a", 0)
-    dma("s", V("TXN"), ext(T.x[:]), 2.8)
     levels("s", 1)
-    dma("a", V("PR", 0, 18), ext(T.pr0[:]), 2.0)
-    dma("a", V("PR", 18, 36), ext(T.pr1[:]), 2.0)
+    dma("a", V("PR", 0, 18), ext(T.pr0[:]))
+    dma("s", V("PR", 18, 36), ext(T.pr1[:]))
+    dma("s", V("TXN"), ext(T.x[:]))
     dma("s", V("QWs"), ext(T.ws[:]))
-    dma("s", u8(V("QWc")), ext(T.wc[:]), 3.5)
-    dma("s", V("QVs"), ext(T.vs[:]))
-    dma("s", u8(V("QVc")), ext(T.vc[:]))
-    dma("s", V("TU"), ext(T.u[:]), 12.0)
+    dma("s", u8(V("QWc")), ext(T.wc[:]))
 
     iota(V("PI", 0, 1), [[1, 1]], 0, 1, fl=False)
-    iota(V("IOTA", 0, 577), [[1, 577]], 0, 0)
+    iota(V("IOTA", 0, 128), [[1, 128]], 0, 0)
     iota(V("J16"), [[0, 14], [1, 16]], 0, 0)
-    iota(V("KEYC"), [[1, 8], [0, 16]], ROUND, 0)
-    iota(V("CJ"), [[-C, N - 1], [0, 2]], C * (N - 2) - 1, 0)
-    iota(V("IOTA", 1731, 2308), [[1, 577]], 1731, 0)
+    iota(V("R32"), [[0, 3], [1024, 32]], 0, 0)
+    iota(V("R3"), [[0, 18], [1024, 3]], 0, 0)
+    iota(V("IOTA", 128, 288), [[1, 160]], 128, 0)
     memset(V("ET"), 0.0)
-    memset(V("TX"), 0.0)
-    memset(V("ST"), 0.0)
-    for n in ("MK", "CS"): memset(V(n), 0.0)
+    memset(V("MK"), 0.0)
     memset(V("CU", 0, 1), 0.0)
+    fill("TX", 4 * M, 512, 0)
+    fill("TYS", 4 * M, 512, 0)
+    fill("ST", 0, 128, 0)
+    fill("ST", 128, 160, 0)
     ts(V("PI", 1, 2), V("PI", 0, 1), 15, A.bitwise_and)
     ts(V("PI", 2, 3), V("PI", 0, 1), 4, A.logical_shift_right, 1, A.bitwise_and)
-    quant("WF1", N * M, 128, V("TX"))
     copy(V("CC", 0, 3), V("PI", 0, 3))
     ts(col(9), col(1), float(2 * M), ADD)
+    lin(col(10), col(1), STEP, -15 * STEP)
+    lin(col(11), col(1), 4096.0 - STEP, 15 * STEP)
     ts(V("ET", 3, 515, 4), V("IOTA", 0, 128), col(0), A.is_equal)
     unit("QE")
     for h in range(2):
         ts(V("ST", h, 4, 2), V("IOTA", 0, 32, 16), col(1), ADD)
         for k in range(2):
-            ts(V("ST", 48 + 12 * k + h, 60 + 12 * k, 2), V("IOTA", 0, M, 16), col(9 if k else 1), ADD)
+            ts(V("ST", 32 + 12 * k + h, 44 + 12 * k, 2), V("IOTA", 0, M, 16), col(9 if k else 1), ADD)
     ts(V("ST", 16, 24), V("IOTA", 0, 8), 0.0, MUL, col(1), ADD)
-    copy(V("ST", 32, 40), V("IOTA", 0, 8))
     lin(V("CC", 5, 7), V("CC", 0, 2), -1.0, 0.0)
-    lin(V("IOTA", 577, 1154), V("IOTA", 0, 577), 1.0, 577.0)
-    lin(V("IOTA", 1154, 1731), V("IOTA", 0, 577), 1.0, 1154.0)
+    lin(V("IOTA", 288, 576), V("IOTA", 0, 288), 1.0, 288.0)
+    for a in (576, 1152, 1728):
+        lin(V("IOTA", a, a + 576), V("IOTA", 0, 576), 1.0, float(a))
+    lin(V("IOTA", 2304, 2308), V("IOTA", 0, 4), 1.0, 2304.0)
 
-    quant("QS", M, C, V("TXN"))
+    quant("QS", 0, C, V("TXN"))
     for b in range(4):
-        mm(bank("PA", b, C), "QE", 128 * b, "QS", M, C)
+        mm(bank("PA", b, C), "QE", 128 * b, "QS", 0, C)
+    ts(V("POSS"), V("LVT"), 0.0, A.is_equal)
+    send_small("p")
+    iota(V("KEYC"), [[1, 8], [0, 16]], ROUND, 0)
+    iota(V("CJ"), [[-C, N - 1], [0, 2]], C * (N - 2) - 1, 0)
+    iota(V("R18"), [[0, 7], [1024, 18]], 0, 0)
     for l in range(3):
         ts(V("MK", 32 * l, 32 * l + 18), V("LVT"), float(l), A.is_equal)
     for b in range(4):
-        act(V("X0", b, 4 * C, 4), bank("PA", b, C))
+        copy(V("X0", C * b, C * b + C), bank("PA", b, C))
     act(V("JT"), V("J16"), ACT.Abs, bias=col(6))
     act(V("DIAG"), V("JT"), ACT.Relu, bias=1.0, scale=-1.0)
+    lin(V("DD"), V("DIAG"), -17 * STEP, STEP)
     act(V("RESET"), V("J16"), ACT.Sign)
-    for l in range(3):
-        mk = V("MK", 32 * l, 32 * l + 18)
-        scan(V("CS", 32 * l, 32 * l + 18), mk, mk, 0.0, ADD, A.max)
+    scan(V("CS"), V("R32"), V("MK"), 0.0, A.min, ADD)
     tr(V("CT"), V("CS"))
     scan(V("CU", 1, 96), V("CT", 0, 95), V("RESET", 1, 96), 0.0, ADD, MUL)
     tr(V("CV"), V("CU"))
     lin(V("NM"), V("MK"), 1000.0, -1000.0)
     tt(V("CW", 0, 82), V("CS", 0, 82), V("NM", 0, 82), ADD)
     for l in range(3):
-        ts(V("CT", 32 * l, 32 * l + 18), V("CW", 32 * l, 32 * l + 18), V("CV", 32 * l + 17, 32 * l + 18), ADD, float(M * l), ADD)
+        ts(V("C3", l, 54, 3), V("CW", 32 * l, 32 * l + 18), V("CV", 32 * l + 17, 32 * l + 18), ADD, float(M * l), ADD)
+    scan(V("PS"), V("R3"), V("C3"), 0.0, A.min, A.max)
+    posw = V("PS", 2, 54, 3)
+    ts(V("POSU"), posw, -1.0, ADD)
     ts(V("t1"), V("PR"), -float(C * (r + 1)), ADD)
     ts(V("t3"), V("PR"), 0.0, A.is_lt, float(C * (r + 1) + 1), MUL)
     ts(V("t2"), V("t1"), 0.0, A.is_lt, float(N * C), MUL)
     tt(V("t4"), V("t1"), V("t3"), ADD)
-    tt(V("TA", 0, 18), V("CT", 0, 18), V("CT", 32, 50), A.max)
     tt(V("t1"), V("t4"), V("t2"), ADD)
-    tt(V("POSW"), V("TA", 0, 18), V("CT", 64, 82), A.max)
-    ts(V("POSS"), V("POSW"), float(M * r - 1), ADD)
-    ts(V("POSU"), V("POSW"), -1.0, ADD)
-    quant("QX0", 0, C, V("X0"))
-    send_small("p")
     copy(V("CODE"), V("t1"))
-    for b in range(4):
-        mm(bank("PB", b, C), "QW", 128 * b, "QX0", 0, C)
-    for b in range(4):
-        act(V("TY0", b, 4 * C, 4), bank("PB", b, C), scale=0.03125)
-    dma("s", V("PPU", 126, 144), V("POSS"), 5.0)
     scatter(V("INVF"), V("POSU"), V("IOTA", 0, C))
-    fold(V("SCI", 0, M), V("INVF", 0, M), M)
-    copy(V("INV0"), V("SCI", 15, M, 16))
-    quant("QY0", 0, C, V("TY0"))
-    pick("QS", 0, "QY0", C, V("INV0"), M)
-    send_big(1)
+    ts(V("INV0"), fold(V("INVF", 0, M), M), col(10), ADD)
 
-    def codes(l):
-        fold(V("NW%d" % l), ind(V("PF"), V("PFO", 12 * (l - 1), 12 * l)), 2 * M)
-
-    def lists(l):
-        use[0] = ""
-        nw, off, tl = V("NW%d" % l, 15, 2 * M, 16), "OFF%d" % l, "TL%d" % l
-        ts(V("t2", 0, 12), nw, float(N * C - 1), A.min, -143.5, ADD)
-        ts(V("TW", 0, 12), V("t2", 0, 12), 1.0 / C, MUL, float(ROUND), ADD)
-        tt(V("L2", 0, 128), ind(V("TW"), V("KOFF")), V("KEYC"), A.is_equal)
-        scan(V("L3", 0, 128), V("RESET", 0, 128), V("L2", 0, 128), 0.0, MUL, ADD)
-        copy(V("TT", 0, 8), V("L3", 15, 128, 16))
-        tr(V("TA"), V("TT"))
-        tt(V("NV"), ind(V("PF"), V("PFO", 12 * (l - 1), 12 * l)), V("E4096"), ADD)
-        scan(V("TB", 1, 32), V("TA", 0, 31), V("RESET", 1, 32), 0.0, ADD, MUL)
-        tr(V("TC"), V("TB"))
-        tt(V("t2", 0, 8), V("TC", 0, 8), V("CB"), ADD)
-        tt(V("L1", 0, 128), ind(V("t2", 0, 8), V("SEGO")), V("L3", 0, 128), ADD)
-        tt(V("L3", 128, 256), V("L1", 0, 128), V("L2", 0, 128), MUL)
-        tt(V("L1", 128, 192), V("L3", 128, 192), V("L3", 192, 256), ADD)
-        tt(V("L1", 192, 224), V("L1", 128, 160), V("L1", 160, 192), ADD)
-        tt(V(off), V("L1", 192, 208), V("L1", 208, 224), ADD)
-        copy(V("OFU"), V(off, 0, 12))
-        scatter(V(tl), V("OFU"), V("NV"))
-        fold(V("L2", 0, K), V(tl, 0, K), K)
-        copy(V("WL%d" % l, 0, 14), V("L2", 15, K, 16))
-        send_small("l%d" % l)
-
-    act(V("PF"), ind(V("IOTA"), V("CODE")))
-    lin(V("CB"), V("IOTA", 0, 8), float(CAP), -1.0)
-    fill("TW", 12, 16, 0)
-    fill("TT", 0, 32, 0)
-    fill("TB", 0, 1, 0)
-    for k in range(2):
-        lin(V("E4096", M * k, M * k + M), V("IOTA", 128 * k, 128 * k + M), 4096.0, 0.0)
-    fill("TL2", 0, K, EMPTY)
-    fill("WL2", 14, 16, 0)
-    lin(col(8), col(2), 0.5, 0.0)
-    lin(col(7), col(2), -0.5, 0.5)
-    ts(V("ET", 3, 515, 4), V("IOTA", 0, 128), col(0), A.is_equal, col(7), MUL)
-    fold(V("SCI", M, C), V("INVF", M, C), 2 * M)
-    copy(V("AU", 0, 176), V("ST"))
-    for l in (2, 1):
-        for k in range(2):
-            a = 12 * (l - 1) + 6 * k
-            ts(V("PFO", a, a + 6), V("SCI", M * l + 15, M * l + M, 16), float(C * k), ADD)
-    for t in range(4):
-        lin(V("OIF", 18 * t, 18 * t + 18), V("SCI", 15, C, 16), 4.0, float(t))
-    codes(2)
-    lists(2)
-    copy(V("OI"), V("OIF"))
-    unit("QH0")
-    ts(V("ET", 3, 515, 4), V("IOTA", 0, 128), col(0), A.is_equal, col(8), MUL)
-    act(V("POSF", 1, C + 1), ind(V("IOTA", 0, C), V("POSU")))
-    fill("PP", 144, 148, N * M)
-    fill("POSF", 0, 1, 2 * M)
-    fill("POSF", C + 1, C + 2, 2 * M)
-    for t in range(2):
-        act(V("DS", 192 * t, 192 * t + 192), ind(V("X0"), V("OI", 18 * t + 6, 18 * t + 18)))
-    codes(1)
-    use[0] = "b"
-    for h in range(2):
-        copy(V("i1", h, 24, 2), V("NW1", 15, 2 * M, 16))
-    ts(V("i2", 0, 24), V("i1", 0, 24), 15, A.bitwise_and)
-    ts(V("i3", 0, 24), V("i1", 0, 24), 4, A.logical_shift_right)
-    copy(V("LO2"), V("i2", 0, 24))
-    copy(V("HI2"), V("i3", 0, 24))
-    act(V("MKL"), ind(V("DIAG", 0, 16), V("LO2")))
-    unit("QH1")
-    pick("WF1", M * r, "QY0", C, V("INV0"), M)
-    for t in range(2, 4):
-        act(V("DS", 192 * t, 192 * t + 192), ind(V("X0"), V("OI", 18 * t + 6, 18 * t + 18)))
-    for t in range(4):
-        act(V("TYS", t, 4 * M, 4), ind(V("TY0"), V("OI", 18 * t, 18 * t + 6)))
-    copy(V("PP", 0, 144), V("PPU"))
-    tt(V("L2"), ind(V("PP"), V("HI2")), V("MKL"), MUL)
-    tr(V("L3"), V("L2"))
-    for h in range(2):
-        scan(V("L1", 192 * h, 192 * h + 192), V("RESET", 0, 192), V("L3", 192 * h, 192 * h + 192), 0.0, MUL, ADD)
-    for h in range(2):
-        copy(V("OF1", 16 * h, 16 * h + 12), V("L1", 16 * h + 15, 384, 32))
-
-    def gather_sum(p, win, wn, of, second, d, between=None):
-        pick(p, 0, win, wn, V(of, 0, 12), 2 * M)
-        pick(p, 2 * M, win, wn, V(of, second, second + 14), K)
-        for b in range(4):
-            mm(bank("PA", b, 128), "QH0", 128 * b, p, 0, 128, start=True, stop=False)
-        for b in range(4):
-            for i in range(1, 4):
-                mm(bank("PA", b, 128), "QH%d" % (i // 2), 128 * b, p, M * i, 128, start=False, stop=i == 3)
-        if between: between()
-        for b in range(4):
-            tt(V("TX", b, 4 * M, 4), d(b), bank("PA", b, M), A.subtract)
-
-    def layer(w, tile, a, between=None):
+    def layer(w, out, between=None):
         quant("QX", 0, 128, V("TX"))
         for b in range(4):
             mm(bank("PB", b, 128), w, 128 * b, "QX", 0, 128)
         if between: between()
         for b in range(4):
-            act(V(tile, a + b, a + 4 * M, 4), bank("PB", b, M), scale=0.03125)
+            act(out(b), bank("PB", b, M), scale=0.03125)
 
-    def compose(k, tile, off):
-        for t in range(4):
-            act(V("SG", t, 4 * K, 4), ind(V(tile), V(off, 14 * t, 14 * t + 14)))
-        quant("S%d" % k, 0, 256, V("SG"))
-        send_big(k)
+    for t in range(4):
+        act(V("TX", t, 4 * M, 4), ind(V("X0", C * t, C * t + C), V("INV0")))
+    layer("QW", lambda b: V("TYS", b, 4 * M, 4))
+    quant("QS", Y0, 128, V("TYS", 0, 512))
+    send_whole()
+    dma("s", u8(V("WF1c", OWN, OWN + 128)), u8(V("QSc", Y0, Y0 + 128)))
+    dma("s", V("WF1s", OWN, OWN + 128), V("QSs", Y0, Y0 + 128))
+    dma("s", V("QVs"), (T.vs[:], V("WF1c", 0, OWN)[1]))
+    dma("s", u8(V("QVc")), ext(T.vc[:]))
+    dma("s", V("TU"), ext(T.u[:]))
+
+    def codes(l):
+        tt(V("NV%d" % l), ind(V("PF"), V("PFO", 12 * (l - 1), 12 * l)), V("E4096"), ADD)
+        tt(V("NW%d" % l), fold(V("NV%d" % l), 2 * M), V("ETAB"), A.subtract)
+
+    def lists(l):
+        use[0] = ""
+        off, tl = "OFF%d" % l, "TL%d" % l
+        ts(V("t2", 0, 12), V("NW%d" % l), float(N * C - 1), A.min, -143.5, ADD)
+        ts(V("TW", 1, 13), V("t2", 0, 12), 1.0 / C, MUL, float(ROUND), ADD)
+        tt(V("L2", 0, 128), ind(V("TW"), V("KOFF")), V("KEYC"), A.is_equal)
+        scan(V("L3", 0, 128), V("RESET", 0, 128), V("L2", 0, 128), 0.0, MUL, ADD)
+        copy(V("TT", 0, 8), V("L3", 15, 128, 16))
+        tr(V("TA"), V("TT"))
+        scan(V("TB", 1, 32), V("TA", 0, 31), V("RESET", 1, 32), 0.0, ADD, MUL)
+        tr(V("TC"), V("TB"))
+        tt(V("L2", 0, 128, 16), V("TC", 0, 8), V("CB"), ADD)
+        scan(V("L1", 0, 128), V("RESET", 0, 128), V("L2", 0, 128), 0.0, MUL, ADD)
+        tt(V("L3", 128, 256), V("L1", 0, 128), V("L2", 0, 128), MUL)
+        tt(V("L1", 128, 192), V("L3", 128, 192), V("L3", 192, 256), ADD)
+        tt(V("L1", 192, 224), V("L1", 128, 160), V("L1", 160, 192), ADD)
+        tt(V(off), V("L1", 192, 208), V("L1", 208, 224), ADD)
+        copy(V("OFU"), V(off, 1, 13))
+        scatter(V(tl), V("OFU"), V("NV%d" % l))
+        ts(V("WL%d" % l, 0, 14), fold(V(tl, 0, K), K), col(10), ADD)
+        send_small("l%d" % l)
+
+    copy(V("PF"), ind(V("IOTA"), V("CODE")))
+    lin(V("CB"), V("IOTA", 0, 8), float(CAP), -1.0)
+    fill("TW", 0, 16, 0)
+    fill("TT", 0, 32, 0)
+    fill("TB", 0, 1, 0)
+    fill("T7", 0, 32, 0)
+    fill("V7", 0, 1, 0)
+    lin(V("B7"), V("IOTA", 0, 7), float(M), 0.0)
+    for k in range(2):
+        lin(V("E4096", M * k, M * k + M), V("IOTA", 128 * k, 128 * k + M), 4096.0, 0.0)
+    ts(V("ETAB"), V("E4096", 0, 2 * M, 16), col(11), ADD)
+    fill("TL2", 0, K, EMPTY)
+    fill("WL2", 14, 16, 0)
+    lin(col(8), col(2), 0.5, 0.0)
+    lin(col(7), col(2), -0.5, 0.5)
+    ts(V("ET", 3, 515, 4), V("IOTA", 0, 128), col(0), A.is_equal, col(7), MUL)
+    scan(V("SCI"), V("DD", 0, 2 * M), V("INVF", M, C), 0.0, ADD, A.max)
+    inv = lambda a, b: V("SCI", a + 15, b, 16)
+    copy(V("AU", 0, 160), V("ST"))
+    for l in (2, 1):
+        for k in range(2):
+            a = 12 * (l - 1) + 6 * k
+            ts(V("PFO", a, a + 6), inv(M * l - M, M * l), col(10), ADD, float(C * k), ADD)
+    ts(V("INV12"), inv(0, 2 * M), col(10), ADD)
+    codes(2)
+    lists(2)
+    unit("QH0")
+    ts(V("ET", 3, 515, 4), V("IOTA", 0, 128), col(0), A.is_equal, col(8), MUL)
+    copy(V("POSF", 1, C + 1), ind(V("IOTA", 0, C), V("POSU")))
+    fill("PP", 144, 148, N * M + 1)
+    ts(V("PP", 126, 144), posw, float(OWN), ADD)
+    fill("POSF", 0, C + 2, 2 * M, C + 1)
+    for t in range(4):
+        copy(V("DS", 192 * t, 192 * t + 192), ind(V("X0", C * t, C * t + C), V("INV12")))
+    codes(1)
+    use[0] = "b"
+    for h in range(2):
+        copy(V("i1", h, 12, 2), V("NW1", 6 * h, 6 * h + 6))
+    ts(V("i2", 0, 12), V("i1", 0, 12), 15, A.bitwise_and)
+    ts(V("i3", 0, 12), V("i1", 0, 12), 4, A.logical_shift_right)
+    copy(V("LO2"), V("i2", 0, 12))
+    copy(V("HI2"), V("i3", 0, 12))
+    copy(V("MKL"), ind(V("DIAG", 0, 16), V("LO2")))
+    unit("QH1")
+    for t in range(4):
+        copy(V("YP", YW * t, YW * t + M), V("TYS", t, 4 * M, 4))
+    fill("YP", 2 * M, 4 * YW, 0, YW)
+    fill("ZP", M, 4 * ZW, 0, ZW)
+    copy(V("MP"), V("PPU", 0, 126))
+    scan(V("PP", 0, 126), V("R18"), V("MP"), 0.0, A.min, ADD)
+    copy(V("T7", 0, 7), V("PP", 17, 126, 18))
+    tr(V("U7"), V("T7"))
+    tt(V("MP", 0, 126, 18), V("MP", 0, 126, 18), V("B7"), ADD)
+    scan(V("V7", 1, 32), V("U7", 0, 31), V("RESET", 1, 32), 0.0, ADD, MUL)
+    tr(V("W7"), V("V7"))
+    tt(V("MP", 0, 126, 18), V("MP", 0, 126, 18), V("W7", 0, 7), ADD)
+    scan(V("PP", 0, 126), V("R18"), V("MP"), 0.0, A.min, ADD)
+    tt(V("L2", 0, 192), ind(V("PP"), V("HI2")), V("MKL"), MUL)
+    tr(V("L3", 0, 192), V("L2", 0, 192))
+    scan(V("L1", 0, 192), V("RESET", 0, 192), V("L3", 0, 192), 0.0, MUL, ADD)
+    copy(V("T7", 0, 12), V("L1", 15, 192, 16))
+    tr(V("U7"), V("T7"))
+    copy(V("L2", 192, 256), ind(V("U7"), V("DUPO")))
+    for k in range(2):
+        tr(V("L3", 192 + 12 * k, 224 + 12 * k), V("L2", 192 + 32 * k, 224 + 32 * k))
+    for h in range(2):
+        ts(V("OF1", 16 * h, 16 * h + 12), V("L3", 192 + h, 216, 2), -1.0, ADD)
+
+    def gather_sum(p, win, wn, of, second, d, between=None):
+        pick(p, 3 * M, win, wn, V(of, second + 6, second + 14), 128)
+        pick(p, 2 * M, win, wn, V(of, second, second + 6), M)
+        pick(p, 0, win, wn, V(of, 0, 12), 2 * M)
+        for i in (3, 2):
+            for b in range(4):
+                mm(bank("PA", b, 128), "QH1", 128 * b, p, M * i, 128, start=i == 3, stop=False)
+        for b in range(4):
+            for i in (1, 0):
+                mm(bank("PA", b, 128), "QH0", 128 * b, p, M * i, 128, start=False, stop=i == 0)
+        if between: between()
+        for b in range(4):
+            tt(V("TX", b, 4 * M, 4), d(b), bank("PA", b, M), A.subtract)
+
+    def compose(k, plane, off):
+        for h in range(2):
+            for t in range(4):
+                act(V("SG", 512 * h + t, 4 * K if h else 512, 4), ind(plane(t), V(off, 8 * h, 14 if h else 8)))
+            quant("QS", HALF + 128 * (2 * (k - 2) + h), 128, V("SG", 512 * h, 512 * h + 512))
+            send_half(k, h)
 
     def arrived(l):
         use[0] = "c"
@@ -567,25 +564,20 @@ def rank_program(g, core, T, topo):
         ts(V("i2", 0, 14), V("i1", 0, 14), 4095, A.bitwise_and)
         tt(V("t2", 0, 14), V("i2", 0, 14), V("CJ"), A.subtract)
         ts(V("JU"), V("t2", 0, 14), float(C + 1), A.min)
-        fold(V("L2", 0, K), ind(V("POSF", 0, C + 2), V("JU")), K)
-
-    def keep(l):
-        use[0] = "c"
-        copy(V("PC%d" % l, 0, 14), V("L2", 15, K, 16))
+        got = fold(ind(V("POSF", 0, C + 2), V("JU")), K)
+        if l == 2: ts(V("G2"), got, col(10), ADD)
+        ts(V("PC%d" % l, 0, 14), got, col(10), ADD)
         ts(V("KC%d" % l, 0, 14), V("LL%d" % l), 4096.0 * 128, A.is_ge, float(2 * M), MUL)
 
     def own(l):
-        use[0] = "b"
-        ts(V("JO"), V("NW%d" % l, 15, 2 * M, 16), -float(C * (N - 1) - 1), ADD)
-        fold(V("L2", 0, 2 * M), ind(V("POSF", 0, C + 2), V("JO")), 2 * M)
-        copy(V("PC%d" % l, 14, 26), V("L2", 15, 2 * M, 16))
+        ts(V("JO"), V("NW%d" % l), -float(C * (N - 1) - 1), ADD)
+        ts(V("PC%d" % l, 14, 26), fold(ind(V("POSF", 0, C + 2), V("JO")), 2 * M), col(10), ADD)
 
     def back_send(l, out):
         use[0] = "d"
         copy(V("i1", 0, 14), V("WL%d" % l, 0, 14))
         ts(V("i2", 0, 14), V("i1", 0, 14), 12, A.logical_shift_right, 127, A.bitwise_and)
-        for t in range(4):
-            ts(V(out, 14 * t, 14 * t + 14), V("i2", 0, 14), 4.0, MUL, float(t), ADD)
+        copy(V(out), V("i2", 0, 14))
 
     def successors(l):
         use[0] = "d"
@@ -596,7 +588,7 @@ def rank_program(g, core, T, topo):
         tt(V("t1", 0, 26), V("t3", 0, 26), V("t4", 0, 26), ADD)
         copy(V("SUO"), V("t1", 0, 26))
         scatter(V("SU"), V("SUO"), V("VAL%d" % l))
-        act(V("SD"), ind(V("SU", M * (l - 1), 4 * M), V("DBL")))
+        copy(V("SD"), ind(V("SU", M * (l - 1), 4 * M), V("DBL")))
 
     def successors_end(of):
         use[0] = "d"
@@ -606,22 +598,29 @@ def rank_program(g, core, T, topo):
 
     def places():
         use[0] = "c"
-        ts(V("t1", 0, 18), V("POSW"), M + 0.5, A.is_ge, -float(K), MUL)
-        ts(V("t2", 0, 18), V("POSW"), 2 * M + 0.5, A.is_ge, -float(2 * K), MUL)
-        tt(V("t3", 0, 18), V("t1", 0, 18), V("POSW"), ADD)
+        ts(V("t1", 0, 18), posw, M + 0.5, A.is_ge, -float(K), MUL)
+        ts(V("t2", 0, 18), posw, 2 * M + 0.5, A.is_ge, -float(2 * K), MUL)
+        tt(V("t3", 0, 18), V("t1", 0, 18), posw, ADD)
         tt(V("t4", 0, 18), V("t3", 0, 18), V("t2", 0, 18), ADD)
         ts(V("POSZ"), V("t4", 0, 18), float(2 * K + 255), ADD)
 
-    def asked():
-        fill("TYS", 8 * M, 896, 0)
-        fill("SG", 4 * K, 1024, 0)
-        arrived(2)
-        for t in range(4):
-            ts(V("G2", 14 * t, 14 * t + 14), V("L2", 15, K, 16), 4.0, MUL, float(t), ADD)
+    yplane = lambda t: V("YP", YW * t, YW * t + 2 * M + 1)
+    zplane = lambda t: V("ZP", ZW * t, ZW * t + M + 1)
+    znew = lambda b: V("ZP", ZW * b, ZW * b + M)
 
-    gather_sum("P1", "WF1", 896, "OF1", 16, lambda b: V("DS", 192 * b, 192 * b + M), asked)
-    layer("QW", "TYS", 4 * M, lambda: keep(2))
-    compose(2, "TYS", "G2")
+    def ztile(at):
+        for b in range(4):
+            copy(V("TZ", b, 4 * M, 4), znew(b))
+        quant("WB", at, 128, V("TZ"))
+
+    fill("TYS", 8 * M, 896, 0)
+    fill("SG", 4 * K, 1024, 0)
+    arrived(2)
+    gather_sum("P1", "WF1", OWN + 128, "OF1", 16, lambda b: V("DS", 192 * b, 192 * b + M))
+    layer("QW", lambda b: V("YP", YW * b + M, YW * b + 2 * M))
+    compose(2, yplane, "G2")
+    for b in range(4):
+        copy(V("TYS", 4 * M + b, 8 * M, 4), V("YP", YW * b + M, YW * b + 2 * M))
     fill("W32", 0, 32, 0)
     lin(V("IDXC"), V("IOTA", 0, 416, 16), 1.0, col(1))
     lin(V("IDXC", 14, 20), V("IDXC", 14, 20), 1.0, float(2 * M))
@@ -636,15 +635,15 @@ def rank_program(g, core, T, topo):
         mm(bank("PA", b, 2 * M), "QE", 128 * b, "WF2", K, 2 * M)
     for b in range(4):
         act(V("DY", 192 * b, 192 * b + 192), bank("PA", b, 2 * M))
-    for n in ("TY2", "TZ2", "TZ1", "TZ0"):
-        fill(n, 4 * M, 512, 0)
+    fill("TZ", 4 * M, 512, 0)
     fill("TL1", 0, K, EMPTY)
     fill("WL1", 14, 16, 0)
     lin(V("VAL1"), V("VAL2"), 1.0, float(K + 128))
     own(2)
-    ts(V("t1", 0, 12), V("OFF2", 0, 12), float(K), A.is_ge, 1000.0, MUL)
+    use[0] = "b"
+    ts(V("t1", 0, 12), V("OFF2", 1, 13), float(K), A.is_ge, 1000.0, MUL)
     ts(V("t2", 0, 12), V("PC2", 14, 26), float(K), ADD)
-    tt(V("t3", 0, 12), V("t1", 0, 12), V("OFF2", 0, 12), ADD)
+    tt(V("t3", 0, 12), V("t1", 0, 12), V("OFF2", 1, 13), ADD)
     tt(V("W32", 0, 12), V("t3", 0, 12), V("t2", 0, 12), A.min)
     tr(V("D1"), V("W32"))
     copy(V("D2"), ind(V("D1"), V("DUPO")))
@@ -653,36 +652,40 @@ def rank_program(g, core, T, topo):
     successors(2)
 
     gather_sum("P2", "WF2", 448, "OF2", 32, lambda b: V("DS", 192 * b + M, 192 * b + 2 * M), lambda: (back_send(2, "G3"), successors_end("OF3")))
-    layer("QW", "TY2", 0, lambda: quant("QU", 0, 128, V("TU")))
-    quant("QY2", 0, 128, V("TY2"))
+    layer("QW", lambda b: V("TZ", b, 4 * M, 4), lambda: quant("QU", 0, 128, V("TU")))
+    quant("QY2", 0, 128, V("TZ"))
     for b in range(4):
         mm(bank("PA", b, 128), "QE", 128 * b, "QY2", 0, 128)
     for b in range(4):
         act(V("TX", b, 4 * M, 4), bank("PA", b, M))
-    layer("QV", "TZ2", 0)
-    compose(3, "TZ2", "G3")
+    layer("QV", znew)
+    compose(3, zplane, "G3")
+    ztile(K)
     lists(1)
-    quant("WB", K, 128, V("TZ2"))
 
     gather_sum("P3", "WB", K + 128, "OF3", 16, lambda b: V("DY", 192 * b + M, 192 * b + 2 * M), lambda: (back_send(1, "G4"), own(1)))
-    layer("QV", "TZ1", 0)
-    compose(4, "TZ1", "G4")
+    layer("QV", znew)
+    compose(4, zplane, "G4")
+    ztile(2 * K + 128)
     arrived(1)
-    keep(1)
     successors(1)
-    quant("WB", 2 * K + 128, 128, V("TZ1"))
     successors_end("OF4")
 
     gather_sum("P4", "WB", 2 * K + 256, "OF4", 16, lambda b: V("DY", 192 * b, 192 * b + M), places)
-    layer("QV", "TZ0", 0)
-    quant("WB", 2 * K + 256, 128, V("TZ0"))
-    pick("QO", 0, "WB", 832, V("POSZ"), C)
-    mm(bank("PA", 0, C), "QU", 0, "QO", 0, C)
+    layer("QV", lambda b: V("TZ", b, 4 * M, 4))
+    quant("WB", 2 * K + 256, 128, V("TZ"))
+    runs = [(0, 160), (160, C)]
+    for a, b in runs:
+        pick("QO", a, "WB", 832, V("POSZ", a // 16, b // 16), b - a)
+    for i, (a, b) in enumerate(runs):
+        mm(bank("PA", i, b - a), "QU", 0, "QO", a, b - a)
     dma("s", ext(T.oc[:]), u8(V("QOc")))
-    for k in range(4):
-        dma("a" if k else "s", ext(T.osc[4 * k:4 * k + 4, :]), (T.QOs[32 * k:32 * k + 4, :], V("QOs")[1]))
-    copy(V("YO"), bank("PA", 0, C))
+    dma("s", ext(T.osc[0:4, :]), (T.QOs[0:4, :], V("QOs")[1]))
+    for i, (a, b) in enumerate(runs):
+        copy(V("YO", a, b), bank("PA", i, b - a))
     dma("s", ext(T.y[:]), V("YO"))
+    for k in range(1, 4):
+        dma("a", ext(T.osc[4 * k:4 * k + 4, :]), (T.QOs[32 * k:32 * k + 4, :], V("QOs")[1]))
     schedule()
     g.wait_ge(T.sem.ls, count["ls"])
     for s in sorted(final):

@@ -4,45 +4,44 @@ from concourse.mybir import dt, AluOpType, ActivationFunctionType
 N, C, M, CAP = 8, 288, 96, 32
 K = (N - 1) * CAP
 F, B, I, U, X4, SC = "float32", "bfloat16", "int32", "uint16", "float8_e4m3fn_x4", "uint8"
-ROUND = 12582912
-EMPTY = 4095 + 4096 * (128 + M)
+KS = C + 2
 STEP = float(1 << 20)
 Y0, HALF = C, C + 128
 OWN = (N - 1) * M
 YW, ZW = 208, 112
 
-PACK_U = "DUPO KOFF DBL OF1 OF3 OF4 CODE POSU POSZ INV0 INV12 PFO OFU HI2 LO2 JU JO SUO OF2 G2 G3 G4".split()
-PACK_F = ("t1 t2 t3 t4 TA TB TC TT TW D1 D2 D3 W32 OFF1 OFF2 PC1 PC2 KC1 KC2 CB CJ IDXC ETAB NW1 NW2 MK CS NM CT CU CV CW "
-          "C3 PS R3 R32 R18 MP T7 U7 V7 W7 B7").split()
+PACK_U = "DB2 DBL WL2 OF1 OF3 OF4 WL1 CODE POSU POSZ INV0 INV12 OFU1 OFU2 HI2 LO2 JO SUO OF2 G2 G3 G4".split()
+PACK_F = "t1 t2 t3 t4 D1 D2 D3 W32 OFF2 PC1 PC2 KC1 KC2 CJ IDXC ETAB NW1 NW2 MK CS NM CT CU CV CW C3 PS R3 R32".split()
 PLACE = {}
 TEMPS = "t1 t2 t3 t4 i1 i2 i3 L1 L2 L3".split()
-LAID = "010a0I1g0O1m221W0U281E1sb80m0d2w3G1L0s10fubD2f0y3i3p162UazbP0E612I1c2C6j3A2O3vk32k36qfbI3d67313N1z6d4K455k5q5w4SbUqw6o7y7s3T6M6ubkqC1Q6A6S3Z6G7Ec67K6Y747ajW4a7g7Q7mfp7W4g824pat4v4B4H51542r5C5Pr15ac05gaR88bf5U5Jccci8ebqcocG8D8x8lcM8rf6cSqPaEr7cucY8Igad5ql8R8Xda939d99gg9j9pdg9vfH9AaLdncAb3gmeU9Ia2fZdsgsa8f0fTC29OdyfcssC9dEs5gyfi9Xbxi1szaXqJi6dKgEgKicdQhqijshfBdWhkGoe2ioGviugQe8iACehPqVeeiGh8hDgWekiMsEeqsLh3g5sQiSsXewqriYeDCkeKj4CreTjaNQCwjgt2jmCCwqt8jtO2tejyCItlwwjEhJCOwCaejQhVjKheakl7l0aqljlclDlvlolJlPlVCUhxm1fNm7mdmjmpk8kUmvmBkemHD0mNmTkkmZnen5kqn8nkkxnqtqnwD6kCnFnLDcnRo1nXkIkPDio7octwoptCoioAovGAoHtItOpnoMp5tUpgpboUpWpRq8q3u0psp0DorcpAu6rlrrpGrxrHrDsbpPrZDurNsnrTudupuiuuuBuVuGuNv1v7wIvdvjvpvvDAvBvHvNvTvZw5wbx6whx0wnxcwOxixoDGxxG6xDxJxZGcxPy4yaxSyhymwUyvyByHyQyNyWGiz3z9zeznztzzzJzFzOzUA0AdA6ApAiANAZAuASB5ACBEBRBKBaAIByBWBiGGBoBxDODXE5DYEaEhEBEmEtEHENJYETEZF5K4FbFhKaFnFtKgFzFFKnFLFRGSFXGMG3GYH4HaKsHjNWHpKEHvKzHEHBO8HLKKHRKQI2HXI9IeIlKWIJIqJ1L2IOIVIyL8JvJGJNJ6JBIELeJeJkJtOeLlLqJSLCLILPLwM1LUMlMdM6MrMxMDMJMPMVN1N7NdNjNpOkNvNBOqNHNNOwOCOIOROXP3P9PjPdPoPuPAPGPNPSPZQ7QkQRQdQqQtQyQLQIQX"
+LAID = "1s010a0I1m0O0d0m280s221g0yaw100E2e1z4t0U361E31ph3Hip1c6d5V16aq4h4c5k5e5q617K6i3N6G3c546o676MdGb46u4n7E2q6A2D7Q3A3T746S6Y7W451WoY7a4y3Z7m7g2k4Z827u3uaF88op4Tdz2V5Jaz3i3obk4H8e4N5O5x8k2wps5C8JaS8rbw8CbD8wbIexaYer8OdKc7bO9f2PoOaK992Ic1eC93ok8X9BbU1S9u9o9jeI1MqIdRccov9GqPeOcico9Oa8aebqqxb8f0uNcuEc58beLIcBeUfoEyqU9UfigWABcGpAe9fcoHcMAvel7DpccShrf6hDr6hlcYfBfwhPEFhwhehIrcdXd4hUqEgLgFr1oTroLCdarji0efe3dgfGi6doiwfSfYiiicg4fMa3akj4jbdxjgjngajTjHjzjZjsjNgRgsiBk5kbgmknkhggkRh3gykXrukFAGkLloktlikzrAiYl3l9rHlcANluiGlAlJrMiTEKiMlPrYASlVm4m1mbs4rSmgmnmymtmEmLsanUnfAYocmQo7sgo1nknrmYpEn9n4smB5nwpTssq5nEpZqfpNqlnKqrBah9wkBgnTq9sLsEsQsXBmtht2t9tttntLoBBstztXsztFufulu3u9uDvytRvsuJuruxvKvEvQByvZvaw5whwrwbwIwxwCwOuSx3xfx9xpwXxBxvvgxjxGuYvmxVxPy7v4ygy1ybysyFymyyyRyKzlzqzfyWp5zwERA1z4AiBEAdzCA6zaBKEgzKzQBSEmpoLOAozZC9C2CeClCqCXCxCLCFEsCRDlD9D3DfC1DPI9E1E7DrDVFeDxIqDDF8DJEWF2IeFkLUIlFtFLIwICFFFOFzG7IIG0GSFVGvGcGjGoGYHbIOH5GAHFHQHLGIIUHWHgJ0GOHoHuI2J6M0JcHDJoJiJBJuJNJGKpJZK7JSKjKdKHKvKBKNLtLzKTLhMoLnKZMiM6L5LbMcMuMJMPMVN4MDNaNhMYNmNzNsNLNENTO6NZOJOcOeOkOxODOu"
 LETTERS = "0123456789abcdefghijklmnopqrstuvwxyzABCDEFGHIJKLMNOPQRSTUVWXYZ"
 
 
 def _scratch():
     s = {}
     for n, w, d in [
-        ("IOTA", 2308, F), ("PI", 4, I), ("CC", 16, F), ("J16", 224, F), ("JT", 224, F), ("DIAG", 224, B), ("RESET", 224, B), ("DD", 224, F),
-        ("KEYC", 128, F), ("CJ", 14, F), ("CB", 8, F), ("IDXC", 26, F), ("E4096", 192, F), ("ETAB", 12, F), ("VAL2", 416, F), ("VAL1", 416, F),
-        ("DUPO", 4, U), ("KOFF", 8, U), ("ST", 160, F),
+        ("IOTA", 2308, F), ("PI", 4, I), ("CC", 24, F), ("J16", 224, F), ("JT", 224, F), ("DIAG", 224, B), ("RESET", 224, B), ("RS2", 384, B), ("DD", 224, F),
+        ("CJ", 14, F), ("IDXC", 26, F), ("PLC", 192, F), ("DO", 384, B), ("ZR", 192, B), ("ETAB", 12, F), ("VAL2", 416, F), ("VAL1", 416, F),
+        ("DB2", 24, U), ("ST", 56, F),
         ("ET", 520, B), ("LVT", 18, I), ("PR", 36, I), ("CODE", 36, U), ("PF", 576, F),
         ("t1", 36, F), ("t2", 36, F), ("t3", 36, F), ("t4", 36, F), ("i1", 32, I), ("i2", 32, I), ("i3", 32, I),
         ("MK", 96, F), ("CS", 96, F), ("NM", 96, F), ("CT", 96, F), ("CU", 96, F), ("CV", 96, F), ("CW", 96, F),
         ("C3", 54, F), ("PS", 54, F), ("R3", 54, F), ("R32", 96, F),
-        ("R18", 126, F), ("MP", 126, F), ("T7", 32, F), ("U7", 32, F), ("V7", 32, F), ("W7", 32, F), ("B7", 7, F),
-        ("L1", 384, F), ("L2", 384, F), ("L3", 384, F), ("MKL", 192, B), ("SD", 384, F),
-        ("POSU", 18, U), ("POSS", 18, U), ("POSZ", 18, U), ("POSF", 292, F), ("PP", 148, F), ("PPU", 128, U),
-        ("INVF", 288, F), ("SCI", 192, F), ("INV0", 6, U), ("INV12", 12, U), ("PFO", 24, U),
-        ("NW1", 12, F), ("NW2", 12, F), ("NV1", 192, F), ("NV2", 192, F), ("TW", 16, F), ("TT", 32, F), ("TA", 32, F), ("TB", 32, F), ("TC", 32, F),
-        ("OFF1", 16, F), ("OFF2", 16, F), ("OFU", 12, U), ("TL1", 416, F), ("TL2", 416, F), ("WL1", 16, F), ("WL2", 16, F),
-        ("LL1", 14, F), ("LL2", 14, F), ("HI2", 12, U), ("LO2", 12, U), ("JU", 14, U), ("JO", 12, U),
+        ("L1", 384, F), ("L2", 384, F), ("L3", 384, F), ("MKL", 384, B), ("SD", 384, F),
+        ("POSU", 18, U), ("POSS", 18, B), ("POSZ", 18, U), ("POSF", 2 * KS, B), ("PP", 148, F), ("PPU", 128, B),
+        ("INVF", 288, F), ("SCI", 192, F), ("INV0", 8, U), ("INV12", 12, U),
+        ("NW1", 12, F), ("NW2", 12, F), ("NV1", 192, F), ("NV2", 192, F),
+        ("OFF2", 16, F), ("OFU1", 12, U), ("OFU2", 12, U), ("TL1", 416, F), ("TL2", 416, F), ("TP1", 416, F), ("TP2", 416, F),
+        ("WL1", 16, U), ("WL2", 16, U),
+        ("UA", 192, F), ("MA", 192, B), ("NA", 192, B), ("CA", 192, B), ("XA", 192, B), ("DA", 384, B), ("TA", 384, B), ("OA1", 384, F), ("OA2", 384, F),
+        ("LL1", 14, U), ("LL2", 14, U), ("HI2", 24, U), ("LO2", 24, U), ("JO", 12, U),
         ("PC1", 26, F), ("PC2", 26, F), ("KC1", 26, F), ("KC2", 26, F), ("SUO", 26, U), ("SU", 800, F),
         ("W32", 32, F), ("D1", 32, F), ("D2", 64, F), ("D3", 64, F), ("DBL", 24, U),
         ("OF1", 32, U), ("OF2", 64, U), ("OF3", 32, U), ("OF4", 32, U), ("G2", 14, U), ("G3", 14, U), ("G4", 14, U),
         ("TXN", 1152, B), ("X0", 1152, B), ("TX", 512, B), ("TYS", 896, B), ("TZ", 512, B), ("YP", 4 * YW, B), ("ZP", 4 * ZW, B),
         ("SG", 1024, B), ("DS", 768, B), ("DY", 768, B),
-        ("TU", 512, B), ("YO", 288, F), ("HP", 18, U), ("HL1", 4, F), ("HL2", 4, F),
+        ("TU", 512, B), ("YO", 288, F), ("HP", 18, B), ("HL1", 4, U), ("HL2", 4, U),
     ]:
         s[n] = ("sbuf", [128, w], d)
     for n, w in [("QE", 512), ("QH0", 512), ("QH1", 512), ("QW", 512), ("QV", 512), ("QU", 128), ("QS", HALF + 6 * 128),
@@ -73,6 +72,8 @@ BIG = {1: ("WF1", M, 0), 2: ("WF2", CAP, 0), 3: ("WB", CAP, 0), 4: ("WB", CAP, K
 SMALL = {"p": ("POSS", "HP", "PPU", 18), "l2": ("WL2", "HL2", "LL2", 2), "l1": ("WL1", "HL1", "LL1", 2)}
 ORDER = ["p", 1, "l2", 2, 3, "l1", 4]
 SCALES = [4, 5, 6, 3]
+SLOTS = {0: ("c", [0, 1]), 1: ("c", [2, 3]), 4: ("s", [0, 1]), 5: ("s", [2, 3]), 3: ("c", [6]), 6: ("s", [6])}
+LAST = (("c", 3), ("s", 6))
 
 
 def _bits(engines):
@@ -114,8 +115,10 @@ def helper_program(g, core, T, topo, r, h):
             continue
         land, w, o0 = BIG[k]
         jobs = []
-        if h <= 3: jobs.append(("c", pair(h)))
-        if h in SCALES: jobs.append(("s", pair(SCALES.index(h))))
+        if k == 1:
+            if h <= 3: jobs.append(("c", pair(h)))
+            if h in SCALES: jobs.append(("s", pair(SCALES.index(h))))
+        elif h in SLOTS: jobs.append(SLOTS[h])
         at = 0
         for kind, us in jobs:
             g.wait_ge(T.sem["h%s%d" % (kind, k)], 4 if k == 1 else 8)
@@ -125,9 +128,10 @@ def helper_program(g, core, T, topo, r, h):
                 a = 0 if k == 1 else w * (u % 2)
                 src, dst = T["H%d%s" % (k, kind)][:, a:a + w], T[land + kind][:, o:o + w]
                 if kind == "c": src, dst = src.bitcast(dt.uint8), dst.bitcast(dt.uint8)
-                ts.append(_to(topo, core, peer[u], _bits(eng[half * at:half * at + half]), T.sem["x%d" % k], src, dst))
+                n = len(eng) if k > 1 and len(us) == 1 else half
+                ts.append(_to(topo, core, peer[u], _bits(eng[n * at:n * at + n]), T.sem["x%d" % k], src, dst))
                 at += 1
-                sent += half
+                sent += n
             g.remote_dma_fused(ts, local_sem=T.sem.ls)
     g.wait_ge(T.sem.ls, sent)
 
@@ -228,14 +232,16 @@ def rank_program(g, core, T, topo):
     def memset(o, c): op("v", lambda: g.vector.memset(o[0], c), [o], [])
     def real(v): return SCRATCH[v[1][0][0]][2] in (F, B, SC)
 
-    def either(o, i, scale=None, bias=None):
+    def either(o, i, scale=None, bias=None, pat=None):
         kw = {k: raw(x) for k, x in (("scale", scale), ("bias", bias)) if x is not None}
         if scale is None and bias is None: v = lambda: g.vector.tensor_copy(o[0], i[0])
         elif bias is None: v = lambda: g.vector.tensor_scalar(o[0], i[0], raw(scale), None, MUL)
         elif scale is None: v = lambda: g.vector.tensor_scalar(o[0], i[0], raw(bias), None, ADD)
         else: v = lambda: g.vector.tensor_scalar(o[0], i[0], raw(scale), raw(bias), MUL, ADD)
         f = ACT.Copy if bias is None else ACT.Identity
-        op("av", {"a": lambda: g.scalar.activation(o[0], i[0], f, **kw), "v": v}, [o], [i, scale, bias])
+        calls = {"a": lambda: g.scalar.activation(o[0], i[0], f, **kw), "v": v}
+        if pat: calls["g"] = lambda: g.iota(o[0], pat[0], pat[1], 0, allow_small_or_imprecise_dtypes=True)
+        op("".join(calls), calls, [o], [i, scale, bias])
 
     def copy(o, i):
         if real(o) and real(i): either(o, i)
@@ -292,19 +298,21 @@ def rank_program(g, core, T, topo):
 
     peer = [T.cores[(r + 1 + u) % N] for u in range(N - 1)]
     help_ = _helpers(topo, core)
-    out_engines = len(topo.engines(core, peer[0]))
+    out = topo.engines(core, peer[0])
+    out_engines = len(out)
     u8 = lambda v: (v[0].bitcast(dt.uint8), v[1])
 
-    def hand(e, jobs):
-        reads = [j[2] for j in jobs]
-        mask = lambda h, i: _bits(topo.engines(core, help_[h])[2 * e * (i // 2):2 * e * (i // 2 + 1)][i % 2::2])
-
+    def call(transfers, reads, engines):
         def emit(_e):
             order("g", reads, [])
-            g.remote_dma_fused([_to(topo, core, help_[h], mask(h, i), T.sem[sem], src[0], dst)
-                                for i, (h, sem, src, dst) in enumerate(jobs)], local_sem=T.sem.ls)
-            count["ls"] += e * len(jobs)
+            g.remote_dma_fused(transfers, local_sem=T.sem.ls)
+            count["ls"] += engines
         later("g", emit, [], reads)
+
+    def hand(e, jobs):
+        mask = lambda h, i: _bits(topo.engines(core, help_[h])[2 * e * (i // 2):2 * e * (i // 2 + 1)][i % 2::2])
+        call([_to(topo, core, help_[h], mask(h, i), T.sem[sem], src[0], dst) for i, (h, sem, src, dst) in enumerate(jobs)],
+             [j[2] for j in jobs], e * len(jobs))
 
     def arrives(views, k, n):
         later("x", lambda _e: note([], [x for v in views for x in v[1]], ("x%s" % k, n * out_engines, {})), views, [])
@@ -322,17 +330,32 @@ def rank_program(g, core, T, topo):
 
     def send_half(k, h):
         a = HALF + 128 * (2 * (k - 2) + h)
-        hand(8, [(2 * h + i, "hc%d" % k, u8(V("QSc", a + 64 * i, a + 64 * i + 64)), T["H%dc" % k][:, 0:64].bitcast(dt.uint8)) for i in range(2)])
-        hand(8, [(SCALES[2 * h + i], "hs%d" % k, V("QSs", a + 64 * i, a + 64 * i + 64), T["H%ds" % k][:, 0:64]) for i in range(2)])
-        if h:
-            land, _w, o0 = BIG[k]
-            arrives([V(land + c, o0, o0 + K) for c in "cs"], k, N - 1)
+        land, w, o0 = BIG[k]
+        if h == 0:
+            hand(8, [(i, "hc%d" % k, u8(V("QSc", a + 64 * i, a + 64 * i + 64)), T["H%dc" % k][:, 0:64].bitcast(dt.uint8)) for i in range(2)])
+            hand(8, [(4 + i, "hs%d" % k, V("QSs", a + 64 * i, a + 64 * i + 64), T["H%ds" % k][:, 0:64]) for i in range(2)])
+            return
+        n = out_engines // 2
+        for c, hh in LAST:
+            cast = (lambda x: x.bitcast(dt.uint8)) if c == "c" else (lambda x: x)
+            src = [V("QS" + c, a + w * i, a + w * i + w) for i in range(3)]
+            rest = [e for e in topo.engines(core, help_[hh]) if e not in out]
+            moves = [_to(topo, core, peer[4 + i], _bits(out[n * i:n * i + n]), T.sem["x%d" % k], cast(src[i][0]),
+                         cast(T[land + c][:, o0 + w * (N - 6 - i):o0 + w * (N - 5 - i)])) for i in range(2)]
+            moves.append(_to(topo, core, help_[hh], _bits(rest), T.sem["h%s%d" % (c, k)], cast(src[2][0]), cast(T["H%d%s" % (k, c)][:, 0:w])))
+            call(moves, src, out_engines + len(rest))
+        arrives([V(land + c, o0, o0 + K) for c in "cs"], k, N)
 
     def scatter(win, off, val):
         op("v", lambda: g.vector.tensor_copy(win[0].indirect(off[0]), val[0]), [win], [off, val])
 
     def fill(name, a, b, c, step=1):
-        either(V(name, a, b, step), V("IOTA", 0, -(-(b - a) // step)), 0.0, float(c))
+        n = -(-(b - a) // step)
+        either(V(name, a, b, step), V("IOTA", 0, n), 0.0, float(c), None if step > 1 else ([[0, n]], int(c)))
+
+    def seq(o, step, base):
+        n = o[0].shape[1]
+        either(o, V("IOTA", 0, n), float(step), float(base), ([[step, n]], base))
 
     def lin(o, i, scale, bias):
         either(o, i, scale, bias)
@@ -367,35 +390,33 @@ def rank_program(g, core, T, topo):
     memset(V("CU", 0, 1), 0.0)
     fill("TX", 4 * M, 512, 0)
     fill("TYS", 4 * M, 512, 0)
-    fill("ST", 0, 128, 0)
-    fill("ST", 128, 160, 0)
+    iota(V("ST", 0, 32), [[16, 16], [0, 2]], 0, 0)
+    iota(V("ST", 32, 56), [[2 * M, 2], [16, 6], [0, 2]], 0, 0)
+    memset(V("AU", 64, 192), 0)
     ts(V("PI", 1, 2), V("PI", 0, 1), 15, A.bitwise_and)
     ts(V("PI", 2, 3), V("PI", 0, 1), 4, A.logical_shift_right, 1, A.bitwise_and)
     copy(V("CC", 0, 3), V("PI", 0, 3))
-    ts(col(9), col(1), float(2 * M), ADD)
     lin(col(10), col(1), STEP, -15 * STEP)
-    lin(col(11), col(1), 4096.0 - STEP, 15 * STEP)
+    lin(col(11), col(1), -float(C), -(C - 1) / 2)
+    ts(col(14), col(1), N - 1.5, A.is_lt)
+    lin(col(12), col(1), float(CAP), -float(15 * CAP + 2 * M))
+    ts(col(15), col(14), float(15 * CAP + 2 * M), MUL, col(12), ADD)
+    lin(col(16), col(2), 1024.0, 2.0 * M - 1025)
+    lin(col(17), col(2), -5120.0, 1024.0)
+    lin(col(8), col(2), 0.5, 0.0)
+    lin(col(7), col(2), -0.5, 0.5)
     ts(V("ET", 3, 515, 4), V("IOTA", 0, 128), col(0), A.is_equal)
     unit("QE")
-    for h in range(2):
-        ts(V("ST", h, 4, 2), V("IOTA", 0, 32, 16), col(1), ADD)
-        for k in range(2):
-            ts(V("ST", 32 + 12 * k + h, 44 + 12 * k, 2), V("IOTA", 0, M, 16), col(9 if k else 1), ADD)
-    ts(V("ST", 16, 24), V("IOTA", 0, 8), 0.0, MUL, col(1), ADD)
     lin(V("CC", 5, 7), V("CC", 0, 2), -1.0, 0.0)
-    lin(V("IOTA", 288, 576), V("IOTA", 0, 288), 1.0, 288.0)
-    for a in (576, 1152, 1728):
-        lin(V("IOTA", a, a + 576), V("IOTA", 0, 576), 1.0, float(a))
-    lin(V("IOTA", 2304, 2308), V("IOTA", 0, 4), 1.0, 2304.0)
+    for a in range(C, N * C, C):
+        seq(V("IOTA", a, a + C), 1, a)
+    seq(V("IOTA", N * C, N * C + 4), 1, N * C)
 
     quant("QS", 0, C, V("TXN"))
     for b in range(4):
         mm(bank("PA", b, C), "QE", 128 * b, "QS", 0, C)
-    ts(V("POSS"), V("LVT"), 0.0, A.is_equal)
-    send_small("p")
-    iota(V("KEYC"), [[1, 8], [0, 16]], ROUND, 0)
-    iota(V("CJ"), [[-C, N - 1], [0, 2]], C * (N - 2) - 1, 0)
-    iota(V("R18"), [[0, 7], [1024, 18]], 0, 0)
+    iota(V("t2b", 0, 14), [[-C, N - 1], [0, 2]], 1, 0)
+    ts(V("CJ"), V("t2b", 0, 14), col(10), ADD)
     for l in range(3):
         ts(V("MK", 32 * l, 32 * l + 18), V("LVT"), float(l), A.is_equal)
     for b in range(4):
@@ -415,25 +436,26 @@ def rank_program(g, core, T, topo):
     scan(V("PS"), V("R3"), V("C3"), 0.0, A.min, A.max)
     posw = V("PS", 2, 54, 3)
     ts(V("POSU"), posw, -1.0, ADD)
-    ts(V("t1"), V("PR"), -float(C * (r + 1)), ADD)
+    copy(V("POSS"), posw)
+    send_small("p")
     ts(V("t3"), V("PR"), 0.0, A.is_lt, float(C * (r + 1) + 1), MUL)
-    ts(V("t2"), V("t1"), 0.0, A.is_lt, float(N * C), MUL)
-    tt(V("t4"), V("t1"), V("t3"), ADD)
-    tt(V("t1"), V("t4"), V("t2"), ADD)
-    copy(V("CODE"), V("t1"))
+    ts(V("t2"), V("PR"), float(C * (r + 1)), A.is_lt, float(N * C), MUL)
+    tt(V("t4"), V("PR"), V("t2"), ADD)
+    tt(V("t1"), V("t4"), V("t3"), ADD)
+    ts(V("CODE"), V("t1"), -float(C * (r + 1)), ADD, float(N * C), A.min)
     scatter(V("INVF"), V("POSU"), V("IOTA", 0, C))
-    ts(V("INV0"), fold(V("INVF", 0, M), M), col(10), ADD)
+    ts(V("INV0", 0, 6), fold(V("INVF", 0, M), M), col(10), ADD)
 
-    def layer(w, out, between=None):
+    def layer(w, to, between=None):
         quant("QX", 0, 128, V("TX"))
         for b in range(4):
             mm(bank("PB", b, 128), w, 128 * b, "QX", 0, 128)
         if between: between()
         for b in range(4):
-            act(out(b), bank("PB", b, M), scale=0.03125)
+            act(to(b), bank("PB", b, M), scale=0.03125)
 
     for t in range(4):
-        act(V("TX", t, 4 * M, 4), ind(V("X0", C * t, C * t + C), V("INV0")))
+        act(V("TX", t, 4 * M, 4), ind(V("X0", C * t, C * t + C), V("INV0", 0, 6)))
     layer("QW", lambda b: V("TYS", b, 4 * M, 4))
     quant("QS", Y0, 128, V("TYS", 0, 512))
     send_whole()
@@ -443,99 +465,79 @@ def rank_program(g, core, T, topo):
     dma("s", u8(V("QVc")), ext(T.vc[:]))
     dma("s", V("TU"), ext(T.u[:]))
 
+    def entries(l, k):
+        return ind(V("PF", C * k, C * k + C), V("INV12", 6 * l - 6, 6 * l))
+
     def codes(l):
-        tt(V("NV%d" % l), ind(V("PF"), V("PFO", 12 * (l - 1), 12 * l)), V("E4096"), ADD)
-        tt(V("NW%d" % l), fold(V("NV%d" % l), 2 * M), V("ETAB"), A.subtract)
+        for k in range(2):
+            act(V("NV%d" % l, M * k, M * k + M), entries(l, k), bias=float(KS) if k else None)
+        tt(V("NW%d" % l), fold(V("NV%d" % l), 2 * M), V("ETAB"), ADD)
 
     def lists(l):
+        tl, oa, ofu = "TL%d" % l, "OA%d" % l, V("OFU%d" % l)
+        for k in range(2):
+            act(V("UA", M * k, M * k + M), entries(l, k), ACT.Abs, bias=col(11))
+        ts(V("MA"), V("UA"), col(14), MUL, C / 2, A.is_lt)
+        lin(V("NA"), V("MA"), 1024.0, -1024.0)
+        scan(V("CA"), V("MA"), V("ZR"), col(15), ADD, ADD)
+        scan(V("XA"), V("CA"), V("NA"), -1024.0, A.max, ADD)
+        copy(V("DA"), ind(V("XA"), V("DB2")))
+        tr(V("TA"), V("DA"))
+        scan(V(oa), V("DO"), V("TA"), 0.0, ADD, A.max)
+        ts(ofu, V(oa, 31, 384, 32), col(16), ADD)
+        scatter(V(tl), ofu, V("NV%d" % l))
         use[0] = ""
-        off, tl = "OFF%d" % l, "TL%d" % l
-        ts(V("t2", 0, 12), V("NW%d" % l), float(N * C - 1), A.min, -143.5, ADD)
-        ts(V("TW", 1, 13), V("t2", 0, 12), 1.0 / C, MUL, float(ROUND), ADD)
-        tt(V("L2", 0, 128), ind(V("TW"), V("KOFF")), V("KEYC"), A.is_equal)
-        scan(V("L3", 0, 128), V("RESET", 0, 128), V("L2", 0, 128), 0.0, MUL, ADD)
-        copy(V("TT", 0, 8), V("L3", 15, 128, 16))
-        tr(V("TA"), V("TT"))
-        scan(V("TB", 1, 32), V("TA", 0, 31), V("RESET", 1, 32), 0.0, ADD, MUL)
-        tr(V("TC"), V("TB"))
-        tt(V("L2", 0, 128, 16), V("TC", 0, 8), V("CB"), ADD)
-        scan(V("L1", 0, 128), V("RESET", 0, 128), V("L2", 0, 128), 0.0, MUL, ADD)
-        tt(V("L3", 128, 256), V("L1", 0, 128), V("L2", 0, 128), MUL)
-        tt(V("L1", 128, 192), V("L3", 128, 192), V("L3", 192, 256), ADD)
-        tt(V("L1", 192, 224), V("L1", 128, 160), V("L1", 160, 192), ADD)
-        tt(V(off), V("L1", 192, 208), V("L1", 208, 224), ADD)
-        copy(V("OFU"), V(off, 1, 13))
-        scatter(V(tl), V("OFU"), V("NV%d" % l))
-        ts(V("WL%d" % l, 0, 14), fold(V(tl, 0, K), K), col(10), ADD)
+        tt(V("t2", 0, 14), fold(V(tl, 2 * M, 2 * M + K), K), V("CJ"), ADD)
+        copy(V("WL%d" % l, 0, 14), V("t2", 0, 14))
         send_small("l%d" % l)
 
+    def no_requests(l):
+        iota(V("TL%d" % l, 2 * M, 2 * M + K), [[C, N - 1], [0, CAP]], -1, 0)
+
     copy(V("PF"), ind(V("IOTA"), V("CODE")))
-    lin(V("CB"), V("IOTA", 0, 8), float(CAP), -1.0)
-    fill("TW", 0, 16, 0)
-    fill("TT", 0, 32, 0)
-    fill("TB", 0, 1, 0)
-    fill("T7", 0, 32, 0)
-    fill("V7", 0, 1, 0)
-    lin(V("B7"), V("IOTA", 0, 7), float(M), 0.0)
-    for k in range(2):
-        lin(V("E4096", M * k, M * k + M), V("IOTA", 128 * k, 128 * k + M), 4096.0, 0.0)
-    ts(V("ETAB"), V("E4096", 0, 2 * M, 16), col(11), ADD)
-    fill("TL2", 0, K, EMPTY)
-    fill("WL2", 14, 16, 0)
-    lin(col(8), col(2), 0.5, 0.0)
-    lin(col(7), col(2), -0.5, 0.5)
-    ts(V("ET", 3, 515, 4), V("IOTA", 0, 128), col(0), A.is_equal, col(7), MUL)
+    ts(V("ETAB", 0, 6), V("IOTA", 0, 6), 0.0, MUL, col(10), ADD)
+    ts(V("ETAB", 6, 12), V("ETAB", 0, 6), -float(KS), ADD)
+    no_requests(2)
+    fill("ZR", 0, 2 * M, 0)
+    fill("DO", 0, 384, 0)
+    fill("DO", 0, 384, -4096, 32)
+    ts(V("DO", 16, 384, 32), V("IOTA", 0, 12), 0.0, MUL, col(17), ADD)
     scan(V("SCI"), V("DD", 0, 2 * M), V("INVF", M, C), 0.0, ADD, A.max)
-    inv = lambda a, b: V("SCI", a + 15, b, 16)
-    copy(V("AU", 0, 160), V("ST"))
-    for l in (2, 1):
-        for k in range(2):
-            a = 12 * (l - 1) + 6 * k
-            ts(V("PFO", a, a + 6), inv(M * l - M, M * l), col(10), ADD, float(C * k), ADD)
-    ts(V("INV12"), inv(0, 2 * M), col(10), ADD)
+    ts(V("AU", 0, 56), V("ST"), col(1), ADD)
+    ts(V("INV12"), V("SCI", 15, 2 * M, 16), col(10), ADD)
     codes(2)
     lists(2)
-    unit("QH0")
-    ts(V("ET", 3, 515, 4), V("IOTA", 0, 128), col(0), A.is_equal, col(8), MUL)
     copy(V("POSF", 1, C + 1), ind(V("IOTA", 0, C), V("POSU")))
     fill("PP", 144, 148, N * M + 1)
     ts(V("PP", 126, 144), posw, float(OWN), ADD)
     fill("POSF", 0, C + 2, 2 * M, C + 1)
+    copy(V("POSF", KS, 2 * KS), V("POSF", 0, KS))
     for t in range(4):
         copy(V("DS", 192 * t, 192 * t + 192), ind(V("X0", C * t, C * t + C), V("INV12")))
     codes(1)
     use[0] = "b"
-    for h in range(2):
-        copy(V("i1", h, 12, 2), V("NW1", 6 * h, 6 * h + 6))
+    copy(V("i1", 0, 12), V("NW1"))
     ts(V("i2", 0, 12), V("i1", 0, 12), 15, A.bitwise_and)
     ts(V("i3", 0, 12), V("i1", 0, 12), 4, A.logical_shift_right)
-    copy(V("LO2"), V("i2", 0, 12))
-    copy(V("HI2"), V("i3", 0, 12))
+    for h in range(2):
+        copy(V("LO2", h, 24, 2), V("i2", 0, 12))
+        copy(V("HI2", h, 24, 2), V("i3", 0, 12))
+    iota(V("RS2"), [[0, 24], [1024, 16]], 0, 0)
     copy(V("MKL"), ind(V("DIAG", 0, 16), V("LO2")))
-    unit("QH1")
+    for q, c in (("QH1", 8), ("QH0", 7)):
+        ts(V("ET", 3, 515, 4), V("IOTA", 0, 128), col(0), A.is_equal, col(c), MUL)
+        unit(q)
     for t in range(4):
         copy(V("YP", YW * t, YW * t + M), V("TYS", t, 4 * M, 4))
     fill("YP", 2 * M, 4 * YW, 0, YW)
     fill("ZP", M, 4 * ZW, 0, ZW)
-    copy(V("MP"), V("PPU", 0, 126))
-    scan(V("PP", 0, 126), V("R18"), V("MP"), 0.0, A.min, ADD)
-    copy(V("T7", 0, 7), V("PP", 17, 126, 18))
-    tr(V("U7"), V("T7"))
-    tt(V("MP", 0, 126, 18), V("MP", 0, 126, 18), V("B7"), ADD)
-    scan(V("V7", 1, 32), V("U7", 0, 31), V("RESET", 1, 32), 0.0, ADD, MUL)
-    tr(V("W7"), V("V7"))
-    tt(V("MP", 0, 126, 18), V("MP", 0, 126, 18), V("W7", 0, 7), ADD)
-    scan(V("PP", 0, 126), V("R18"), V("MP"), 0.0, A.min, ADD)
-    tt(V("L2", 0, 192), ind(V("PP"), V("HI2")), V("MKL"), MUL)
-    tr(V("L3", 0, 192), V("L2", 0, 192))
-    scan(V("L1", 0, 192), V("RESET", 0, 192), V("L3", 0, 192), 0.0, MUL, ADD)
-    copy(V("T7", 0, 12), V("L1", 15, 192, 16))
-    tr(V("U7"), V("T7"))
-    copy(V("L2", 192, 256), ind(V("U7"), V("DUPO")))
-    for k in range(2):
-        tr(V("L3", 192 + 12 * k, 224 + 12 * k), V("L2", 192 + 32 * k, 224 + 32 * k))
-    for h in range(2):
-        ts(V("OF1", 16 * h, 16 * h + 12), V("L3", 192 + h, 216, 2), -1.0, ADD)
+    for u in range(N - 1):
+        ts(V("PP", 18 * u, 18 * u + 18), V("PPU", 18 * u, 18 * u + 18), float(M * u), ADD)
+    tt(V("L2"), ind(V("PP"), V("HI2")), V("MKL"), MUL)
+    tr(V("L3"), V("L2"))
+    scan(V("L1"), V("RS2"), V("L3"), 0.0, A.min, ADD)
+    for h in (1, 0):
+        ts(V("OF1", 16 * h, 16 * h + 12), V("L1", 16 * h + 15, 384, 32), -1.0, ADD)
 
     def gather_sum(p, win, wn, of, second, d, between=None):
         pick(p, 3 * M, win, wn, V(of, second + 6, second + 14), 128)
@@ -559,25 +561,20 @@ def rank_program(g, core, T, topo):
             send_half(k, h)
 
     def arrived(l):
-        use[0] = "c"
-        copy(V("i1", 0, 14), V("LL%d" % l))
-        ts(V("i2", 0, 14), V("i1", 0, 14), 4095, A.bitwise_and)
-        tt(V("t2", 0, 14), V("i2", 0, 14), V("CJ"), A.subtract)
-        ts(V("JU"), V("t2", 0, 14), float(C + 1), A.min)
-        got = fold(ind(V("POSF", 0, C + 2), V("JU")), K)
+        got = fold(ind(V("POSF"), V("LL%d" % l)), K)
         if l == 2: ts(V("G2"), got, col(10), ADD)
         ts(V("PC%d" % l, 0, 14), got, col(10), ADD)
-        ts(V("KC%d" % l, 0, 14), V("LL%d" % l), 4096.0 * 128, A.is_ge, float(2 * M), MUL)
+        ts(V("KC%d" % l, 0, 14), V("LL%d" % l), float(KS), A.is_ge, float(2 * M), MUL)
 
     def own(l):
         ts(V("JO"), V("NW%d" % l), -float(C * (N - 1) - 1), ADD)
         ts(V("PC%d" % l, 14, 26), fold(ind(V("POSF", 0, C + 2), V("JO")), 2 * M), col(10), ADD)
 
-    def back_send(l, out):
-        use[0] = "d"
-        copy(V("i1", 0, 14), V("WL%d" % l, 0, 14))
-        ts(V("i2", 0, 14), V("i1", 0, 14), 12, A.logical_shift_right, 127, A.bitwise_and)
-        copy(V(out), V("i2", 0, 14))
+    def back_send(l, to):
+        tp = "TP%d" % l
+        fill(tp, 2 * M, 2 * M + K, M)
+        scatter(V(tp), V("OFU%d" % l), V("PLC"))
+        ts(V(to), fold(V(tp, 2 * M, 2 * M + K), K), col(10), ADD)
 
     def successors(l):
         use[0] = "d"
@@ -623,12 +620,15 @@ def rank_program(g, core, T, topo):
         copy(V("TYS", 4 * M + b, 8 * M, 4), V("YP", YW * b + M, YW * b + 2 * M))
     fill("W32", 0, 32, 0)
     lin(V("IDXC"), V("IOTA", 0, 416, 16), 1.0, col(1))
-    lin(V("IDXC", 14, 20), V("IDXC", 14, 20), 1.0, float(2 * M))
+    lin(V("IDXC", 0, 20), V("IDXC", 0, 20), 1.0, float(2 * M))
+    for k in range(2):
+        seq(V("PLC", M * k, M * k + M), 1, 0)
     for l in (2, 1):
         fill("KC%d" % l, 14, 20, 0)
         fill("KC%d" % l, 20, 26, 2 * M)
-    act(V("VAL2", 0, K + M), V("IOTA", 0, K + M))
-    act(V("VAL2", K + M, K + 2 * M), V("IOTA", K, K + M))
+    for l in (2, 1):
+        seq(V("VAL%d" % l, 0, K + M), 1, (2 - l) * (K + 128))
+        seq(V("VAL%d" % l, K + M, K + 2 * M), 1, K + (2 - l) * (K + 128))
     fill("SU", 0, 4 * M, K + M)
     quant("WF2", K, K, V("TYS"))
     for b in range(4):
@@ -636,17 +636,16 @@ def rank_program(g, core, T, topo):
     for b in range(4):
         act(V("DY", 192 * b, 192 * b + 192), bank("PA", b, 2 * M))
     fill("TZ", 4 * M, 512, 0)
-    fill("TL1", 0, K, EMPTY)
-    fill("WL1", 14, 16, 0)
-    lin(V("VAL1"), V("VAL2"), 1.0, float(K + 128))
+    no_requests(1)
     own(2)
     use[0] = "b"
-    ts(V("t1", 0, 12), V("OFF2", 1, 13), float(K), A.is_ge, 1000.0, MUL)
+    ts(V("OFF2", 0, 12), V("OA2", 31, 384, 32), col(16), ADD, -2.0 * M, ADD)
+    ts(V("t1", 0, 12), V("OFF2", 0, 12), 0.0, A.is_lt, 1000.0, MUL)
     ts(V("t2", 0, 12), V("PC2", 14, 26), float(K), ADD)
-    tt(V("t3", 0, 12), V("t1", 0, 12), V("OFF2", 1, 13), ADD)
+    tt(V("t3", 0, 12), V("t1", 0, 12), V("OFF2", 0, 12), ADD)
     tt(V("W32", 0, 12), V("t3", 0, 12), V("t2", 0, 12), A.min)
     tr(V("D1"), V("W32"))
-    copy(V("D2"), ind(V("D1"), V("DUPO")))
+    copy(V("D2"), ind(V("D1"), V("DB2", 0, 4)))
     tr(V("D3"), V("D2"))
     copy(V("OF2"), V("D3"))
     successors(2)

from concourse.bass import DstId, RemoteDMATransfer
from concourse.mybir import dt, AluOpType, ActivationFunctionType

N, C, M, CAP = 8, 288, 96, 32
K = (N - 1) * CAP
F, B, I, U, X4, SC = "float32", "bfloat16", "int32", "uint16", "float8_e4m3fn_x4", "uint8"
KS = C + 2
STEP = float(1 << 20)
Y0, HALF = C, C + 128
OWN = (N - 1) * M
YW, ZW = 208, 112

PACK_U = "DB2 DBL WL2 OF1 OF3 OF4 WL1 CODE POSU POSZ INV0 INV12 OFU1 OFU2 HI2 LO2 JO SUO OF2 G2 G3 G4".split()
PACK_F = "t1 t2 t3 t4 D1 D2 D3 W32 OFF2 PC1 PC2 KC1 KC2 CJ IDXC ETAB NW1 NW2 MK CS NM CT CU CV CW C3 PS R3 R32".split()
PLACE = {}
TEMPS = "t1 t2 t3 t4 i1 i2 i3 L1 L2 L3".split()
LAID = "1s010a0I1m0O0d0m280s221g0yaw100E2e1z4t0U361E31ph3Hip1c6d5V16aq4h4c5k5e5q617K6i3N6G3c546o676MdGb46u4n7E2q6A2D7Q3A3T746S6Y7W451WoY7a4y3Z7m7g2k4Z827u3uaF88op4Tdz2V5Jaz3i3obk4H8e4N5O5x8k2wps5C8JaS8rbw8CbD8wbIexaYer8OdKc7bO9f2PoOaK992Ic1eC93ok8X9BbU1S9u9o9jeI1MqIdRccov9GqPeOcico9Oa8aebqqxb8f0uNcuEc58beLIcBeUfoEyqU9UfigWABcGpAe9fcoHcMAvel7DpccShrf6hDr6hlcYfBfwhPEFhwhehIrcdXd4hUqEgLgFr1oTroLCdarji0efe3dgfGi6doiwfSfYiiicg4fMa3akj4jbdxjgjngajTjHjzjZjsjNgRgsiBk5kbgmknkhggkRh3gykXrukFAGkLloktlikzrAiYl3l9rHlcANluiGlAlJrMiTEKiMlPrYASlVm4m1mbs4rSmgmnmymtmEmLsanUnfAYocmQo7sgo1nknrmYpEn9n4smB5nwpTssq5nEpZqfpNqlnKqrBah9wkBgnTq9sLsEsQsXBmtht2t9tttntLoBBstztXsztFufulu3u9uDvytRvsuJuruxvKvEvQByvZvaw5whwrwbwIwxwCwOuSx3xfx9xpwXxBxvvgxjxGuYvmxVxPy7v4ygy1ybysyFymyyyRyKzlzqzfyWp5zwERA1z4AiBEAdzCA6zaBKEgzKzQBSEmpoLOAozZC9C2CeClCqCXCxCLCFEsCRDlD9D3DfC1DPI9E1E7DrDVFeDxIqDDF8DJEWF2IeFkLUIlFtFLIwICFFFOFzG7IIG0GSFVGvGcGjGoGYHbIOH5GAHFHQHLGIIUHWHgJ0GOHoHuI2J6M0JcHDJoJiJBJuJNJGKpJZK7JSKjKdKHKvKBKNLtLzKTLhMoLnKZMiM6L5LbMcMuMJMPMVN4MDNaNhMYNmNzNsNLNENTO6NZOJOcOeOkOxODOu"
LETTERS = "0123456789abcdefghijklmnopqrstuvwxyzABCDEFGHIJKLMNOPQRSTUVWXYZ"


def _scratch():
    s = {}
    for n, w, d in [
        ("IOTA", 2308, F), ("PI", 4, I), ("CC", 24, F), ("J16", 224, F), ("JT", 224, F), ("DIAG", 224, B), ("RESET", 224, B), ("RS2", 384, B), ("DD", 224, F),
        ("CJ", 14, F), ("IDXC", 26, F), ("PLC", 192, F), ("DO", 384, B), ("ZR", 192, B), ("ETAB", 12, F), ("VAL2", 416, F), ("VAL1", 416, F),
        ("DB2", 24, U), ("ST", 56, F),
        ("ET", 520, B), ("LVT", 18, I), ("PR", 36, I), ("CODE", 36, U), ("PF", 576, F),
        ("t1", 36, F), ("t2", 36, F), ("t3", 36, F), ("t4", 36, F), ("i1", 32, I), ("i2", 32, I), ("i3", 32, I),
        ("MK", 96, F), ("CS", 96, F), ("NM", 96, F), ("CT", 96, F), ("CU", 96, F), ("CV", 96, F), ("CW", 96, F),
        ("C3", 54, F), ("PS", 54, F), ("R3", 54, F), ("R32", 96, F),
        ("L1", 384, F), ("L2", 384, F), ("L3", 384, F), ("MKL", 384, B), ("SD", 384, F),
        ("POSU", 18, U), ("POSS", 18, B), ("POSZ", 18, U), ("POSF", 2 * KS, B), ("PP", 148, F), ("PPU", 128, B),
        ("INVF", 288, F), ("SCI", 192, F), ("INV0", 8, U), ("INV12", 12, U),
        ("NW1", 12, F), ("NW2", 12, F), ("NV1", 192, F), ("NV2", 192, F),
        ("OFF2", 16, F), ("OFU1", 12, U), ("OFU2", 12, U), ("TL1", 416, F), ("TL2", 416, F), ("TP1", 416, F), ("TP2", 416, F),
        ("WL1", 16, U), ("WL2", 16, U),
        ("UA", 192, F), ("MA", 192, B), ("NA", 192, B), ("CA", 192, B), ("XA", 192, B), ("DA", 384, B), ("TA", 384, B), ("OA1", 384, F), ("OA2", 384, F),
        ("LL1", 14, U), ("LL2", 14, U), ("HI2", 24, U), ("LO2", 24, U), ("JO", 12, U),
        ("PC1", 26, F), ("PC2", 26, F), ("KC1", 26, F), ("KC2", 26, F), ("SUO", 26, U), ("SU", 800, F),
        ("W32", 32, F), ("D1", 32, F), ("D2", 64, F), ("D3", 64, F), ("DBL", 24, U),
        ("OF1", 32, U), ("OF2", 64, U), ("OF3", 32, U), ("OF4", 32, U), ("G2", 14, U), ("G3", 14, U), ("G4", 14, U),
        ("TXN", 1152, B), ("X0", 1152, B), ("TX", 512, B), ("TYS", 896, B), ("TZ", 512, B), ("YP", 4 * YW, B), ("ZP", 4 * ZW, B),
        ("SG", 1024, B), ("DS", 768, B), ("DY", 768, B),
        ("TU", 512, B), ("YO", 288, F), ("HP", 18, B), ("HL1", 4, U), ("HL2", 4, U),
    ]:
        s[n] = ("sbuf", [128, w], d)
    for n, w in [("QE", 512), ("QH0", 512), ("QH1", 512), ("QW", 512), ("QV", 512), ("QU", 128), ("QS", HALF + 6 * 128),
                 ("QX", 128), ("QY2", 128), ("WF1", OWN + 128), ("WF2", 448), ("WB", 832), ("QO", 288),
                 ("P1", 416), ("P2", 416), ("P3", 416), ("P4", 416),
                 ("H1", 96), ("H2", 64), ("H3", 64), ("H4", 64)]:
        s[n + "c"] = ("sbuf", [128, w], X4)
        s[n + "s"] = ("sbuf", [128, w], SC)
    for n in TEMPS:
        for c in "bcd": s[n + c] = s[n]
    for c in "01234567": s["FL" + c] = ("sbuf", [128, 224], F)
    more = lambda first: [n + c for n in TEMPS if n[0] in first for c in ("", "b", "c", "d") if n + c not in PACK_F]
    for arena, d, names in (("AU", U, PACK_U), ("AF", F, PACK_F + more("tL") + ["FL" + c for c in "01234567"]), ("AI", I, more("i"))):
        at = 0
        for n in names:
            PLACE[n] = (arena, at, s[n][1][1])
            at += -(-s.pop(n)[1][1] // 16) * 16
        s[arena] = ("sbuf", [128, at], d)
    s["PA"] = ("psum", [128, 2048], F)
    s["PB"] = ("psum", [128, 2048], F)
    return s


SCRATCH = _scratch()
SEMAPHORES = (["cv", "ca", "cp", "cg", "ls", "dl"] + ["d%d" % i for i in range(22)] + ["xp", "xl1", "xl2", "x1", "x2", "x3", "x4"]
              + ["hp", "hl1", "hl2"] + ["hc%d" % i for i in (1, 2, 3, 4)] + ["hs%d" % i for i in (1, 2, 3, 4)])
BIG = {1: ("WF1", M, 0), 2: ("WF2", CAP, 0), 3: ("WB", CAP, 0), 4: ("WB", CAP, K + 128)}
SMALL = {"p": ("POSS", "HP", "PPU", 18), "l2": ("WL2", "HL2", "LL2", 2), "l1": ("WL1", "HL1", "LL1", 2)}
ORDER = ["p", 1, "l2", 2, 3, "l1", 4]
SCALES = [4, 5, 6, 3]
SLOTS = {0: ("c", [0, 1]), 1: ("c", [2, 3]), 4: ("s", [0, 1]), 5: ("s", [2, 3]), 3: ("c", [6]), 6: ("s", [6])}
LAST = (("c", 3), ("s", 6))


def _bits(engines):
    return sum(1 << e for e in engines)


def _helpers(topo, rc):
    rest = [c for c in topo.cores_of(rc) if c != rc]
    near = [c for c in rest if topo.die(c) == topo.die(rc)]
    far = [c for c in rest if topo.die(c) != topo.die(rc)]
    mixed = []
    while near or far:
        if near: mixed.append(near.pop(0))
        if far: mixed.append(far.pop(0))
    return mixed


def _to(topo, src, dst, mask, sem, a, b):
    rid, pid = topo.addr(dst, src)
    return RemoteDMATransfer(dst_ids=[DstId(rid=rid, pnc=pid)], dma_engine_mask=mask, remote_sem=sem, src=a, dst=b)


def helper_program(g, core, T, topo, r, h):
    peer = [T.cores[(r + 1 + u) % N] for u in range(N - 1)]
    eng = topo.engines(core, peer[0])
    half = len(eng) // 2
    pair = lambda i: [u for u in (2 * i, 2 * i + 1) if u < N - 1]
    sent = 0
    for k in ORDER:
        if k in SMALL:
            _s, hb, land, w = SMALL[k]
            if k != "p" and h not in SCALES: continue
            us = [h] if k == "p" else pair(SCALES.index(h))
            n = len(eng) // len(us)
            g.wait_ge(T.sem["h" + k], 2 if k == "p" else 4)
            g.remote_dma_fused([_to(topo, core, peer[u], _bits(eng[n * j:n * j + n]), T.sem["x" + k], T[hb][:, w * j:w * j + w],
                                    T[land][:, w * (N - 2 - u):w * (N - 1 - u)]) for j, u in enumerate(us)], local_sem=T.sem.ls)
            sent += len(eng)
            continue
        land, w, o0 = BIG[k]
        jobs = []
        if k == 1:
            if h <= 3: jobs.append(("c", pair(h)))
            if h in SCALES: jobs.append(("s", pair(SCALES.index(h))))
        elif h in SLOTS: jobs.append(SLOTS[h])
        at = 0
        for kind, us in jobs:
            g.wait_ge(T.sem["h%s%d" % (kind, k)], 4 if k == 1 else 8)
            ts = []
            for u in us:
                o = o0 + w * (N - 2 - u)
                a = 0 if k == 1 else w * (u % 2)
                src, dst = T["H%d%s" % (k, kind)][:, a:a + w], T[land + kind][:, o:o + w]
                if kind == "c": src, dst = src.bitcast(dt.uint8), dst.bitcast(dt.uint8)
                n = len(eng) if k > 1 and len(us) == 1 else half
                ts.append(_to(topo, core, peer[u], _bits(eng[n * at:n * at + n]), T.sem["x%d" % k], src, dst))
                at += 1
                sent += n
            g.remote_dma_fused(ts, local_sem=T.sem.ls)
    g.wait_ge(T.sem.ls, sent)


def rank_program(g, core, T, topo):
    r = T.rank_of(core)
    if r is None:
        for i, rc in enumerate(T.cores):
            if core in topo.cores_of(rc):
                helper_program(g, core, T, topo, i, _helpers(topo, rc).index(core))
        return
    A, ACT = AluOpType, ActivationFunctionType
    MUL, ADD = A.mult, A.add
    queue = {"v": g.vector, "a": g.scalar, "p": g.tensor, "g": g, "s": g.sync}
    count = {"v": 0, "a": 0, "p": 0, "g": 0, "ls": 0, "d": 0}
    known = {e: {} for e in queue}
    log = {}
    final = {}
    use, folds, nodes = [""], [0], []

    def V(name, a=0, b=None, step=1):
        if name in TEMPS: name += use[0]
        if name in PLACE:
            name, at, w = PLACE[name]
            a, b = at + a, at + (w if b is None else b)
        b = T[name].shape[1] if b is None else b
        ap = T[name][:, a:b] if step == 1 else T[name][:, a:b:step]
        return (ap, [(name, a, b, step)])

    def bank(name, i, n):
        return (T[name][:, 512 * i:512 * i + n], [(name, 512 * i, 512 * i + 512, 1)])

    def ind(win, off):
        return (win[0].indirect(off[0]), win[1] + off[1])

    def words(v):
        return (v[0].bitcast(dt.uint32), v[1])

    def meet(a, b):
        if a[1] >= b[2] or b[1] >= a[2]: return False
        return not (a[3] > 1 and a[3] == b[3] and (a[1] - b[1]) % a[3] != 0)

    def wait(e, tok):
        if known[e].get(tok[0], 0) >= tok[1]: return
        queue[e].wait_ge(T.sem[tok[0]], tok[1])
        for s, n in list(tok[2].items()) + [(tok[0], tok[1])]:
            known[e][s] = max(known[e].get(s, 0), n)

    def order(e, reads, writes, acc=False):
        rs = [x for v in reads if isinstance(v, tuple) for x in v[1]]
        ws = [x for v in writes for x in v[1]] + [x for x in rs if x[0] in ("PA", "PB")]
        need = {}
        for x, w in [(x, False) for x in rs] + [(x, True) for x in ws]:
            for y, yw, tok in log.get(x[0], []):
                if (w or yw) and meet(x, y) and not (acc and w and tok[0] == "cp"):
                    if tok[0] not in need or need[tok[0]][1] < tok[1]: need[tok[0]] = tok
        for tok in sorted(need.values(), key=lambda t: -len(t[2])):
            wait(e, tok)
        return rs, ws

    def note(rs, ws, tok):
        for x in rs: log.setdefault(x[0], []).append((x, False, tok))
        for x in ws: log.setdefault(x[0], []).append((x, True, tok))
        final[tok[0]] = max(final.get(tok[0], 0), tok[1])

    def later(e, emit, writes, reads):
        rs = [x for v in reads if isinstance(v, tuple) for x in v[1]]
        nodes.append((e, emit, rs, [x for v in writes for x in v[1]] + [x for x in rs if x[0] in ("PA", "PB")]))

    def op(e, call, writes, reads, acc=False):
        def emit(e):
            rs, ws = order(e, reads, writes, acc)
            count[e] += 1
            (call[e] if isinstance(call, dict) else call)().then_inc(T.sem["c" + e], 1)
            note(rs, ws, ("c" + e, count[e], dict(known[e])))
        later(e, emit, writes, reads)

    def schedule():
        for k in range(0, len(LAID), 2):
            z = len(LETTERS) * LETTERS.index(LAID[k]) + LETTERS.index(LAID[k + 1])
            nodes[z // 6][1]("vagpsx"[z % 6])

    def raw(v):
        return v[0] if isinstance(v, tuple) else v

    def dma(e, out, in_):
        def emit(_e):
            rs, ws = order(e, [in_], [out])
            s = "d%d" % count["d"]
            count["d"] += 1
            queue[e].dma_start(out[0], in_[0]).then_inc(T.sem[s], 16)
            note(rs, ws, (s, 16, dict(known[e])))
        later(e, emit, [out], [in_])

    def ext(ap):
        return (ap, [])

    def memset(o, c): op("v", lambda: g.vector.memset(o[0], c), [o], [])
    def real(v): return SCRATCH[v[1][0][0]][2] in (F, B, SC)

    def either(o, i, scale=None, bias=None, pat=None):
        kw = {k: raw(x) for k, x in (("scale", scale), ("bias", bias)) if x is not None}
        if scale is None and bias is None: v = lambda: g.vector.tensor_copy(o[0], i[0])
        elif bias is None: v = lambda: g.vector.tensor_scalar(o[0], i[0], raw(scale), None, MUL)
        elif scale is None: v = lambda: g.vector.tensor_scalar(o[0], i[0], raw(bias), None, ADD)
        else: v = lambda: g.vector.tensor_scalar(o[0], i[0], raw(scale), raw(bias), MUL, ADD)
        f = ACT.Copy if bias is None else ACT.Identity
        calls = {"a": lambda: g.scalar.activation(o[0], i[0], f, **kw), "v": v}
        if pat: calls["g"] = lambda: g.iota(o[0], pat[0], pat[1], 0, allow_small_or_imprecise_dtypes=True)
        op("".join(calls), calls, [o], [i, scale, bias])

    def copy(o, i):
        if real(o) and real(i): either(o, i)
        else: op("v", lambda: g.vector.tensor_copy(o[0], i[0]), [o], [i])

    def tt(o, a, b, f): op("v", lambda: g.vector.tensor_tensor(o[0], a[0], b[0], f), [o], [a, b])
    def tr(o, i): op("v", lambda: g.vector.transpose(o[0], i[0]), [o], [i])

    def ts(o, a, s1, f1, s2=None, f2=None):
        if real(o) and real(a) and f2 is None and f1 is MUL: either(o, a, scale=s1)
        elif real(o) and real(a) and f2 is None and f1 is ADD: either(o, a, bias=s1)
        elif real(o) and real(a) and f1 is MUL and f2 is ADD: either(o, a, s1, s2)
        elif f2 is None: op("v", lambda: g.vector.tensor_scalar(o[0], a[0], raw(s1), None, f1), [o], [a, s1])
        else: op("v", lambda: g.vector.tensor_scalar(o[0], a[0], raw(s1), raw(s2), f1, f2), [o], [a, s1, s2])

    def scan(o, a, b, init, f0, f1):
        op("v", lambda: g.vector.tensor_tensor_scan(o[0], a[0], b[0], raw(init), f0, f1), [o], [a, b, init])

    def act(o, i, f=None, bias=None, scale=None):
        if f is None: return either(o, i, scale, bias)
        kw = {}
        if bias is not None: kw["bias"] = raw(bias)
        if scale is not None: kw["scale"] = raw(scale)
        op("a", lambda: g.scalar.activation(o[0], i[0], f, **kw), [o], [i, bias, scale])

    def iota(o, pat, base, cm, fl=True):
        if fl: op("g", lambda: g.iota(o[0], pat, base, cm, allow_small_or_imprecise_dtypes=True), [o], [])
        else: op("g", lambda: g.iota(o[0], pat, base, cm), [o], [])

    def quant(q, a, n, tile):
        c, s = V(q + "c", a, a + n), V(q + "s", a, a + n)
        op("v", lambda: g.vector.quantize_mx(c[0], s[0], tile[0]), [c, s], [tile])

    def mm(out, w, wa, x, xa, n, start=True, stop=True):
        wc, ws, xc, xs = V(w + "c", wa, wa + 128), V(w + "s", wa, wa + 128), V(x + "c", xa, xa + n), V(x + "s", xa, xa + n)
        op("p", lambda: g.tensor.matmul_mx(out[0], wc[0], ws[0], xc[0], xs[0], start, stop), [out], [wc, ws, xc, xs], acc=not start)

    def pick(q, a, win, wn, off, n):
        copy(words(V(q + "c", a, a + n)), ind(words(V(win + "c", 0, wn)), off))
        copy(V(q + "s", a, a + n), ind(V(win + "s", 0, wn), off))

    def col(i): return V("CC", i, i + 1)

    def fold(table, n):
        if len(table[1]) == 2:
            folds[0] += 1
            tmp = V("FL%d" % (folds[0] % 8), 0, n)
            copy(tmp, table)
            table = tmp
        folds[0] += 1
        name = "FL%d" % (folds[0] % 8)
        scan(V(name, 0, n), V("DD", 0, n), table, 0.0, ADD, A.max)
        return V(name, 15, n, 16)

    peer = [T.cores[(r + 1 + u) % N] for u in range(N - 1)]
    help_ = _helpers(topo, core)
    out = topo.engines(core, peer[0])
    out_engines = len(out)
    u8 = lambda v: (v[0].bitcast(dt.uint8), v[1])

    def call(transfers, reads, engines):
        def emit(_e):
            order("g", reads, [])
            g.remote_dma_fused(transfers, local_sem=T.sem.ls)
            count["ls"] += engines
        later("g", emit, [], reads)

    def hand(e, jobs):
        mask = lambda h, i: _bits(topo.engines(core, help_[h])[2 * e * (i // 2):2 * e * (i // 2 + 1)][i % 2::2])
        call([_to(topo, core, help_[h], mask(h, i), T.sem[sem], src[0], dst) for i, (h, sem, src, dst) in enumerate(jobs)],
             [j[2] for j in jobs], e * len(jobs))

    def arrives(views, k, n):
        later("x", lambda _e: note([], [x for v in views for x in v[1]], ("x%s" % k, n * out_engines, {})), views, [])

    def send_small(k):
        src, hb, land, w = SMALL[k]
        if k == "p": hand(2, [(h, "hp", V(src), T[hb][:, 0:w]) for h in range(N - 1)])
        else: hand(4, [(h, "h" + k, V(src, 2 * w * i, 2 * w * i + 2 * w), T[hb][:, 0:2 * w]) for i, h in enumerate(SCALES)])
        arrives([V(land, 0, w * (N - 1))], k, N - 1 if k == "p" else 4)

    def send_whole():
        hand(4, [(h, "hc1", u8(V("QSc", Y0, Y0 + M)), T.H1c[:, 0:M].bitcast(dt.uint8)) for h in range(4)])
        hand(4, [(h, "hs1", V("QSs", Y0, Y0 + M), T.H1s[:, 0:M]) for h in SCALES])
        arrives([V("WF1" + c, 0, OWN) for c in "cs"], 1, N - 1)

    def send_half(k, h):
        a = HALF + 128 * (2 * (k - 2) + h)
        land, w, o0 = BIG[k]
        if h == 0:
            hand(8, [(i, "hc%d" % k, u8(V("QSc", a + 64 * i, a + 64 * i + 64)), T["H%dc" % k][:, 0:64].bitcast(dt.uint8)) for i in range(2)])
            hand(8, [(4 + i, "hs%d" % k, V("QSs", a + 64 * i, a + 64 * i + 64), T["H%ds" % k][:, 0:64]) for i in range(2)])
            return
        n = out_engines // 2
        for c, hh in LAST:
            cast = (lambda x: x.bitcast(dt.uint8)) if c == "c" else (lambda x: x)
            src = [V("QS" + c, a + w * i, a + w * i + w) for i in range(3)]
            rest = [e for e in topo.engines(core, help_[hh]) if e not in out]
            moves = [_to(topo, core, peer[4 + i], _bits(out[n * i:n * i + n]), T.sem["x%d" % k], cast(src[i][0]),
                         cast(T[land + c][:, o0 + w * (N - 6 - i):o0 + w * (N - 5 - i)])) for i in range(2)]
            moves.append(_to(topo, core, help_[hh], _bits(rest), T.sem["h%s%d" % (c, k)], cast(src[2][0]), cast(T["H%d%s" % (k, c)][:, 0:w])))
            call(moves, src, out_engines + len(rest))
        arrives([V(land + c, o0, o0 + K) for c in "cs"], k, N)

    def scatter(win, off, val):
        op("v", lambda: g.vector.tensor_copy(win[0].indirect(off[0]), val[0]), [win], [off, val])

    def fill(name, a, b, c, step=1):
        n = -(-(b - a) // step)
        either(V(name, a, b, step), V("IOTA", 0, n), 0.0, float(c), None if step > 1 else ([[0, n]], int(c)))

    def seq(o, step, base):
        n = o[0].shape[1]
        either(o, V("IOTA", 0, n), float(step), float(base), ([[step, n]], base))

    def lin(o, i, scale, bias):
        either(o, i, scale, bias)

    def unit(q):
        for b in range(4):
            quant(q, 128 * b, 128, V("ET", 3 - b, 515 - b))

    def levels(e, h):
        def emit(_e):
            for k in range(4 * h, 4 * h + 4):
                queue[e].dma_start(T.LVT[16 * k:16 * k + 16, :], T.lv[:]).then_inc(T.sem.dl, 16)
            note([], V("LVT", 9 * h, 9 * h + 9)[1], ("dl", 128, {}))
        later(e, emit, [V("LVT", 9 * h, 9 * h + 9)], [])

    levels("a", 0)
    levels("s", 1)
    dma("a", V("PR", 0, 18), ext(T.pr0[:]))
    dma("s", V("PR", 18, 36), ext(T.pr1[:]))
    dma("s", V("TXN"), ext(T.x[:]))
    dma("s", V("QWs"), ext(T.ws[:]))
    dma("s", u8(V("QWc")), ext(T.wc[:]))

    iota(V("PI", 0, 1), [[1, 1]], 0, 1, fl=False)
    iota(V("IOTA", 0, 128), [[1, 128]], 0, 0)
    iota(V("J16"), [[0, 14], [1, 16]], 0, 0)
    iota(V("R32"), [[0, 3], [1024, 32]], 0, 0)
    iota(V("R3"), [[0, 18], [1024, 3]], 0, 0)
    iota(V("IOTA", 128, 288), [[1, 160]], 128, 0)
    memset(V("ET"), 0.0)
    memset(V("MK"), 0.0)
    memset(V("CU", 0, 1), 0.0)
    fill("TX", 4 * M, 512, 0)
    fill("TYS", 4 * M, 512, 0)
    iota(V("ST", 0, 32), [[16, 16], [0, 2]], 0, 0)
    iota(V("ST", 32, 56), [[2 * M, 2], [16, 6], [0, 2]], 0, 0)
    memset(V("AU", 64, 192), 0)
    ts(V("PI", 1, 2), V("PI", 0, 1), 15, A.bitwise_and)
    ts(V("PI", 2, 3), V("PI", 0, 1), 4, A.logical_shift_right, 1, A.bitwise_and)
    copy(V("CC", 0, 3), V("PI", 0, 3))
    lin(col(10), col(1), STEP, -15 * STEP)
    lin(col(11), col(1), -float(C), -(C - 1) / 2)
    ts(col(14), col(1), N - 1.5, A.is_lt)
    lin(col(12), col(1), float(CAP), -float(15 * CAP + 2 * M))
    ts(col(15), col(14), float(15 * CAP + 2 * M), MUL, col(12), ADD)
    lin(col(16), col(2), 1024.0, 2.0 * M - 1025)
    lin(col(17), col(2), -5120.0, 1024.0)
    lin(col(8), col(2), 0.5, 0.0)
    lin(col(7), col(2), -0.5, 0.5)
    ts(V("ET", 3, 515, 4), V("IOTA", 0, 128), col(0), A.is_equal)
    unit("QE")
    lin(V("CC", 5, 7), V("CC", 0, 2), -1.0, 0.0)
    for a in range(C, N * C, C):
        seq(V("IOTA", a, a + C), 1, a)
    seq(V("IOTA", N * C, N * C + 4), 1, N * C)

    quant("QS", 0, C, V("TXN"))
    for b in range(4):
        mm(bank("PA", b, C), "QE", 128 * b, "QS", 0, C)
    iota(V("t2b", 0, 14), [[-C, N - 1], [0, 2]], 1, 0)
    ts(V("CJ"), V("t2b", 0, 14), col(10), ADD)
    for l in range(3):
        ts(V("MK", 32 * l, 32 * l + 18), V("LVT"), float(l), A.is_equal)
    for b in range(4):
        copy(V("X0", C * b, C * b + C), bank("PA", b, C))
    act(V("JT"), V("J16"), ACT.Abs, bias=col(6))
    act(V("DIAG"), V("JT"), ACT.Relu, bias=1.0, scale=-1.0)
    lin(V("DD"), V("DIAG"), -17 * STEP, STEP)
    act(V("RESET"), V("J16"), ACT.Sign)
    scan(V("CS"), V("R32"), V("MK"), 0.0, A.min, ADD)
    tr(V("CT"), V("CS"))
    scan(V("CU", 1, 96), V("CT", 0, 95), V("RESET", 1, 96), 0.0, ADD, MUL)
    tr(V("CV"), V("CU"))
    lin(V("NM"), V("MK"), 1000.0, -1000.0)
    tt(V("CW", 0, 82), V("CS", 0, 82), V("NM", 0, 82), ADD)
    for l in range(3):
        ts(V("C3", l, 54, 3), V("CW", 32 * l, 32 * l + 18), V("CV", 32 * l + 17, 32 * l + 18), ADD, float(M * l), ADD)
    scan(V("PS"), V("R3"), V("C3"), 0.0, A.min, A.max)
    posw = V("PS", 2, 54, 3)
    ts(V("POSU"), posw, -1.0, ADD)
    copy(V("POSS"), posw)
    send_small("p")
    ts(V("t3"), V("PR"), 0.0, A.is_lt, float(C * (r + 1) + 1), MUL)
    ts(V("t2"), V("PR"), float(C * (r + 1)), A.is_lt, float(N * C), MUL)
    tt(V("t4"), V("PR"), V("t2"), ADD)
    tt(V("t1"), V("t4"), V("t3"), ADD)
    ts(V("CODE"), V("t1"), -float(C * (r + 1)), ADD, float(N * C), A.min)
    scatter(V("INVF"), V("POSU"), V("IOTA", 0, C))
    ts(V("INV0", 0, 6), fold(V("INVF", 0, M), M), col(10), ADD)

    def layer(w, to, between=None):
        quant("QX", 0, 128, V("TX"))
        for b in range(4):
            mm(bank("PB", b, 128), w, 128 * b, "QX", 0, 128)
        if between: between()
        for b in range(4):
            act(to(b), bank("PB", b, M), scale=0.03125)

    for t in range(4):
        act(V("TX", t, 4 * M, 4), ind(V("X0", C * t, C * t + C), V("INV0", 0, 6)))
    layer("QW", lambda b: V("TYS", b, 4 * M, 4))
    quant("QS", Y0, 128, V("TYS", 0, 512))
    send_whole()
    dma("s", u8(V("WF1c", OWN, OWN + 128)), u8(V("QSc", Y0, Y0 + 128)))
    dma("s", V("WF1s", OWN, OWN + 128), V("QSs", Y0, Y0 + 128))
    dma("s", V("QVs"), (T.vs[:], V("WF1c", 0, OWN)[1]))
    dma("s", u8(V("QVc")), ext(T.vc[:]))
    dma("s", V("TU"), ext(T.u[:]))

    def entries(l, k):
        return ind(V("PF", C * k, C * k + C), V("INV12", 6 * l - 6, 6 * l))

    def codes(l):
        for k in range(2):
            act(V("NV%d" % l, M * k, M * k + M), entries(l, k), bias=float(KS) if k else None)
        tt(V("NW%d" % l), fold(V("NV%d" % l), 2 * M), V("ETAB"), ADD)

    def lists(l):
        tl, oa, ofu = "TL%d" % l, "OA%d" % l, V("OFU%d" % l)
        for k in range(2):
            act(V("UA", M * k, M * k + M), entries(l, k), ACT.Abs, bias=col(11))
        ts(V("MA"), V("UA"), col(14), MUL, C / 2, A.is_lt)
        lin(V("NA"), V("MA"), 1024.0, -1024.0)
        scan(V("CA"), V("MA"), V("ZR"), col(15), ADD, ADD)
        scan(V("XA"), V("CA"), V("NA"), -1024.0, A.max, ADD)
        copy(V("DA"), ind(V("XA"), V("DB2")))
        tr(V("TA"), V("DA"))
        scan(V(oa), V("DO"), V("TA"), 0.0, ADD, A.max)
        ts(ofu, V(oa, 31, 384, 32), col(16), ADD)
        scatter(V(tl), ofu, V("NV%d" % l))
        use[0] = ""
        tt(V("t2", 0, 14), fold(V(tl, 2 * M, 2 * M + K), K), V("CJ"), ADD)
        copy(V("WL%d" % l, 0, 14), V("t2", 0, 14))
        send_small("l%d" % l)

    def no_requests(l):
        iota(V("TL%d" % l, 2 * M, 2 * M + K), [[C, N - 1], [0, CAP]], -1, 0)

    copy(V("PF"), ind(V("IOTA"), V("CODE")))
    ts(V("ETAB", 0, 6), V("IOTA", 0, 6), 0.0, MUL, col(10), ADD)
    ts(V("ETAB", 6, 12), V("ETAB", 0, 6), -float(KS), ADD)
    no_requests(2)
    fill("ZR", 0, 2 * M, 0)
    fill("DO", 0, 384, 0)
    fill("DO", 0, 384, -4096, 32)
    ts(V("DO", 16, 384, 32), V("IOTA", 0, 12), 0.0, MUL, col(17), ADD)
    scan(V("SCI"), V("DD", 0, 2 * M), V("INVF", M, C), 0.0, ADD, A.max)
    ts(V("AU", 0, 56), V("ST"), col(1), ADD)
    ts(V("INV12"), V("SCI", 15, 2 * M, 16), col(10), ADD)
    codes(2)
    lists(2)
    copy(V("POSF", 1, C + 1), ind(V("IOTA", 0, C), V("POSU")))
    fill("PP", 144, 148, N * M + 1)
    ts(V("PP", 126, 144), posw, float(OWN), ADD)
    fill("POSF", 0, C + 2, 2 * M, C + 1)
    copy(V("POSF", KS, 2 * KS), V("POSF", 0, KS))
    for t in range(4):
        copy(V("DS", 192 * t, 192 * t + 192), ind(V("X0", C * t, C * t + C), V("INV12")))
    codes(1)
    use[0] = "b"
    copy(V("i1", 0, 12), V("NW1"))
    ts(V("i2", 0, 12), V("i1", 0, 12), 15, A.bitwise_and)
    ts(V("i3", 0, 12), V("i1", 0, 12), 4, A.logical_shift_right)
    for h in range(2):
        copy(V("LO2", h, 24, 2), V("i2", 0, 12))
        copy(V("HI2", h, 24, 2), V("i3", 0, 12))
    iota(V("RS2"), [[0, 24], [1024, 16]], 0, 0)
    copy(V("MKL"), ind(V("DIAG", 0, 16), V("LO2")))
    for q, c in (("QH1", 8), ("QH0", 7)):
        ts(V("ET", 3, 515, 4), V("IOTA", 0, 128), col(0), A.is_equal, col(c), MUL)
        unit(q)
    for t in range(4):
        copy(V("YP", YW * t, YW * t + M), V("TYS", t, 4 * M, 4))
    fill("YP", 2 * M, 4 * YW, 0, YW)
    fill("ZP", M, 4 * ZW, 0, ZW)
    for u in range(N - 1):
        ts(V("PP", 18 * u, 18 * u + 18), V("PPU", 18 * u, 18 * u + 18), float(M * u), ADD)
    tt(V("L2"), ind(V("PP"), V("HI2")), V("MKL"), MUL)
    tr(V("L3"), V("L2"))
    scan(V("L1"), V("RS2"), V("L3"), 0.0, A.min, ADD)
    for h in (1, 0):
        ts(V("OF1", 16 * h, 16 * h + 12), V("L1", 16 * h + 15, 384, 32), -1.0, ADD)

    def gather_sum(p, win, wn, of, second, d, between=None):
        pick(p, 3 * M, win, wn, V(of, second + 6, second + 14), 128)
        pick(p, 2 * M, win, wn, V(of, second, second + 6), M)
        pick(p, 0, win, wn, V(of, 0, 12), 2 * M)
        for i in (3, 2):
            for b in range(4):
                mm(bank("PA", b, 128), "QH1", 128 * b, p, M * i, 128, start=i == 3, stop=False)
        for b in range(4):
            for i in (1, 0):
                mm(bank("PA", b, 128), "QH0", 128 * b, p, M * i, 128, start=False, stop=i == 0)
        if between: between()
        for b in range(4):
            tt(V("TX", b, 4 * M, 4), d(b), bank("PA", b, M), A.subtract)

    def compose(k, plane, off):
        for h in range(2):
            for t in range(4):
                act(V("SG", 512 * h + t, 4 * K if h else 512, 4), ind(plane(t), V(off, 8 * h, 14 if h else 8)))
            quant("QS", HALF + 128 * (2 * (k - 2) + h), 128, V("SG", 512 * h, 512 * h + 512))
            send_half(k, h)

    def arrived(l):
        got = fold(ind(V("POSF"), V("LL%d" % l)), K)
        if l == 2: ts(V("G2"), got, col(10), ADD)
        ts(V("PC%d" % l, 0, 14), got, col(10), ADD)
        ts(V("KC%d" % l, 0, 14), V("LL%d" % l), float(KS), A.is_ge, float(2 * M), MUL)

    def own(l):
        ts(V("JO"), V("NW%d" % l), -float(C * (N - 1) - 1), ADD)
        ts(V("PC%d" % l, 14, 26), fold(ind(V("POSF", 0, C + 2), V("JO")), 2 * M), col(10), ADD)

    def back_send(l, to):
        tp = "TP%d" % l
        fill(tp, 2 * M, 2 * M + K, M)
        scatter(V(tp), V("OFU%d" % l), V("PLC"))
        ts(V(to), fold(V(tp, 2 * M, 2 * M + K), K), col(10), ADD)

    def successors(l):
        use[0] = "d"
        pc, kc = V("PC%d" % l), V("KC%d" % l)
        ts(V("t2", 0, 26), pc, float(2 * M), A.is_ge)
        tt(V("t3", 0, 26), pc, kc, ADD)
        tt(V("t4", 0, 26), V("t2", 0, 26), V("IDXC"), MUL)
        tt(V("t1", 0, 26), V("t3", 0, 26), V("t4", 0, 26), ADD)
        copy(V("SUO"), V("t1", 0, 26))
        scatter(V("SU"), V("SUO"), V("VAL%d" % l))
        copy(V("SD"), ind(V("SU", M * (l - 1), 4 * M), V("DBL")))

    def successors_end(of):
        use[0] = "d"
        tr(V("L3"), V("SD"))
        for h in range(2):
            copy(V(of, 16 * h, 16 * h + 12), V("L3", 16 * h, 384, 32))

    def places():
        use[0] = "c"
        ts(V("t1", 0, 18), posw, M + 0.5, A.is_ge, -float(K), MUL)
        ts(V("t2", 0, 18), posw, 2 * M + 0.5, A.is_ge, -float(2 * K), MUL)
        tt(V("t3", 0, 18), V("t1", 0, 18), posw, ADD)
        tt(V("t4", 0, 18), V("t3", 0, 18), V("t2", 0, 18), ADD)
        ts(V("POSZ"), V("t4", 0, 18), float(2 * K + 255), ADD)

    yplane = lambda t: V("YP", YW * t, YW * t + 2 * M + 1)
    zplane = lambda t: V("ZP", ZW * t, ZW * t + M + 1)
    znew = lambda b: V("ZP", ZW * b, ZW * b + M)

    def ztile(at):
        for b in range(4):
            copy(V("TZ", b, 4 * M, 4), znew(b))
        quant("WB", at, 128, V("TZ"))

    fill("TYS", 8 * M, 896, 0)
    fill("SG", 4 * K, 1024, 0)
    arrived(2)
    gather_sum("P1", "WF1", OWN + 128, "OF1", 16, lambda b: V("DS", 192 * b, 192 * b + M))
    layer("QW", lambda b: V("YP", YW * b + M, YW * b + 2 * M))
    compose(2, yplane, "G2")
    for b in range(4):
        copy(V("TYS", 4 * M + b, 8 * M, 4), V("YP", YW * b + M, YW * b + 2 * M))
    fill("W32", 0, 32, 0)
    lin(V("IDXC"), V("IOTA", 0, 416, 16), 1.0, col(1))
    lin(V("IDXC", 0, 20), V("IDXC", 0, 20), 1.0, float(2 * M))
    for k in range(2):
        seq(V("PLC", M * k, M * k + M), 1, 0)
    for l in (2, 1):
        fill("KC%d" % l, 14, 20, 0)
        fill("KC%d" % l, 20, 26, 2 * M)
    for l in (2, 1):
        seq(V("VAL%d" % l, 0, K + M), 1, (2 - l) * (K + 128))
        seq(V("VAL%d" % l, K + M, K + 2 * M), 1, K + (2 - l) * (K + 128))
    fill("SU", 0, 4 * M, K + M)
    quant("WF2", K, K, V("TYS"))
    for b in range(4):
        mm(bank("PA", b, 2 * M), "QE", 128 * b, "WF2", K, 2 * M)
    for b in range(4):
        act(V("DY", 192 * b, 192 * b + 192), bank("PA", b, 2 * M))
    fill("TZ", 4 * M, 512, 0)
    no_requests(1)
    own(2)
    use[0] = "b"
    ts(V("OFF2", 0, 12), V("OA2", 31, 384, 32), col(16), ADD, -2.0 * M, ADD)
    ts(V("t1", 0, 12), V("OFF2", 0, 12), 0.0, A.is_lt, 1000.0, MUL)
    ts(V("t2", 0, 12), V("PC2", 14, 26), float(K), ADD)
    tt(V("t3", 0, 12), V("t1", 0, 12), V("OFF2", 0, 12), ADD)
    tt(V("W32", 0, 12), V("t3", 0, 12), V("t2", 0, 12), A.min)
    tr(V("D1"), V("W32"))
    copy(V("D2"), ind(V("D1"), V("DB2", 0, 4)))
    tr(V("D3"), V("D2"))
    copy(V("OF2"), V("D3"))
    successors(2)

    gather_sum("P2", "WF2", 448, "OF2", 32, lambda b: V("DS", 192 * b + M, 192 * b + 2 * M), lambda: (back_send(2, "G3"), successors_end("OF3")))
    layer("QW", lambda b: V("TZ", b, 4 * M, 4), lambda: quant("QU", 0, 128, V("TU")))
    quant("QY2", 0, 128, V("TZ"))
    for b in range(4):
        mm(bank("PA", b, 128), "QE", 128 * b, "QY2", 0, 128)
    for b in range(4):
        act(V("TX", b, 4 * M, 4), bank("PA", b, M))
    layer("QV", znew)
    compose(3, zplane, "G3")
    ztile(K)
    lists(1)

    gather_sum("P3", "WB", K + 128, "OF3", 16, lambda b: V("DY", 192 * b + M, 192 * b + 2 * M), lambda: (back_send(1, "G4"), own(1)))
    layer("QV", znew)
    compose(4, zplane, "G4")
    ztile(2 * K + 128)
    arrived(1)
    successors(1)
    successors_end("OF4")

    gather_sum("P4", "WB", 2 * K + 256, "OF4", 16, lambda b: V("DY", 192 * b, 192 * b + M), places)
    layer("QV", lambda b: V("TZ", b, 4 * M, 4))
    quant("WB", 2 * K + 256, 128, V("TZ"))
    runs = [(0, 160), (160, C)]
    for a, b in runs:
        pick("QO", a, "WB", 832, V("POSZ", a // 16, b // 16), b - a)
    for i, (a, b) in enumerate(runs):
        mm(bank("PA", i, b - a), "QU", 0, "QO", a, b - a)
    dma("s", ext(T.oc[:]), u8(V("QOc")))
    dma("s", ext(T.osc[0:4, :]), (T.QOs[0:4, :], V("QOs")[1]))
    for i, (a, b) in enumerate(runs):
        copy(V("YO", a, b), bank("PA", i, b - a))
    dma("s", ext(T.y[:]), V("YO"))
    for k in range(1, 4):
        dma("a", ext(T.osc[4 * k:4 * k + 4, :]), (T.QOs[32 * k:32 * k + 4, :], V("QOs")[1]))
    schedule()
    g.wait_ge(T.sem.ls, count["ls"])
    for s in sorted(final):
        wait("g", (s, final[s], {}))
